import numpy as np
import ml_dtypes


def mxq(x, axis, fmt="e4m3"):
    dtype, down = {"e4m3": (ml_dtypes.float8_e4m3fn, 7), "e5m2": (ml_dtypes.float8_e5m2, 14)}[fmt]
    v = np.moveaxis(np.asarray(x, np.float32).astype(ml_dtypes.bfloat16).astype(np.float64), axis, -1)
    blocks = v.reshape(v.shape[:-1] + (-1, 32))
    amax = np.abs(blocks).max(-1, keepdims=True)
    byte = np.maximum(np.where(amax > 0, np.frexp(amax)[1] - 1 + 127, 0) - down, 1)
    scale = np.exp2(byte - 127.0)
    codes = (blocks / scale).astype(np.float32).astype(dtype).astype(np.float64)
    return np.moveaxis((codes * scale).reshape(v.shape), -1, axis)


WIDE = False


def mx_kscale(k):
    if not WIDE:
        return np.ones(k)
    levels = np.array([18, -18])
    if k % 512:
        return np.exp2(np.random.permutation(np.resize(levels, k // 32))).repeat(32)
    a = np.empty((k // 512, 16))
    for p in range(k // 512):
        a[p, :8] = np.random.permutation(np.resize(levels, 8))
        for g in range(8):
            far = levels[np.abs(levels - a[p, g]) >= 10]
            a[p, g + 8] = far[np.random.randint(len(far))]
    return np.exp2(a.ravel()).repeat(32)


def f64(x):
    return np.asarray(x).astype(np.float64)


def striped(idx):
    return np.tile(np.asarray(idx).reshape(-1, 16).T, (8, 1)).astype(np.uint16)


def unstriped(offs):
    return offs[:16].T.reshape(-1).astype(np.int64)


E2M1 = np.array([0.0, 0.5, 1.0, 1.5, 2.0, 3.0, 4.0, 6.0, -0.0, -0.5, -1.0, -1.5, -2.0, -3.0, -4.0, -6.0])


def pack_weight(w, fmt):
    k, n = w.shape
    w = f64(np.asarray(w, np.float32).astype(ml_dtypes.bfloat16)).reshape(k // 32, 32, n)
    amax = np.abs(w).max(1)
    if fmt == "e4m3":
        byte = np.frexp(amax)[1] - 1 + 127 - 7
    else:
        mant, ex = np.frexp(amax / 6.0)
        byte = np.where(mant > 0.5, ex, ex - 1) + 127
    byte = np.clip(np.where(amax > 0, byte, 1), 1, 254)
    scaled = (w * np.exp2(127.0 - byte)[:, None, :]).reshape(k, n).astype(np.float32)
    by_word = np.ascontiguousarray(scaled.reshape(k // 512, 128, 4, n).transpose(0, 1, 3, 2))
    if fmt == "e4m3":
        words = by_word.astype(ml_dtypes.float8_e4m3fn).view(np.uint8)
    else:
        c = by_word.astype(ml_dtypes.float4_e2m1fn).view(np.uint8) & 0xF
        words = (c[..., 0::2] | (c[..., 1::2] << 4)).reshape(k // 512, 128, 2 * n)
    return np.ascontiguousarray(words), np.ascontiguousarray(byte.astype(np.uint8).reshape(k // 512, 16, n))


def unpack_weight(words, scales, fmt):
    g, _, n = scales.shape
    words = np.ascontiguousarray(words).reshape(g, 128, n, -1)
    if fmt == "e4m3":
        vals = words.view(ml_dtypes.float8_e4m3fn).astype(np.float64)
    else:
        nib = np.empty((g, 128, n, 4), np.uint8)
        nib[..., 0::2] = words & 0xF
        nib[..., 1::2] = words >> 4
        vals = E2M1[nib]
    vals = vals * np.repeat(np.exp2(scales.astype(np.float64) - 127.0), 8, axis=1)[..., None]
    return vals.transpose(0, 1, 3, 2).reshape(g * 512, n)


def planes(y):
    n, m = y.shape
    v = y.astype(np.float32).astype(ml_dtypes.bfloat16).astype(np.float64).reshape(n // 32, 32, m)
    top = np.abs(v).max(1)
    byte = np.clip(np.where(top > 0, np.frexp(top)[1] - 1 + 127 - 7, 1), 1, 254)
    codes = (v * np.exp2(127.0 - byte)[:, None, :]).reshape(n, m).astype(np.float32).astype(ml_dtypes.float8_e4m3fn).view(np.uint8)
    words = codes.reshape(n // 512, 128, 4, m).transpose(0, 1, 3, 2)
    return np.ascontiguousarray(words), np.ascontiguousarray(byte.astype(np.uint8).reshape(n // 512, 16, m))


N, T, D, V = 512, 2048, 512, 512


def setup_inputs():
    n = np.random.standard_normal
    idx = np.random.permutation(T)[:N]
    s = mx_kscale(D)[:, None]
    z = mx_kscale(V)[:, None]
    w = n((D, V)) / np.sqrt(D)
    wd, wv = pack_weight(w * s, "e2m1"), pack_weight(w.T / z, "e2m1")
    return {
        "xT": (n((D, T)) / s).astype(np.float32),
        "wd_words": wd[0],
        "wd_scales": wd[1],
        "wv_words": wv[0],
        "wv_scales": wv[1],
        "y": np.random.randint(0, 2, (V, N)).astype(np.float32),
        "cw": (np.random.uniform(0.5, 1.5, (V, 1)) / np.sqrt(V) * z).astype(np.float32),
        "rw": np.tile(np.random.uniform(0.5, 1.5, N), (128, 1)).astype(np.float32),
        "offs": striped(idx),
    }


def reference(xT, wd_words, wd_scales, wv_words, wv_scales, y, cw, rw, offs):
    idx = unstriped(offs)
    a = unpack_weight(wd_words, wd_scales, "e2m1").T @ mxq(f64(xT)[:, idx], 0, "e4m3")
    g = f64(cw) * f64(rw)[:1] * (1.0 / (1.0 + np.exp(-a)) - f64(y))
    dx = unpack_weight(wv_words, wv_scales, "e2m1").T @ mxq(g, 0, "e5m2")
    gx = np.zeros((D, T))
    gx[:, idx] = dx
    out_0 = gx
    return (out_0,) + planes(out_0)

@@ -1,0 +1,198 @@
+from contextlib import ExitStack
+
+import concourse.mybir as mybir
+from concourse.masks import make_identity
+
+N, T, D, V = 512, 2048, 512, 512
+FLOPS = 2 * 2 * N * D * V
+
+F32 = mybir.dt.float32
+BF16 = mybir.dt.bfloat16
+I32 = mybir.dt.int32
+U32 = mybir.dt.uint32
+U16 = mybir.dt.uint16
+U8 = mybir.dt.uint8
+E4M3 = mybir.dt.float8_e4m3fn_x4
+E5M2 = mybir.dt.float8_e5m2_x4
+E2M1 = mybir.dt.float4_e2m1fn_x4
+ACT = mybir.ActivationFunctionType
+ALU = mybir.AluOpType
+
+P = 128
+L = 4
+HALF = N // 2
+CH = 128
+WIDTHS = [256, 512, 512, 512, 256]
+
+
+def load_head(nc, pool, name, words, scales, queue):
+    raw_w = pool.tile([P, 2 * 512], U8, name=name + "_raw_w", align_bytes=64)
+    raw_s = pool.tile([P, 512], U8, name=name + "_raw_s", align_bytes=64)
+    nc.vector.memset(raw_s[:].bitcast(I32), 0)
+    queue.dma_start(out=raw_w[:].bitcast(I32), in_=words[0].bitcast(I32))
+    for q in range(4):
+        queue.dma_start(out=raw_s[32 * q : 32 * q + 4, :].bitcast(I32), in_=scales[0, 4 * q : 4 * q + 4, :].bitcast(I32))
+    return raw_w, raw_s
+
+
+def deal_head(nc, pool, name, raw_w, raw_s):
+    w = pool.tile([P, 2 * 512], U8, name=name + "_w", align_bytes=64)
+    s = pool.tile([P, 512], U8, name=name + "_s", align_bytes=64)
+    nc.vector.tensor_copy(
+        out=w[:].bitcast(U16).rearrange("p (r s) -> p r s", r=L),
+        in_=raw_w[:].bitcast(U16).rearrange("p (s r) -> p r s", r=L),
+    )
+    nc.vector.tensor_copy(
+        out=s[:].rearrange("p (r s) -> p r s", r=L),
+        in_=raw_s[:].rearrange("p (s r) -> p r s", r=L),
+    )
+    return w, s
+
+
+def tile_attend_gml_pl_nce_kernel(
+    tc, xT, wd_words, wd_scales, wv_words, wv_scales, y, cw, rw, offs, out_0, out_1, out_2
+):
+    nc = tc.nc
+    with ExitStack() as ctx:
+        lists = ctx.enter_context(tc.tile_pool(name="lists", bufs=1))
+        sb = ctx.enter_context(tc.tile_pool(name="sb", bufs=1))
+        ps = ctx.enter_context(tc.psum_pool(name="ps", bufs=1))
+
+        offsets = lists.tile([P, N // 16], U16, name="offsets")
+        nc.sync.dma_start(offsets[:], offs)
+
+        x_rows = xT.rearrange("(p r) t -> p r t", r=L)
+        x_pl = [sb.tile([P, T], F32, name=f"x_pl{r}") for r in range(L)]
+        for r in range(L):
+            nc.sync.dma_start(out=x_pl[r][:], in_=x_rows[:, r, :])
+        y_rows = y.rearrange("(p r) i -> p r i", r=L)
+        y_h = [sb.tile([P, L, HALF], F32, name=f"y_h{h}") for h in range(2)]
+        for h in range(2):
+            nc.sync.dma_start(out=y_h[h][:], in_=y_rows[:, :, h * HALF : (h + 1) * HALF])
+
+        warm = sb.tile([P, 1], F32, name="warm")
+        warm2 = sb.tile([P, 1], F32, name="warm2")
+        nc.gpsimd.memset(warm[:], 0.0)
+        nc.scalar.activation(warm2[:], warm[:], ACT.Sigmoid)
+
+        cw_sb = sb.tile([P, L], F32, name="cw_sb")
+        rw_sb = sb.tile([P, L], F32, name="rw_sb")
+        nc.scalar.dma_start(out=rw_sb[:], in_=rw[0].rearrange("(c m) -> c m", m=L))
+        nc.scalar.dma_start(out=cw_sb[:], in_=cw.rearrange("(p r) o -> p (r o)", r=L))
+        wd_raw = load_head(nc, sb, "wd", wd_words, wd_scales, nc.scalar)
+        wv_raw = load_head(nc, sb, "wv", wv_words, wv_scales, nc.scalar)
+
+        win = [sb.tile([P, T], F32, name=f"win{r}") for r in range(L)]
+        for r in range(L):
+            nc.vector.memset(win[r][:].bitcast(I32), 0)
+
+        ident = sb.tile([P, P], F32, name="ident")
+        make_identity(nc, ident[:])
+        rw_ps = ps.tile([P, L, P], F32, name="rw_ps", tag="bank7")
+        for m in range(L):
+            nc.tensor.transpose(rw_ps[:, m, :], rw_sb[:, m : m + 1].to_broadcast([P, P]), ident[:])
+        cc = sb.tile([P, P, L, L], F32, name="cc")
+        for r in range(L):
+            nc.scalar.activation(cc[:, :, r, :], rw_ps[:].rearrange("p m c -> p c m"), ACT.Copy, scale=cw_sb[:, r : r + 1])
+
+        wd_w, wd_s = deal_head(nc, sb, "wd", *wd_raw)
+        wv_w, wv_s = deal_head(nc, sb, "wv", *wv_raw)
+
+        xb = [sb.tile([P, HALF, L], BF16, name=f"xb{h}", align_bytes=64) for h in range(2)]
+        xq = [sb.tile([P, HALF], U32, name=f"xq{h}", align_bytes=64) for h in range(2)]
+        xs = [sb.tile([P, HALF], U8, name=f"xs{h}", align_bytes=64) for h in range(2)]
+        for r in range(L):
+            for h in range(2):
+                nc.vector.tensor_copy(xb[h][:, :, r], x_pl[r][:].indirect(offsets[:, 16 * h : 16 * (h + 1)]))
+                if r == L - 1:
+                    nc.vector.quantize_mx(out=xq[h][:].bitcast(E4M3), scales=xs[h][:], in_=xb[h][:].rearrange("p n r -> p (n r)"))
+
+        gq = sb.tile([P, HALF + N], U32, name="gq", align_bytes=64)
+        gs = sb.tile([P, HALF + N], U8, name="gs", align_bytes=64)
+        nc.gpsimd.memset(gq[:, :HALF], 0)
+        nc.gpsimd.memset(gs[:, :HALF].bitcast(U32), 0)
+        dx = [sb.tile([P, N], F32, name=f"dx{r}") for r in range(L)]
+
+        def back(r, first, tag):
+            acc = ps.tile([P, N], F32, name=f"dx_ps{r}", tag=tag)
+            nc.tensor.matmul_mx(
+                out=acc[:],
+                lhsT=wv_w[:, 2 * P * r : 2 * P * (r + 1)].bitcast(E2M1),
+                lhsT_scale=wv_s[:, P * r : P * (r + 1)],
+                rhs=gq[:, first : first + N].bitcast(E5M2),
+                rhs_scale=gs[:, first : first + N],
+                start=True,
+                stop=True,
+            )
+            return acc
+
+        gb = [sb.tile([P, HALF * L], BF16, name=f"gb{h}", align_bytes=64) for h in range(2)]
+        for k in range(N // CH):
+            h, j = divmod(k, 2)
+            cols = slice(j * CH, (j + 1) * CH)
+            sc = ps.tile([P, L, CH], F32, name=f"sc{k}", tag=f"bank{k}")
+            for r in range(L):
+                nc.tensor.matmul_mx(
+                    out=sc[:, r, :],
+                    lhsT=wd_w[:, 2 * P * r : 2 * P * (r + 1)].bitcast(E2M1),
+                    lhsT_scale=wd_s[:, P * r : P * (r + 1)],
+                    rhs=xq[h][:, cols].bitcast(E4M3),
+                    rhs_scale=xs[h][:, cols],
+                    start=True,
+                    stop=True,
+                )
+            sig = sb.tile([P, L, CH], F32, name=f"sig{k}")
+            nc.scalar.activation(sig[:], sc[:], ACT.Sigmoid)
+            dif = sb.tile([P, L, CH], F32, name=f"dif{k}")
+            nc.vector.tensor_tensor(dif[:], sig[:], y_h[h][:, :, cols], ALU.subtract)
+            nc.vector.tensor_tensor(
+                gb[h][:, j * CH * L : (j + 1) * CH * L].rearrange("p (c i r) -> p c r i", i=L, r=L),
+                dif[:].rearrange("p r (c i) -> p c r i", i=L),
+                cc[:, k * (CH // L) : (k + 1) * (CH // L), :, :],
+                ALU.mult,
+            )
+            if j == 1:
+                nc.vector.quantize_mx(
+                    out=gq[:, (h + 1) * HALF : (h + 2) * HALF].bitcast(E5M2), scales=gs[:, (h + 1) * HALF : (h + 2) * HALF], in_=gb[h][:]
+                )
+            if k == 1:
+                early = back(0, 0, "bank7")
+                nc.scalar.copy(dx[0][:, :HALF], early[:, HALF:])
+
+        o_rows = out_0.rearrange("(p r) t -> p r t", r=L)
+        starts = [sum(WIDTHS[:k]) for k in range(len(WIDTHS))]
+        pairs = [sb.tile([P, 2, w, 2], BF16, name=f"pairs{k}", align_bytes=64) for k, w in enumerate(WIDTHS)]
+        nc.vector.tensor_copy(win[0][:].indirect(offsets[:, :16]), dx[0][:, :HALF])
+        for r in range(L):
+            acc = back(r, HALF, f"bank{(4 + r) % 7}")
+            if r == 0:
+                nc.scalar.copy(dx[0][:, HALF:], acc[:, HALF:])
+                nc.vector.tensor_copy(win[0][:].indirect(offsets[:, 16:]), dx[0][:, HALF:])
+            else:
+                nc.scalar.copy(dx[r][:], acc[:])
+                nc.vector.tensor_copy(win[r][:].indirect(offsets[:]), dx[r][:])
+            nc.sync.dma_start(out=o_rows[:, r, :], in_=win[r][:])
+        for r in range(L):
+            for k, w in enumerate(WIDTHS):
+                nc.scalar.copy(pairs[k][:, r // 2, :, r % 2], win[r][:, starts[k] : starts[k] + w])
+
+        os_ = sb.tile([P, T], U8, name="os_", align_bytes=64)
+        o1 = out_1[0].rearrange("p n t -> p (n t)")
+        for k, w in enumerate(WIDTHS):
+            ob = sb.tile([P, w * L], BF16, name=f"ob{k}", align_bytes=64)
+            oq = sb.tile([P, w], U32, name=f"oq{k}", align_bytes=64)
+            if k == len(WIDTHS) - 1:
+                nc.scalar.copy(
+                    ob[:].bitcast(U32).rearrange("p (n u) -> p n u", u=2),
+                    pairs[k][:].rearrange("p u n e -> p u (n e)").bitcast(U32).rearrange("p u n -> p n u"),
+                )
+            else:
+                nc.vector.tensor_copy(
+                    out=ob[:].bitcast(I32).rearrange("p (n u) -> p n u", u=2),
+                    in_=pairs[k][:].rearrange("p u n e -> p u (n e)").bitcast(I32).rearrange("p u n -> p n u"),
+                )
+            nc.vector.quantize_mx(out=oq[:].bitcast(E4M3), scales=os_[:, starts[k] : starts[k] + w], in_=ob[:])
+            nc.sync.dma_start(out=o1[:, L * starts[k] : L * (starts[k] + w)].bitcast(I32), in_=oq[:].bitcast(I32))
+        for q in range(4):
+            queue = nc.scalar if q % 2 == 0 else nc.sync
+            queue.dma_start(out=out_2[0, 4 * q : 4 * q + 4, :].bitcast(I32), in_=os_[32 * q : 32 * q + 4, :].bitcast(I32))

@@ -22,12 +22,13 @@ P = 128
 L = 4
 HALF = N // 2
 CH = 128
+BLK = 256
 WIDTHS = [256, 512, 512, 512, 256]
 
 
 def load_head(nc, pool, name, words, scales, queue):
-    raw_w = pool.tile([P, 2 * 512], U8, name=name + "_raw_w", align_bytes=64)
-    raw_s = pool.tile([P, 512], U8, name=name + "_raw_s", align_bytes=64)
+    raw_w = pool.tile([P, 2 * 512], U8, name=name + "_raw_w", tag="raw_w", align_bytes=64)
+    raw_s = pool.tile([P, 512], U8, name=name + "_raw_s", tag="raw_s", align_bytes=64)
     nc.vector.memset(raw_s[:].bitcast(I32), 0)
     queue.dma_start(out=raw_w[:].bitcast(I32), in_=words[0].bitcast(I32))
     for q in range(4):
@@ -65,11 +66,6 @@ def tile_attend_gml_pl_nce_kernel(
         x_pl = [sb.tile([P, T], F32, name=f"x_pl{r}") for r in range(L)]
         for r in range(L):
             nc.sync.dma_start(out=x_pl[r][:], in_=x_rows[:, r, :])
-        y_rows = y.rearrange("(p r) i -> p r i", r=L)
-        y_h = [sb.tile([P, L, HALF], F32, name=f"y_h{h}") for h in range(2)]
-        for h in range(2):
-            nc.sync.dma_start(out=y_h[h][:], in_=y_rows[:, :, h * HALF : (h + 1) * HALF])
-
         warm = sb.tile([P, 1], F32, name="warm")
         warm2 = sb.tile([P, 1], F32, name="warm2")
         nc.gpsimd.memset(warm[:], 0.0)
@@ -80,23 +76,24 @@ def tile_attend_gml_pl_nce_kernel(
         nc.scalar.dma_start(out=rw_sb[:], in_=rw[0].rearrange("(c m) -> c m", m=L))
         nc.scalar.dma_start(out=cw_sb[:], in_=cw.rearrange("(p r) o -> p (r o)", r=L))
         wd_raw = load_head(nc, sb, "wd", wd_words, wd_scales, nc.scalar)
-        wv_raw = load_head(nc, sb, "wv", wv_words, wv_scales, nc.scalar)
 
-        win = [sb.tile([P, T], F32, name=f"win{r}") for r in range(L)]
-        for r in range(L):
-            nc.vector.memset(win[r][:].bitcast(I32), 0)
 
         ident = sb.tile([P, P], F32, name="ident")
         make_identity(nc, ident[:])
+        win = [sb.tile([P, T], F32, name=f"win{r}") for r in range(L)]
+        for r in range(2):
+            nc.vector.memset(win[r][:].bitcast(I32), 0)
+        for r in range(2, L):
+            for h in range(2):
+                nc.gpsimd.memset(win[r][:, h * (T // 2) : (h + 1) * (T // 2)].bitcast(I32), 0)
         rw_ps = ps.tile([P, L, P], F32, name="rw_ps", tag="bank7")
         for m in range(L):
             nc.tensor.transpose(rw_ps[:, m, :], rw_sb[:, m : m + 1].to_broadcast([P, P]), ident[:])
-        cc = sb.tile([P, P, L, L], F32, name="cc")
+        cc = sb.tile([P, L, N], F32, name="cc")
         for r in range(L):
-            nc.scalar.activation(cc[:, :, r, :], rw_ps[:].rearrange("p m c -> p c m"), ACT.Copy, scale=cw_sb[:, r : r + 1])
+            nc.scalar.activation(cc[:, r, :].rearrange("p (c m) -> p c m", m=L), rw_ps[:].rearrange("p m c -> p c m"), ACT.Copy, scale=cw_sb[:, r : r + 1])
 
         wd_w, wd_s = deal_head(nc, sb, "wd", *wd_raw)
-        wv_w, wv_s = deal_head(nc, sb, "wv", *wv_raw)
 
         xb = [sb.tile([P, HALF, L], BF16, name=f"xb{h}", align_bytes=64) for h in range(2)]
         xq = [sb.tile([P, HALF], U32, name=f"xq{h}", align_bytes=64) for h in range(2)]
@@ -106,6 +103,14 @@ def tile_attend_gml_pl_nce_kernel(
                 nc.vector.tensor_copy(xb[h][:, :, r], x_pl[r][:].indirect(offsets[:, 16 * h : 16 * (h + 1)]))
                 if r == L - 1:
                     nc.vector.quantize_mx(out=xq[h][:].bitcast(E4M3), scales=xs[h][:], in_=xb[h][:].rearrange("p n r -> p (n r)"))
+
+        y_rows = y.rearrange("(p r) i -> p r i", r=L)
+        y_h = [sb.tile([P, L, HALF], F32, name=f"y_h{h}", tag=f"x_pl{h}") for h in range(2)]
+        for h in range(2):
+            nc.sync.dma_start(out=y_h[h][:], in_=y_rows[:, :, h * HALF : (h + 1) * HALF])
+
+        wv_raw = load_head(nc, sb, "wv", wv_words, wv_scales, nc.sync)
+        wv_w, wv_s = deal_head(nc, sb, "wv", *wv_raw)
 
         gq = sb.tile([P, HALF + N], U32, name="gq", align_bytes=64)
         gs = sb.tile([P, HALF + N], U8, name="gs", align_bytes=64)
@@ -146,9 +151,9 @@ def tile_attend_gml_pl_nce_kernel(
             dif = sb.tile([P, L, CH], F32, name=f"dif{k}")
             nc.vector.tensor_tensor(dif[:], sig[:], y_h[h][:, :, cols], ALU.subtract)
             nc.vector.tensor_tensor(
-                gb[h][:, j * CH * L : (j + 1) * CH * L].rearrange("p (c i r) -> p c r i", i=L, r=L),
-                dif[:].rearrange("p r (c i) -> p c r i", i=L),
-                cc[:, k * (CH // L) : (k + 1) * (CH // L), :, :],
+                gb[h][:, j * CH * L : (j + 1) * CH * L].rearrange("p (c i r) -> p c r i", i=2, r=L),
+                dif[:].rearrange("p r (c i) -> p c r i", i=2),
+                cc[:, :, k * CH : (k + 1) * CH].rearrange("p r (c i) -> p c r i", i=2),
                 ALU.mult,
             )
             if j == 1:
@@ -157,12 +162,13 @@ def tile_attend_gml_pl_nce_kernel(
                 )
             if k == 1:
                 early = back(0, 0, "bank7")
-                nc.scalar.copy(dx[0][:, :HALF], early[:, HALF:])
+        dx_early = sb.tile([P, HALF], F32, name="dx_early", tag="dif3")
+        nc.scalar.copy(dx_early[:], early[:, HALF:])
 
         o_rows = out_0.rearrange("(p r) t -> p r t", r=L)
         starts = [sum(WIDTHS[:k]) for k in range(len(WIDTHS))]
-        pairs = [sb.tile([P, 2, w, 2], BF16, name=f"pairs{k}", align_bytes=64) for k, w in enumerate(WIDTHS)]
-        nc.vector.tensor_copy(win[0][:].indirect(offsets[:, :16]), dx[0][:, :HALF])
+        pairs = sb.tile([P, T * L], BF16, name="pairs", align_bytes=64)
+        nc.vector.tensor_copy(win[0][:].indirect(offsets[:, :16]), dx_early[:])
         for r in range(L):
             acc = back(r, HALF, f"bank{(4 + r) % 7}")
             if r == 0:
@@ -173,23 +179,27 @@ def tile_attend_gml_pl_nce_kernel(
                 nc.vector.tensor_copy(win[r][:].indirect(offsets[:]), dx[r][:])
             nc.sync.dma_start(out=o_rows[:, r, :], in_=win[r][:])
         for r in range(L):
-            for k, w in enumerate(WIDTHS):
-                nc.scalar.copy(pairs[k][:, r // 2, :, r % 2], win[r][:, starts[k] : starts[k] + w])
+            for first, w in zip(starts, WIDTHS) if r == L - 1 else [(0, T)]:
+                nc.scalar.copy(
+                    pairs[:, L * first : L * (first + w)].rearrange("p (b u n e) -> p b u n e", u=2, n=BLK, e=2)[:, :, r // 2, :, r % 2],
+                    win[r][:, first : first + w].rearrange("p (b n) -> p b n", n=BLK),
+                )
 
         os_ = sb.tile([P, T], U8, name="os_", align_bytes=64)
         o1 = out_1[0].rearrange("p n t -> p (n t)")
         for k, w in enumerate(WIDTHS):
             ob = sb.tile([P, w * L], BF16, name=f"ob{k}", align_bytes=64)
             oq = sb.tile([P, w], U32, name=f"oq{k}", align_bytes=64)
+            src = pairs[:, L * starts[k] : L * (starts[k] + w)]
             if k == len(WIDTHS) - 1:
                 nc.scalar.copy(
-                    ob[:].bitcast(U32).rearrange("p (n u) -> p n u", u=2),
-                    pairs[k][:].rearrange("p u n e -> p u (n e)").bitcast(U32).rearrange("p u n -> p n u"),
+                    ob[:].bitcast(U32).rearrange("p (b n u) -> p b n u", n=BLK, u=2),
+                    src.bitcast(U32).rearrange("p (b u n) -> p b n u", u=2, n=BLK),
                 )
             else:
                 nc.vector.tensor_copy(
-                    out=ob[:].bitcast(I32).rearrange("p (n u) -> p n u", u=2),
-                    in_=pairs[k][:].rearrange("p u n e -> p u (n e)").bitcast(I32).rearrange("p u n -> p n u"),
+                    out=ob[:].bitcast(I32).rearrange("p (b n u) -> p b n u", n=BLK, u=2),
+                    in_=src.bitcast(I32).rearrange("p (b u n) -> p b n u", u=2, n=BLK),
                 )
             nc.vector.quantize_mx(out=oq[:].bitcast(E4M3), scales=os_[:, starts[k] : starts[k] + w], in_=ob[:])
             nc.sync.dma_start(out=o1[:, L * starts[k] : L * (starts[k] + w)].bitcast(I32), in_=oq[:].bitcast(I32))

@@ -23,14 +23,14 @@ L = 4
 HALF = N // 2
 CH = 128
 BLK = 256
-WIDTHS = [256, 512, 512, 512, 256]
+WIDTHS = [256, 512, 512, 256, 256, 256]
 
 
-def load_head(nc, pool, name, words, scales, queue):
-    raw_w = pool.tile([P, 2 * 512], U8, name=name + "_raw_w", tag="raw_w", align_bytes=64)
-    raw_s = pool.tile([P, 512], U8, name=name + "_raw_s", tag="raw_s", align_bytes=64)
-    nc.vector.memset(raw_s[:].bitcast(I32), 0)
-    queue.dma_start(out=raw_w[:].bitcast(I32), in_=words[0].bitcast(I32))
+def load_head(nc, pool, name, words, scales, word_queue, queue, clear):
+    raw_w = pool.tile([P, 2 * 512], U8, name=name + "_raw_w", align_bytes=64)
+    raw_s = pool.tile([P, 512], U8, name=name + "_raw_s", align_bytes=64)
+    clear.memset(raw_s[:].bitcast(I32), 0)
+    word_queue.dma_start(out=raw_w[:].bitcast(I32), in_=words[0].bitcast(I32))
     for q in range(4):
         queue.dma_start(out=raw_s[32 * q : 32 * q + 4, :].bitcast(I32), in_=scales[0, 4 * q : 4 * q + 4, :].bitcast(I32))
     return raw_w, raw_s
@@ -66,24 +66,20 @@ def tile_attend_gml_pl_nce_kernel(
         x_pl = [sb.tile([P, T], F32, name=f"x_pl{r}") for r in range(L)]
         for r in range(L):
             nc.sync.dma_start(out=x_pl[r][:], in_=x_rows[:, r, :])
-        warm = sb.tile([P, 1], F32, name="warm")
-        warm2 = sb.tile([P, 1], F32, name="warm2")
-        nc.gpsimd.memset(warm[:], 0.0)
-        nc.scalar.activation(warm2[:], warm[:], ACT.Sigmoid)
-
         cw_sb = sb.tile([P, L], F32, name="cw_sb")
         rw_sb = sb.tile([P, L], F32, name="rw_sb")
         nc.scalar.dma_start(out=rw_sb[:], in_=rw[0].rearrange("(c m) -> c m", m=L))
         nc.scalar.dma_start(out=cw_sb[:], in_=cw.rearrange("(p r) o -> p (r o)", r=L))
-        wd_raw = load_head(nc, sb, "wd", wd_words, wd_scales, nc.scalar)
+        wd_raw = load_head(nc, sb, "wd", wd_words, wd_scales, nc.scalar, nc.scalar, nc.vector)
 
 
         ident = sb.tile([P, P], F32, name="ident")
         make_identity(nc, ident[:])
+        wv_raw = load_head(nc, sb, "wv", wv_words, wv_scales, nc.sync, nc.gpsimd, nc.gpsimd)
         win = [sb.tile([P, T], F32, name=f"win{r}") for r in range(L)]
-        for r in range(2):
+        for r in range(3):
             nc.vector.memset(win[r][:].bitcast(I32), 0)
-        for r in range(2, L):
+        for r in range(3, L):
             for h in range(2):
                 nc.gpsimd.memset(win[r][:, h * (T // 2) : (h + 1) * (T // 2)].bitcast(I32), 0)
         rw_ps = ps.tile([P, L, P], F32, name="rw_ps", tag="bank7")
@@ -95,23 +91,22 @@ def tile_attend_gml_pl_nce_kernel(
 
         wd_w, wd_s = deal_head(nc, sb, "wd", *wd_raw)
 
-        xb = [sb.tile([P, HALF, L], BF16, name=f"xb{h}", align_bytes=64) for h in range(2)]
+        xb = sb.tile([P, N, L], BF16, name="xb", align_bytes=64)
         xq = [sb.tile([P, HALF], U32, name=f"xq{h}", align_bytes=64) for h in range(2)]
         xs = [sb.tile([P, HALF], U8, name=f"xs{h}", align_bytes=64) for h in range(2)]
-        for r in range(L):
-            for h in range(2):
-                nc.vector.tensor_copy(xb[h][:, :, r], x_pl[r][:].indirect(offsets[:, 16 * h : 16 * (h + 1)]))
-                if r == L - 1:
-                    nc.vector.quantize_mx(out=xq[h][:].bitcast(E4M3), scales=xs[h][:], in_=xb[h][:].rearrange("p n r -> p (n r)"))
+        for r in range(L - 1):
+            nc.vector.tensor_copy(xb[:, :, r], x_pl[r][:].indirect(offsets[:]))
+        for h, (lo, hi) in enumerate([(0, 16), (14, 32)]):
+            nc.vector.tensor_copy(xb[:, 16 * lo : 16 * hi, L - 1], x_pl[L - 1][:].indirect(offsets[:, lo:hi]))
+            nc.vector.quantize_mx(out=xq[h][:].bitcast(E4M3), scales=xs[h][:], in_=xb[:, h * HALF : (h + 1) * HALF, :].rearrange("p n r -> p (n r)"))
 
         y_rows = y.rearrange("(p r) i -> p r i", r=L)
         y_h = [sb.tile([P, L, HALF], F32, name=f"y_h{h}", tag=f"x_pl{h}") for h in range(2)]
         for h in range(2):
             nc.sync.dma_start(out=y_h[h][:], in_=y_rows[:, :, h * HALF : (h + 1) * HALF])
 
-        wv_raw = load_head(nc, sb, "wv", wv_words, wv_scales, nc.sync)
-        wv_w, wv_s = deal_head(nc, sb, "wv", *wv_raw)
 
+        wv_w, wv_s = deal_head(nc, sb, "wv", *wv_raw)
         gq = sb.tile([P, HALF + N], U32, name="gq", align_bytes=64)
         gs = sb.tile([P, HALF + N], U8, name="gs", align_bytes=64)
         nc.gpsimd.memset(gq[:, :HALF], 0)
@@ -187,21 +182,27 @@ def tile_attend_gml_pl_nce_kernel(
 
         os_ = sb.tile([P, T], U8, name="os_", align_bytes=64)
         o1 = out_1[0].rearrange("p n t -> p (n t)")
-        for k, w in enumerate(WIDTHS):
-            ob = sb.tile([P, w * L], BF16, name=f"ob{k}", align_bytes=64)
-            oq = sb.tile([P, w], U32, name=f"oq{k}", align_bytes=64)
-            src = pairs[:, L * starts[k] : L * (starts[k] + w)]
-            if k == len(WIDTHS) - 1:
+        ob = [sb.tile([P, w * L], BF16, name=f"ob{k}", align_bytes=64) for k, w in enumerate(WIDTHS)]
+
+        def weave(k):
+            src = pairs[:, L * starts[k] : L * (starts[k] + WIDTHS[k])]
+            if k >= len(WIDTHS) - 2:
                 nc.scalar.copy(
-                    ob[:].bitcast(U32).rearrange("p (b n u) -> p b n u", n=BLK, u=2),
+                    ob[k][:].bitcast(U32).rearrange("p (b n u) -> p b n u", n=BLK, u=2),
                     src.bitcast(U32).rearrange("p (b u n) -> p b n u", u=2, n=BLK),
                 )
             else:
                 nc.vector.tensor_copy(
-                    out=ob[:].bitcast(I32).rearrange("p (b n u) -> p b n u", n=BLK, u=2),
+                    out=ob[k][:].bitcast(I32).rearrange("p (b n u) -> p b n u", n=BLK, u=2),
                     in_=src.bitcast(I32).rearrange("p (b u n) -> p b n u", u=2, n=BLK),
                 )
-            nc.vector.quantize_mx(out=oq[:].bitcast(E4M3), scales=os_[:, starts[k] : starts[k] + w], in_=ob[:])
+
+        weave(0)
+        for k, w in enumerate(WIDTHS):
+            if k + 1 < len(WIDTHS):
+                weave(k + 1)
+            oq = sb.tile([P, w], U32, name=f"oq{k}", align_bytes=64)
+            nc.vector.quantize_mx(out=oq[:].bitcast(E4M3), scales=os_[:, starts[k] : starts[k] + w], in_=ob[k][:])
             nc.sync.dma_start(out=o1[:, L * starts[k] : L * (starts[k] + w)].bitcast(I32), in_=oq[:].bitcast(I32))
         for q in range(4):
             queue = nc.scalar if q % 2 == 0 else nc.sync

@@ -26,14 +26,9 @@ BLK = 256
 WIDTHS = [256, 512, 512, 256, 256, 256]
 
 
-def load_head(nc, pool, name, words, scales, word_queue, queue, clear):
-    raw_w = pool.tile([P, 2 * 512], U8, name=name + "_raw_w", align_bytes=64)
-    raw_s = pool.tile([P, 512], U8, name=name + "_raw_s", align_bytes=64)
-    clear.memset(raw_s[:].bitcast(I32), 0)
-    word_queue.dma_start(out=raw_w[:].bitcast(I32), in_=words[0].bitcast(I32))
+def load_scales(nc, raw_s, scales):
     for q in range(4):
-        queue.dma_start(out=raw_s[32 * q : 32 * q + 4, :].bitcast(I32), in_=scales[0, 4 * q : 4 * q + 4, :].bitcast(I32))
-    return raw_w, raw_s
+        nc.sync.dma_start(out=raw_s[32 * q : 32 * q + 4, :].bitcast(I32), in_=scales[0, 4 * q : 4 * q + 4, :].bitcast(I32))
 
 
 def deal_head(nc, pool, name, raw_w, raw_s):
@@ -59,29 +54,45 @@ def tile_attend_gml_pl_nce_kernel(
         sb = ctx.enter_context(tc.tile_pool(name="sb", bufs=1))
         ps = ctx.enter_context(tc.psum_pool(name="ps", bufs=1))
 
-        offsets = lists.tile([P, N // 16], U16, name="offsets")
-        nc.sync.dma_start(offsets[:], offs)
+        wd_raw_s = sb.tile([P, 512], U8, name="wd_raw_s", align_bytes=64)
+        wv_raw_s = sb.tile([P, 512], U8, name="wv_raw_s", align_bytes=64)
+        nc.gpsimd.memset(wd_raw_s[:].bitcast(I32), 0)
+        nc.gpsimd.memset(wv_raw_s[:].bitcast(I32), 0)
+        wd_raw_w = sb.tile([P, 2 * 512], U8, name="wd_raw_w", align_bytes=64)
+        wv_raw_w = sb.tile([P, 2 * 512], U8, name="wv_raw_w", align_bytes=64)
 
+        offsets = lists.tile([P, N // 16], U16, name="offsets")
         x_rows = xT.rearrange("(p r) t -> p r t", r=L)
         x_pl = [sb.tile([P, T], F32, name=f"x_pl{r}") for r in range(L)]
-        for r in range(L):
-            nc.sync.dma_start(out=x_pl[r][:], in_=x_rows[:, r, :])
         cw_sb = sb.tile([P, L], F32, name="cw_sb")
         rw_sb = sb.tile([P, L], F32, name="rw_sb")
-        nc.scalar.dma_start(out=rw_sb[:], in_=rw[0].rearrange("(c m) -> c m", m=L))
-        nc.scalar.dma_start(out=cw_sb[:], in_=cw.rearrange("(p r) o -> p (r o)", r=L))
-        wd_raw = load_head(nc, sb, "wd", wd_words, wd_scales, nc.scalar, nc.scalar, nc.vector)
+        y_rows = y.rearrange("(p r) i -> p r i", r=L)
+        y_h = [sb.tile([P, L, HALF], F32, name=f"y_h{h}") for h in range(2)]
 
+        nc.sync.dma_start(offsets[:], offs)
+        nc.sync.dma_start(out=x_pl[0][:], in_=x_rows[:, 0, :])
+        nc.sync.dma_start(out=wd_raw_w[:].bitcast(I32), in_=wd_words[0].bitcast(I32))
+        nc.sync.dma_start(out=rw_sb[:], in_=rw[0].rearrange("(c m) -> c m", m=L))
+        load_scales(nc, wd_raw_s, wd_scales)
+        nc.sync.dma_start(out=x_pl[1][:], in_=x_rows[:, 1, :])
+        nc.sync.dma_start(out=cw_sb[:], in_=cw.rearrange("(p r) o -> p (r o)", r=L))
+        nc.sync.dma_start(out=wv_raw_w[:].bitcast(I32), in_=wv_words[0].bitcast(I32))
+        load_scales(nc, wv_raw_s, wv_scales)
+        for r in range(2, L):
+            nc.sync.dma_start(out=x_pl[r][:], in_=x_rows[:, r, :])
+        for h in range(2):
+            nc.sync.dma_start(out=y_h[h][:], in_=y_rows[:, :, h * HALF : (h + 1) * HALF])
 
         ident = sb.tile([P, P], F32, name="ident")
         make_identity(nc, ident[:])
-        wv_raw = load_head(nc, sb, "wv", wv_words, wv_scales, nc.sync, nc.gpsimd, nc.gpsimd)
-        win = [sb.tile([P, T], F32, name=f"win{r}") for r in range(L)]
-        for r in range(3):
-            nc.vector.memset(win[r][:].bitcast(I32), 0)
-        for r in range(3, L):
-            for h in range(2):
-                nc.gpsimd.memset(win[r][:, h * (T // 2) : (h + 1) * (T // 2)].bitcast(I32), 0)
+        gq = sb.tile([P, HALF + N], U32, name="gq", align_bytes=64)
+        gs = sb.tile([P, HALF + N], U8, name="gs", align_bytes=64)
+        nc.gpsimd.memset(gq[:, :HALF], 0)
+        nc.gpsimd.memset(gs[:, :HALF].bitcast(U32), 0)
+        windows = [sb.tile([P, T], F32, name=f"win{r}") for r in range(L - 1)]
+        for r in range(L - 1):
+            nc.vector.memset(windows[r][:].bitcast(I32), 0)
+        win = windows + windows[:1]
         rw_ps = ps.tile([P, L, P], F32, name="rw_ps", tag="bank7")
         for m in range(L):
             nc.tensor.transpose(rw_ps[:, m, :], rw_sb[:, m : m + 1].to_broadcast([P, P]), ident[:])
@@ -89,7 +100,8 @@ def tile_attend_gml_pl_nce_kernel(
         for r in range(L):
             nc.scalar.activation(cc[:, r, :].rearrange("p (c m) -> p c m", m=L), rw_ps[:].rearrange("p m c -> p c m"), ACT.Copy, scale=cw_sb[:, r : r + 1])
 
-        wd_w, wd_s = deal_head(nc, sb, "wd", *wd_raw)
+        wd_w, wd_s = deal_head(nc, sb, "wd", wd_raw_w, wd_raw_s)
+        wv_w, wv_s = deal_head(nc, sb, "wv", wv_raw_w, wv_raw_s)
 
         xb = sb.tile([P, N, L], BF16, name="xb", align_bytes=64)
         xq = [sb.tile([P, HALF], U32, name=f"xq{h}", align_bytes=64) for h in range(2)]
@@ -100,17 +112,6 @@ def tile_attend_gml_pl_nce_kernel(
             nc.vector.tensor_copy(xb[:, 16 * lo : 16 * hi, L - 1], x_pl[L - 1][:].indirect(offsets[:, lo:hi]))
             nc.vector.quantize_mx(out=xq[h][:].bitcast(E4M3), scales=xs[h][:], in_=xb[:, h * HALF : (h + 1) * HALF, :].rearrange("p n r -> p (n r)"))
 
-        y_rows = y.rearrange("(p r) i -> p r i", r=L)
-        y_h = [sb.tile([P, L, HALF], F32, name=f"y_h{h}", tag=f"x_pl{h}") for h in range(2)]
-        for h in range(2):
-            nc.sync.dma_start(out=y_h[h][:], in_=y_rows[:, :, h * HALF : (h + 1) * HALF])
-
-
-        wv_w, wv_s = deal_head(nc, sb, "wv", *wv_raw)
-        gq = sb.tile([P, HALF + N], U32, name="gq", align_bytes=64)
-        gs = sb.tile([P, HALF + N], U8, name="gs", align_bytes=64)
-        nc.gpsimd.memset(gq[:, :HALF], 0)
-        nc.gpsimd.memset(gs[:, :HALF].bitcast(U32), 0)
         dx = [sb.tile([P, N], F32, name=f"dx{r}") for r in range(L)]
 
         def back(r, first, tag):
@@ -168,12 +169,14 @@ def tile_attend_gml_pl_nce_kernel(
             acc = back(r, HALF, f"bank{(4 + r) % 7}")
             if r == 0:
                 nc.scalar.copy(dx[0][:, HALF:], acc[:, HALF:])
-                nc.vector.tensor_copy(win[0][:].indirect(offsets[:, 16:]), dx[0][:, HALF:])
             else:
                 nc.scalar.copy(dx[r][:], acc[:])
+        for r in range(L):
+            if r == 0:
+                nc.vector.tensor_copy(win[0][:].indirect(offsets[:, 16:]), dx[0][:, HALF:])
+            else:
                 nc.vector.tensor_copy(win[r][:].indirect(offsets[:]), dx[r][:])
             nc.sync.dma_start(out=o_rows[:, r, :], in_=win[r][:])
-        for r in range(L):
             for first, w in zip(starts, WIDTHS) if r == L - 1 else [(0, T)]:
                 nc.scalar.copy(
                     pairs[:, L * first : L * (first + w)].rearrange("p (b u n e) -> p b u n e", u=2, n=BLK, e=2)[:, :, r // 2, :, r % 2],

@@ -21,9 +21,9 @@ ALU = mybir.AluOpType
 P = 128
 L = 4
 HALF = N // 2
-CH = 128
-BLK = 256
-WIDTHS = [256, 512, 512, 256, 256, 256]
+BLK = 128
+WIDTHS = [128, 256, 512, 512, 256, 256, 128]
+STORE_AFTER = [2, 3, 5, 6]
 
 
 def load_scales(nc, raw_s, scales):
@@ -71,11 +71,11 @@ def tile_attend_gml_pl_nce_kernel(
 
         nc.sync.dma_start(offsets[:], offs)
         nc.sync.dma_start(out=x_pl[0][:], in_=x_rows[:, 0, :])
-        nc.sync.dma_start(out=wd_raw_w[:].bitcast(I32), in_=wd_words[0].bitcast(I32))
+        nc.sync.dma_start(out=cw_sb[:], in_=cw.rearrange("(p r) o -> p (r o)", r=L))
         nc.sync.dma_start(out=rw_sb[:], in_=rw[0].rearrange("(c m) -> c m", m=L))
         load_scales(nc, wd_raw_s, wd_scales)
         nc.sync.dma_start(out=x_pl[1][:], in_=x_rows[:, 1, :])
-        nc.sync.dma_start(out=cw_sb[:], in_=cw.rearrange("(p r) o -> p (r o)", r=L))
+        nc.sync.dma_start(out=wd_raw_w[:].bitcast(I32), in_=wd_words[0].bitcast(I32))
         nc.sync.dma_start(out=wv_raw_w[:].bitcast(I32), in_=wv_words[0].bitcast(I32))
         load_scales(nc, wv_raw_s, wv_scales)
         for r in range(2, L):
@@ -87,8 +87,8 @@ def tile_attend_gml_pl_nce_kernel(
         make_identity(nc, ident[:])
         gq = sb.tile([P, HALF + N], U32, name="gq", align_bytes=64)
         gs = sb.tile([P, HALF + N], U8, name="gs", align_bytes=64)
-        nc.gpsimd.memset(gq[:, :HALF], 0)
-        nc.gpsimd.memset(gs[:, :HALF].bitcast(U32), 0)
+        nc.vector.memset(gq[:, :HALF], 0)
+        nc.vector.memset(gs[:, :HALF].bitcast(U32), 0)
         windows = [sb.tile([P, T], F32, name=f"win{r}") for r in range(L - 1)]
         for r in range(L - 1):
             nc.vector.memset(windows[r][:].bitcast(I32), 0)
@@ -100,15 +100,15 @@ def tile_attend_gml_pl_nce_kernel(
         for r in range(L):
             nc.scalar.activation(cc[:, r, :].rearrange("p (c m) -> p c m", m=L), rw_ps[:].rearrange("p m c -> p c m"), ACT.Copy, scale=cw_sb[:, r : r + 1])
 
-        wd_w, wd_s = deal_head(nc, sb, "wd", wd_raw_w, wd_raw_s)
-        wv_w, wv_s = deal_head(nc, sb, "wv", wv_raw_w, wv_raw_s)
-
         xb = sb.tile([P, N, L], BF16, name="xb", align_bytes=64)
         xq = [sb.tile([P, HALF], U32, name=f"xq{h}", align_bytes=64) for h in range(2)]
         xs = [sb.tile([P, HALF], U8, name=f"xs{h}", align_bytes=64) for h in range(2)]
-        for r in range(L - 1):
+        for r in range(2):
             nc.vector.tensor_copy(xb[:, :, r], x_pl[r][:].indirect(offsets[:]))
-        for h, (lo, hi) in enumerate([(0, 16), (14, 32)]):
+        wd_w, wd_s = deal_head(nc, sb, "wd", wd_raw_w, wd_raw_s)
+        wv_w, wv_s = deal_head(nc, sb, "wv", wv_raw_w, wv_raw_s)
+        nc.vector.tensor_copy(xb[:, :, 2], x_pl[2][:].indirect(offsets[:]))
+        for h, (lo, hi) in enumerate([(0, 18), (16, 32)]):
             nc.vector.tensor_copy(xb[:, 16 * lo : 16 * hi, L - 1], x_pl[L - 1][:].indirect(offsets[:, lo:hi]))
             nc.vector.quantize_mx(out=xq[h][:].bitcast(E4M3), scales=xs[h][:], in_=xb[:, h * HALF : (h + 1) * HALF, :].rearrange("p n r -> p (n r)"))
 
@@ -128,37 +128,49 @@ def tile_attend_gml_pl_nce_kernel(
             return acc
 
         gb = [sb.tile([P, HALF * L], BF16, name=f"gb{h}", align_bytes=64) for h in range(2)]
-        for k in range(N // CH):
-            h, j = divmod(k, 2)
-            cols = slice(j * CH, (j + 1) * CH)
-            sc = ps.tile([P, L, CH], F32, name=f"sc{k}", tag=f"bank{k}")
-            for r in range(L):
+        dif = [sb.tile([P, L, HALF], F32, name=f"dif{h}") for h in range(2)]
+
+        def difference(h, u):
+            lanes = slice(2 * u, 2 * u + 2)
+            sc = ps.tile([P, 2, HALF], F32, name=f"sc{h}{u}", tag=f"bank{2 * h + u}")
+            for e in range(2):
+                r = 2 * u + e
                 nc.tensor.matmul_mx(
-                    out=sc[:, r, :],
+                    out=sc[:, e, :],
                     lhsT=wd_w[:, 2 * P * r : 2 * P * (r + 1)].bitcast(E2M1),
                     lhsT_scale=wd_s[:, P * r : P * (r + 1)],
-                    rhs=xq[h][:, cols].bitcast(E4M3),
-                    rhs_scale=xs[h][:, cols],
+                    rhs=xq[h][:].bitcast(E4M3),
+                    rhs_scale=xs[h][:],
                     start=True,
                     stop=True,
                 )
-            sig = sb.tile([P, L, CH], F32, name=f"sig{k}")
+            sig = sb.tile([P, 2, HALF], F32, name=f"sig{h}{u}")
             nc.scalar.activation(sig[:], sc[:], ACT.Sigmoid)
-            dif = sb.tile([P, L, CH], F32, name=f"dif{k}")
-            nc.vector.tensor_tensor(dif[:], sig[:], y_h[h][:, :, cols], ALU.subtract)
+            nc.vector.tensor_tensor(dif[h][:, lanes, :], sig[:], y_h[h][:, lanes, :], ALU.subtract)
+
+        def weigh(h):
             nc.vector.tensor_tensor(
-                gb[h][:, j * CH * L : (j + 1) * CH * L].rearrange("p (c i r) -> p c r i", i=2, r=L),
-                dif[:].rearrange("p r (c i) -> p c r i", i=2),
-                cc[:, :, k * CH : (k + 1) * CH].rearrange("p r (c i) -> p c r i", i=2),
+                gb[h][:].rearrange("p (c i r) -> p c r i", i=2, r=L),
+                dif[h][:].rearrange("p r (c i) -> p c r i", i=2),
+                cc[:, :, h * HALF : (h + 1) * HALF].rearrange("p r (c i) -> p c r i", i=2),
                 ALU.mult,
             )
-            if j == 1:
-                nc.vector.quantize_mx(
-                    out=gq[:, (h + 1) * HALF : (h + 2) * HALF].bitcast(E5M2), scales=gs[:, (h + 1) * HALF : (h + 2) * HALF], in_=gb[h][:]
-                )
-            if k == 1:
-                early = back(0, 0, "bank7")
-        dx_early = sb.tile([P, HALF], F32, name="dx_early", tag="dif3")
+
+        def quantise_g(h):
+            nc.vector.quantize_mx(
+                out=gq[:, (h + 1) * HALF : (h + 2) * HALF].bitcast(E5M2), scales=gs[:, (h + 1) * HALF : (h + 2) * HALF], in_=gb[h][:]
+            )
+
+        difference(0, 0)
+        difference(0, 1)
+        difference(1, 0)
+        weigh(0)
+        difference(1, 1)
+        quantise_g(0)
+        early = back(0, 0, "bank7")
+        weigh(1)
+        quantise_g(1)
+        dx_early = sb.tile([P, HALF], F32, name="dx_early", tag="dif1")
         nc.scalar.copy(dx_early[:], early[:, HALF:])
 
         o_rows = out_0.rearrange("(p r) t -> p r t", r=L)
@@ -200,13 +212,17 @@ def tile_attend_gml_pl_nce_kernel(
                     in_=src.bitcast(I32).rearrange("p (b u n) -> p b n u", u=2, n=BLK),
                 )
 
+        oq = sb.tile([P, T], U32, name="oq", align_bytes=64)
+        stored = 0
         weave(0)
         for k, w in enumerate(WIDTHS):
             if k + 1 < len(WIDTHS):
                 weave(k + 1)
-            oq = sb.tile([P, w], U32, name=f"oq{k}", align_bytes=64)
-            nc.vector.quantize_mx(out=oq[:].bitcast(E4M3), scales=os_[:, starts[k] : starts[k] + w], in_=ob[k][:])
-            nc.sync.dma_start(out=o1[:, L * starts[k] : L * (starts[k] + w)].bitcast(I32), in_=oq[:].bitcast(I32))
+            end = starts[k] + w
+            nc.vector.quantize_mx(out=oq[:, starts[k] : end].bitcast(E4M3), scales=os_[:, starts[k] : end], in_=ob[k][:])
+            if k in STORE_AFTER:
+                nc.sync.dma_start(out=o1[:, L * stored : L * end].bitcast(I32), in_=oq[:, stored:end].bitcast(I32))
+                stored = end
         for q in range(4):
             queue = nc.scalar if q % 2 == 0 else nc.sync
             queue.dma_start(out=out_2[0, 4 * q : 4 * q + 4, :].bitcast(I32), in_=os_[32 * q : 32 * q + 4, :].bitcast(I32))

@@ -21,9 +21,9 @@ ALU = mybir.AluOpType
 P = 128
 L = 4
 HALF = N // 2
-BLK = 128
-WIDTHS = [128, 256, 512, 512, 256, 256, 128]
-STORE_AFTER = [2, 3, 5, 6]
+BLK = 256
+ORDER = [2, 0, 1, 3]
+VECTOR_COLS = 1024
 
 
 def load_scales(nc, raw_s, scales):
@@ -70,12 +70,12 @@ def tile_attend_gml_pl_nce_kernel(
         y_h = [sb.tile([P, L, HALF], F32, name=f"y_h{h}") for h in range(2)]
 
         nc.sync.dma_start(offsets[:], offs)
+        nc.scalar.dma_start(out=rw_sb[:], in_=rw[0].rearrange("(c m) -> c m", m=L))
+        nc.scalar.dma_start(out=cw_sb[:], in_=cw.rearrange("(p r) o -> p (r o)", r=L))
         nc.sync.dma_start(out=x_pl[0][:], in_=x_rows[:, 0, :])
-        nc.sync.dma_start(out=cw_sb[:], in_=cw.rearrange("(p r) o -> p (r o)", r=L))
-        nc.sync.dma_start(out=rw_sb[:], in_=rw[0].rearrange("(c m) -> c m", m=L))
+        nc.sync.dma_start(out=wd_raw_w[:].bitcast(I32), in_=wd_words[0].bitcast(I32))
         load_scales(nc, wd_raw_s, wd_scales)
         nc.sync.dma_start(out=x_pl[1][:], in_=x_rows[:, 1, :])
-        nc.sync.dma_start(out=wd_raw_w[:].bitcast(I32), in_=wd_words[0].bitcast(I32))
         nc.sync.dma_start(out=wv_raw_w[:].bitcast(I32), in_=wv_words[0].bitcast(I32))
         load_scales(nc, wv_raw_s, wv_scales)
         for r in range(2, L):
@@ -92,7 +92,7 @@ def tile_attend_gml_pl_nce_kernel(
         windows = [sb.tile([P, T], F32, name=f"win{r}") for r in range(L - 1)]
         for r in range(L - 1):
             nc.vector.memset(windows[r][:].bitcast(I32), 0)
-        win = windows + windows[:1]
+        win = windows + windows[2:]
         rw_ps = ps.tile([P, L, P], F32, name="rw_ps", tag="bank7")
         for m in range(L):
             nc.tensor.transpose(rw_ps[:, m, :], rw_sb[:, m : m + 1].to_broadcast([P, P]), ident[:])
@@ -103,9 +103,11 @@ def tile_attend_gml_pl_nce_kernel(
         xb = sb.tile([P, N, L], BF16, name="xb", align_bytes=64)
         xq = [sb.tile([P, HALF], U32, name=f"xq{h}", align_bytes=64) for h in range(2)]
         xs = [sb.tile([P, HALF], U8, name=f"xs{h}", align_bytes=64) for h in range(2)]
-        for r in range(2):
-            nc.vector.tensor_copy(xb[:, :, r], x_pl[r][:].indirect(offsets[:]))
+        xg = sb.tile([P, 2, N], BF16, name="xg")
+        nc.vector.tensor_copy(xg[:, 0, :], x_pl[0][:].indirect(offsets[:]))
         wd_w, wd_s = deal_head(nc, sb, "wd", wd_raw_w, wd_raw_s)
+        nc.vector.tensor_copy(xg[:, 1, :], x_pl[1][:].indirect(offsets[:]))
+        nc.scalar.copy(xb[:, :, 0:2], xg[:].rearrange("p r n -> p n r"))
         wv_w, wv_s = deal_head(nc, sb, "wv", wv_raw_w, wv_raw_s)
         nc.vector.tensor_copy(xb[:, :, 2], x_pl[2][:].indirect(offsets[:]))
         for h, (lo, hi) in enumerate([(0, 18), (16, 32)]):
@@ -167,62 +169,66 @@ def tile_attend_gml_pl_nce_kernel(
         weigh(0)
         difference(1, 1)
         quantise_g(0)
-        early = back(0, 0, "bank7")
+        early = back(ORDER[0], 0, "bank7")
         weigh(1)
         quantise_g(1)
         dx_early = sb.tile([P, HALF], F32, name="dx_early", tag="dif1")
         nc.scalar.copy(dx_early[:], early[:, HALF:])
 
         o_rows = out_0.rearrange("(p r) t -> p r t", r=L)
-        starts = [sum(WIDTHS[:k]) for k in range(len(WIDTHS))]
         pairs = sb.tile([P, T * L], BF16, name="pairs", align_bytes=64)
-        nc.vector.tensor_copy(win[0][:].indirect(offsets[:, :16]), dx_early[:])
-        for r in range(L):
-            acc = back(r, HALF, f"bank{(4 + r) % 7}")
-            if r == 0:
-                nc.scalar.copy(dx[0][:, HALF:], acc[:, HALF:])
+
+        def round_lane(copy, r, lo, hi):
+            copy(
+                pairs[:, L * lo : L * hi].rearrange("p (b u n e) -> p b u n e", u=2, n=BLK, e=2)[:, :, r // 2, :, r % 2],
+                win[r][:, lo:hi].rearrange("p (b n) -> p b n", n=BLK),
+            )
+
+        nc.vector.tensor_copy(win[ORDER[0]][:].indirect(offsets[:, :16]), dx_early[:])
+        for k, r in enumerate(ORDER):
+            acc = back(r, HALF, f"bank{(4 + k) % 7}")
+            if k == 0:
+                nc.scalar.copy(dx[r][:, HALF:], acc[:, HALF:])
             else:
                 nc.scalar.copy(dx[r][:], acc[:])
-        for r in range(L):
-            if r == 0:
-                nc.vector.tensor_copy(win[0][:].indirect(offsets[:, 16:]), dx[0][:, HALF:])
+        for k, r in enumerate(ORDER):
+            if k == 0:
+                nc.vector.tensor_copy(win[r][:].indirect(offsets[:, 16:]), dx[r][:, HALF:])
             else:
                 nc.vector.tensor_copy(win[r][:].indirect(offsets[:]), dx[r][:])
             nc.sync.dma_start(out=o_rows[:, r, :], in_=win[r][:])
-            for first, w in zip(starts, WIDTHS) if r == L - 1 else [(0, T)]:
-                nc.scalar.copy(
-                    pairs[:, L * first : L * (first + w)].rearrange("p (b u n e) -> p b u n e", u=2, n=BLK, e=2)[:, :, r // 2, :, r % 2],
-                    win[r][:, first : first + w].rearrange("p (b n) -> p b n", n=BLK),
-                )
+            if r < L - 1:
+                round_lane(nc.scalar.copy, r, 0, VECTOR_COLS)
+                round_lane(nc.scalar.copy, r, VECTOR_COLS, T)
 
         os_ = sb.tile([P, T], U8, name="os_", align_bytes=64)
-        o1 = out_1[0].rearrange("p n t -> p (n t)")
-        ob = [sb.tile([P, w * L], BF16, name=f"ob{k}", align_bytes=64) for k, w in enumerate(WIDTHS)]
-
-        def weave(k):
-            src = pairs[:, L * starts[k] : L * (starts[k] + WIDTHS[k])]
-            if k >= len(WIDTHS) - 2:
-                nc.scalar.copy(
-                    ob[k][:].bitcast(U32).rearrange("p (b n u) -> p b n u", n=BLK, u=2),
-                    src.bitcast(U32).rearrange("p (b u n) -> p b n u", u=2, n=BLK),
-                )
-            else:
-                nc.vector.tensor_copy(
-                    out=ob[k][:].bitcast(I32).rearrange("p (b n u) -> p b n u", n=BLK, u=2),
-                    in_=src.bitcast(I32).rearrange("p (b u n) -> p b n u", u=2, n=BLK),
-                )
-
         oq = sb.tile([P, T], U32, name="oq", align_bytes=64)
-        stored = 0
-        weave(0)
-        for k, w in enumerate(WIDTHS):
-            if k + 1 < len(WIDTHS):
-                weave(k + 1)
-            end = starts[k] + w
-            nc.vector.quantize_mx(out=oq[:, starts[k] : end].bitcast(E4M3), scales=os_[:, starts[k] : end], in_=ob[k][:])
-            if k in STORE_AFTER:
-                nc.sync.dma_start(out=o1[:, L * stored : L * end].bitcast(I32), in_=oq[:, stored:end].bitcast(I32))
-                stored = end
+        o1 = out_1[0].rearrange("p n t -> p (n t)")
+        ob = sb.tile([P, T * L], BF16, name="ob", align_bytes=64)
+
+        def weave(copy, word, lo, hi):
+            copy(
+                ob[:, L * lo : L * hi].bitcast(word).rearrange("p (b n u) -> p b n u", n=BLK, u=2),
+                pairs[:, L * lo : L * hi].bitcast(word).rearrange("p (b u n) -> p b n u", u=2, n=BLK),
+            )
+
+        def quantise_out(lo, hi):
+            nc.vector.quantize_mx(out=oq[:, lo:hi].bitcast(E4M3), scales=os_[:, lo:hi], in_=ob[:, L * lo : L * hi])
+
+        def store_codes(lo, hi):
+            nc.sync.dma_start(out=o1[:, L * lo : L * hi].bitcast(I32), in_=oq[:, lo:hi].bitcast(I32))
+
+        for lo, hi in [(0, 512), (512, 1024)]:
+            round_lane(nc.vector.tensor_copy, L - 1, lo, hi)
+        for lo, hi in [(0, 512), (512, 1024)]:
+            weave(nc.vector.tensor_copy, I32, lo, hi)
+        round_lane(nc.scalar.copy, L - 1, 1024, 1536)
+        round_lane(nc.scalar.copy, L - 1, 1536, 2048)
+        for lo, hi in [(1024, 1536), (1536, 1792), (1792, 2048)]:
+            weave(nc.scalar.copy, U32, lo, hi)
+        for lo, hi in [(0, 512), (512, 1024), (1024, 1536), (1536, 1792), (1792, 2048)]:
+            quantise_out(lo, hi)
+            store_codes(lo, hi)
         for q in range(4):
             queue = nc.scalar if q % 2 == 0 else nc.sync
             queue.dma_start(out=out_2[0, 4 * q : 4 * q + 4, :].bitcast(I32), in_=os_[32 * q : 32 * q + 4, :].bitcast(I32))

@@ -31,18 +31,22 @@ def load_scales(nc, raw_s, scales):
         nc.sync.dma_start(out=raw_s[32 * q : 32 * q + 4, :].bitcast(I32), in_=scales[0, 4 * q : 4 * q + 4, :].bitcast(I32))
 
 
-def deal_head(nc, pool, name, raw_w, raw_s):
+def deal_words(nc, pool, name, raw_w):
     w = pool.tile([P, 2 * 512], U8, name=name + "_w", align_bytes=64)
-    s = pool.tile([P, 512], U8, name=name + "_s", align_bytes=64)
     nc.vector.tensor_copy(
         out=w[:].bitcast(U16).rearrange("p (r s) -> p r s", r=L),
         in_=raw_w[:].bitcast(U16).rearrange("p (s r) -> p r s", r=L),
     )
+    return w
+
+
+def deal_scales(nc, pool, name, raw_s):
+    s = pool.tile([P, 512], U8, name=name + "_s", align_bytes=64)
     nc.vector.tensor_copy(
         out=s[:].rearrange("p (r s) -> p r s", r=L),
         in_=raw_s[:].rearrange("p (s r) -> p r s", r=L),
     )
-    return w, s
+    return s
 
 
 def tile_attend_gml_pl_nce_kernel(
@@ -69,17 +73,17 @@ def tile_attend_gml_pl_nce_kernel(
         y_rows = y.rearrange("(p r) i -> p r i", r=L)
         y_h = [sb.tile([P, L, HALF], F32, name=f"y_h{h}") for h in range(2)]
 
-        nc.sync.dma_start(offsets[:], offs)
+        nc.sync.dma_start(out=x_pl[0][:], in_=x_rows[:, 0, :])
         nc.scalar.dma_start(out=rw_sb[:], in_=rw[0].rearrange("(c m) -> c m", m=L))
         nc.scalar.dma_start(out=cw_sb[:], in_=cw.rearrange("(p r) o -> p (r o)", r=L))
-        nc.sync.dma_start(out=x_pl[0][:], in_=x_rows[:, 0, :])
+        nc.sync.dma_start(offsets[:], offs)
+        nc.sync.dma_start(out=x_pl[1][:], in_=x_rows[:, 1, :])
         nc.sync.dma_start(out=wd_raw_w[:].bitcast(I32), in_=wd_words[0].bitcast(I32))
         load_scales(nc, wd_raw_s, wd_scales)
-        nc.sync.dma_start(out=x_pl[1][:], in_=x_rows[:, 1, :])
-        nc.sync.dma_start(out=wv_raw_w[:].bitcast(I32), in_=wv_words[0].bitcast(I32))
+        nc.sync.dma_start(out=x_pl[2][:], in_=x_rows[:, 2, :])
         load_scales(nc, wv_raw_s, wv_scales)
-        for r in range(2, L):
-            nc.sync.dma_start(out=x_pl[r][:], in_=x_rows[:, r, :])
+        nc.sync.dma_start(out=x_pl[3][:], in_=x_rows[:, 3, :])
+        nc.sync.dma_start(out=wv_raw_w[:].bitcast(I32), in_=wv_words[0].bitcast(I32))
         for h in range(2):
             nc.sync.dma_start(out=y_h[h][:], in_=y_rows[:, :, h * HALF : (h + 1) * HALF])
 
@@ -103,16 +107,21 @@ def tile_attend_gml_pl_nce_kernel(
         xb = sb.tile([P, N, L], BF16, name="xb", align_bytes=64)
         xq = [sb.tile([P, HALF], U32, name=f"xq{h}", align_bytes=64) for h in range(2)]
         xs = [sb.tile([P, HALF], U8, name=f"xs{h}", align_bytes=64) for h in range(2)]
-        xg = sb.tile([P, 2, N], BF16, name="xg")
-        nc.vector.tensor_copy(xg[:, 0, :], x_pl[0][:].indirect(offsets[:]))
-        wd_w, wd_s = deal_head(nc, sb, "wd", wd_raw_w, wd_raw_s)
-        nc.vector.tensor_copy(xg[:, 1, :], x_pl[1][:].indirect(offsets[:]))
-        nc.scalar.copy(xb[:, :, 0:2], xg[:].rearrange("p r n -> p n r"))
-        wv_w, wv_s = deal_head(nc, sb, "wv", wv_raw_w, wv_raw_s)
+        nc.vector.tensor_copy(xb[:, :, 0], x_pl[0][:].indirect(offsets[:]))
+        nc.vector.tensor_copy(xb[:, :, 1], x_pl[1][:].indirect(offsets[:]))
+        wd_w = deal_words(nc, sb, "wd", wd_raw_w)
+        wd_s = deal_scales(nc, sb, "wd", wd_raw_s)
+        wv_s = deal_scales(nc, sb, "wv", wv_raw_s)
         nc.vector.tensor_copy(xb[:, :, 2], x_pl[2][:].indirect(offsets[:]))
-        for h, (lo, hi) in enumerate([(0, 18), (16, 32)]):
-            nc.vector.tensor_copy(xb[:, 16 * lo : 16 * hi, L - 1], x_pl[L - 1][:].indirect(offsets[:, lo:hi]))
-            nc.vector.quantize_mx(out=xq[h][:].bitcast(E4M3), scales=xs[h][:], in_=xb[:, h * HALF : (h + 1) * HALF, :].rearrange("p n r -> p (n r)"))
+
+        def finish_half(h):
+            cols = slice(h * HALF, (h + 1) * HALF)
+            nc.vector.tensor_copy(xb[:, cols, L - 1], x_pl[L - 1][:].indirect(offsets[:, 16 * h : 16 * h + 16]))
+            nc.vector.quantize_mx(out=xq[h][:].bitcast(E4M3), scales=xs[h][:], in_=xb[:, cols, :].rearrange("p n r -> p (n r)"))
+
+        finish_half(0)
+        wv_w = deal_words(nc, sb, "wv", wv_raw_w)
+        finish_half(1)
 
         dx = [sb.tile([P, N], F32, name=f"dx{r}") for r in range(L)]
 
@@ -132,11 +141,11 @@ def tile_attend_gml_pl_nce_kernel(
         gb = [sb.tile([P, HALF * L], BF16, name=f"gb{h}", align_bytes=64) for h in range(2)]
         dif = [sb.tile([P, L, HALF], F32, name=f"dif{h}") for h in range(2)]
 
-        def difference(h, u):
-            lanes = slice(2 * u, 2 * u + 2)
-            sc = ps.tile([P, 2, HALF], F32, name=f"sc{h}{u}", tag=f"bank{2 * h + u}")
-            for e in range(2):
-                r = 2 * u + e
+        def difference(h, first, count, bank):
+            lanes = slice(first, first + count)
+            sc = ps.tile([P, count, HALF], F32, name=f"sc{bank}", tag=f"bank{bank}")
+            for e in range(count):
+                r = first + e
                 nc.tensor.matmul_mx(
                     out=sc[:, e, :],
                     lhsT=wd_w[:, 2 * P * r : 2 * P * (r + 1)].bitcast(E2M1),
@@ -146,7 +155,7 @@ def tile_attend_gml_pl_nce_kernel(
                     start=True,
                     stop=True,
                 )
-            sig = sb.tile([P, 2, HALF], F32, name=f"sig{h}{u}")
+            sig = sb.tile([P, count, HALF], F32, name=f"sig{bank}")
             nc.scalar.activation(sig[:], sc[:], ACT.Sigmoid)
             nc.vector.tensor_tensor(dif[h][:, lanes, :], sig[:], y_h[h][:, lanes, :], ALU.subtract)
 
@@ -163,11 +172,11 @@ def tile_attend_gml_pl_nce_kernel(
                 out=gq[:, (h + 1) * HALF : (h + 2) * HALF].bitcast(E5M2), scales=gs[:, (h + 1) * HALF : (h + 2) * HALF], in_=gb[h][:]
             )
 
-        difference(0, 0)
-        difference(0, 1)
-        difference(1, 0)
+        for r in range(L):
+            difference(0, r, 1, r)
         weigh(0)
-        difference(1, 1)
+        difference(1, 0, 2, 4)
+        difference(1, 2, 2, 5)
         quantise_g(0)
         early = back(ORDER[0], 0, "bank7")
         weigh(1)
@@ -186,7 +195,7 @@ def tile_attend_gml_pl_nce_kernel(
 
         nc.vector.tensor_copy(win[ORDER[0]][:].indirect(offsets[:, :16]), dx_early[:])
         for k, r in enumerate(ORDER):
-            acc = back(r, HALF, f"bank{(4 + k) % 7}")
+            acc = back(r, HALF, f"bank{(6 + k) % 7}")
             if k == 0:
                 nc.scalar.copy(dx[r][:, HALF:], acc[:, HALF:])
             else:

@@ -81,11 +81,11 @@ def tile_attend_gml_pl_nce_kernel(
         nc.sync.dma_start(out=wd_raw_w[:].bitcast(I32), in_=wd_words[0].bitcast(I32))
         load_scales(nc, wd_raw_s, wd_scales)
         nc.sync.dma_start(out=x_pl[2][:], in_=x_rows[:, 2, :])
-        load_scales(nc, wv_raw_s, wv_scales)
         nc.sync.dma_start(out=x_pl[3][:], in_=x_rows[:, 3, :])
+        load_scales(nc, wv_raw_s, wv_scales)
         nc.sync.dma_start(out=wv_raw_w[:].bitcast(I32), in_=wv_words[0].bitcast(I32))
-        for h in range(2):
-            nc.sync.dma_start(out=y_h[h][:], in_=y_rows[:, :, h * HALF : (h + 1) * HALF])
+        nc.sync.dma_start(out=y_h[0][:], in_=y_rows[:, :, :HALF])
+        nc.sync.dma_start(out=y_h[1][:], in_=y_rows[:, :, HALF:])
 
         ident = sb.tile([P, P], F32, name="ident")
         make_identity(nc, ident[:])
@@ -111,7 +111,6 @@ def tile_attend_gml_pl_nce_kernel(
         nc.vector.tensor_copy(xb[:, :, 1], x_pl[1][:].indirect(offsets[:]))
         wd_w = deal_words(nc, sb, "wd", wd_raw_w)
         wd_s = deal_scales(nc, sb, "wd", wd_raw_s)
-        wv_s = deal_scales(nc, sb, "wv", wv_raw_s)
         nc.vector.tensor_copy(xb[:, :, 2], x_pl[2][:].indirect(offsets[:]))
 
         def finish_half(h):
@@ -120,8 +119,9 @@ def tile_attend_gml_pl_nce_kernel(
             nc.vector.quantize_mx(out=xq[h][:].bitcast(E4M3), scales=xs[h][:], in_=xb[:, cols, :].rearrange("p n r -> p (n r)"))
 
         finish_half(0)
-        wv_w = deal_words(nc, sb, "wv", wv_raw_w)
         finish_half(1)
+        wv_w = deal_words(nc, sb, "wv", wv_raw_w)
+        wv_s = deal_scales(nc, sb, "wv", wv_raw_s)
 
         dx = [sb.tile([P, N], F32, name=f"dx{r}") for r in range(L)]
 
@@ -210,7 +210,7 @@ def tile_attend_gml_pl_nce_kernel(
                 round_lane(nc.scalar.copy, r, 0, VECTOR_COLS)
                 round_lane(nc.scalar.copy, r, VECTOR_COLS, T)
 
-        os_ = sb.tile([P, T], U8, name="os_", align_bytes=64)
+        os_ = sb.tile([P, 512], U8, name="os_", align_bytes=64)
         oq = sb.tile([P, T], U32, name="oq", align_bytes=64)
         o1 = out_1[0].rearrange("p n t -> p (n t)")
         ob = sb.tile([P, T * L], BF16, name="ob", align_bytes=64)
@@ -222,7 +222,8 @@ def tile_attend_gml_pl_nce_kernel(
             )
 
         def quantise_out(lo, hi):
-            nc.vector.quantize_mx(out=oq[:, lo:hi].bitcast(E4M3), scales=os_[:, lo:hi], in_=ob[:, L * lo : L * hi])
+            j, first = divmod(lo, 512)
+            nc.vector.quantize_mx(out=oq[:, lo:hi].bitcast(E4M3), scales=os_[4 * j :, first : first + hi - lo], in_=ob[:, L * lo : L * hi])
 
         def store_codes(lo, hi):
             nc.sync.dma_start(out=o1[:, L * lo : L * hi].bitcast(I32), in_=oq[:, lo:hi].bitcast(I32))
@@ -236,8 +237,12 @@ def tile_attend_gml_pl_nce_kernel(
         for lo, hi in [(1024, 1536), (1536, 1792), (1792, 2048)]:
             weave(nc.scalar.copy, U32, lo, hi)
         for lo, hi in [(0, 512), (512, 1024), (1024, 1536), (1536, 1792), (1792, 2048)]:
-            quantise_out(lo, hi)
+            for first in range(lo, hi, 256):
+                quantise_out(first, first + 256)
             store_codes(lo, hi)
         for q in range(4):
             queue = nc.scalar if q % 2 == 0 else nc.sync
-            queue.dma_start(out=out_2[0, 4 * q : 4 * q + 4, :].bitcast(I32), in_=os_[32 * q : 32 * q + 4, :].bitcast(I32))
+            queue.dma_start(
+                out=out_2[0, 4 * q : 4 * q + 4, :].bitcast(I32).rearrange("f (j n) -> j f n", j=4),
+                in_=os_[32 * q : 32 * q + 16, :].bitcast(I32),
+            )

@@ -20,14 +20,25 @@ ALU = mybir.AluOpType
 
 P = 128
 L = 4
+QUADRANTS = 4
 HALF = N // 2
-BLK = 256
+HALF_COLS = HALF // 16
+
 ORDER = [2, 0, 1, 3]
-VECTOR_COLS = 1024
+EARLY = 2
+
+VECTOR_COLS = 1280
+VECTOR_PIECES = [(0, 512), (512, 1024), (1024, VECTOR_COLS)]
+SCALAR_ROUNDS = [(VECTOR_COLS, 1536), (1536, T)]
+SCALAR_WEAVES = [(VECTOR_COLS, 1536), (1536, 1792), (1792, 1920), (1920, T)]
+CODE_STORES = [(0, 512), (512, 1024), (1024, 1536), (1536, 1920), (1920, T)]
+BLK = 128
+PLANE = T // 4
+QUANT = PLANE // 2
 
 
 def load_scales(nc, raw_s, scales):
-    for q in range(4):
+    for q in range(QUADRANTS):
         nc.sync.dma_start(out=raw_s[32 * q : 32 * q + 4, :].bitcast(I32), in_=scales[0, 4 * q : 4 * q + 4, :].bitcast(I32))
 
 
@@ -67,77 +78,65 @@ def tile_attend_gml_pl_nce_kernel(
 
         offsets = lists.tile([P, N // 16], U16, name="offsets")
         x_rows = xT.rearrange("(p r) t -> p r t", r=L)
-        x_pl = [sb.tile([P, T], F32, name=f"x_pl{r}") for r in range(L)]
+        x_lane = [sb.tile([P, T], F32, name=f"x_pl{r}") for r in range(L)]
         cw_sb = sb.tile([P, L], F32, name="cw_sb")
         rw_sb = sb.tile([P, L], F32, name="rw_sb")
         y_rows = y.rearrange("(p r) i -> p r i", r=L)
-        y_h = [sb.tile([P, L, HALF], F32, name=f"y_h{h}") for h in range(2)]
+        y_half = [sb.tile([P, L, HALF], F32, name=f"y_h{h}") for h in range(2)]
 
-        nc.sync.dma_start(out=x_pl[0][:], in_=x_rows[:, 0, :])
+        nc.sync.dma_start(out=x_lane[0][:], in_=x_rows[:, 0, :])
         nc.scalar.dma_start(out=rw_sb[:], in_=rw[0].rearrange("(c m) -> c m", m=L))
         nc.scalar.dma_start(out=cw_sb[:], in_=cw.rearrange("(p r) o -> p (r o)", r=L))
         nc.sync.dma_start(offsets[:], offs)
-        nc.sync.dma_start(out=x_pl[1][:], in_=x_rows[:, 1, :])
+        nc.sync.dma_start(out=x_lane[1][:], in_=x_rows[:, 1, :])
         nc.sync.dma_start(out=wd_raw_w[:].bitcast(I32), in_=wd_words[0].bitcast(I32))
         load_scales(nc, wd_raw_s, wd_scales)
-        nc.sync.dma_start(out=x_pl[2][:], in_=x_rows[:, 2, :])
-        nc.sync.dma_start(out=x_pl[3][:], in_=x_rows[:, 3, :])
+        nc.sync.dma_start(out=x_lane[2][:], in_=x_rows[:, 2, :])
+        nc.sync.dma_start(out=x_lane[3][:], in_=x_rows[:, 3, :])
         load_scales(nc, wv_raw_s, wv_scales)
         nc.sync.dma_start(out=wv_raw_w[:].bitcast(I32), in_=wv_words[0].bitcast(I32))
-        nc.sync.dma_start(out=y_h[0][:], in_=y_rows[:, :, :HALF])
-        nc.sync.dma_start(out=y_h[1][:], in_=y_rows[:, :, HALF:])
+        nc.sync.dma_start(out=y_half[0][:], in_=y_rows[:, :, :HALF])
+        nc.sync.dma_start(out=y_half[1][:], in_=y_rows[:, :, HALF:])
 
         ident = sb.tile([P, P], F32, name="ident")
         make_identity(nc, ident[:])
+
         gq = sb.tile([P, HALF + N], U32, name="gq", align_bytes=64)
         gs = sb.tile([P, HALF + N], U8, name="gs", align_bytes=64)
         nc.vector.memset(gq[:, :HALF], 0)
         nc.vector.memset(gs[:, :HALF].bitcast(U32), 0)
+
         windows = [sb.tile([P, T], F32, name=f"win{r}") for r in range(L - 1)]
-        for r in range(L - 1):
-            nc.vector.memset(windows[r][:].bitcast(I32), 0)
-        win = windows + windows[2:]
+        for window in windows:
+            nc.vector.memset(window[:].bitcast(I32), 0)
+        win = windows + [windows[2]]
+
         rw_ps = ps.tile([P, L, P], F32, name="rw_ps", tag="bank7")
         for m in range(L):
             nc.tensor.transpose(rw_ps[:, m, :], rw_sb[:, m : m + 1].to_broadcast([P, P]), ident[:])
         cc = sb.tile([P, L, N], F32, name="cc")
         for r in range(L):
-            nc.scalar.activation(cc[:, r, :].rearrange("p (c m) -> p c m", m=L), rw_ps[:].rearrange("p m c -> p c m"), ACT.Copy, scale=cw_sb[:, r : r + 1])
+            nc.scalar.activation(
+                cc[:, r, :].rearrange("p (c m) -> p c m", m=L), rw_ps[:].rearrange("p m c -> p c m"), ACT.Copy, scale=cw_sb[:, r : r + 1]
+            )
 
         xb = sb.tile([P, N, L], BF16, name="xb", align_bytes=64)
         xq = [sb.tile([P, HALF], U32, name=f"xq{h}", align_bytes=64) for h in range(2)]
         xs = [sb.tile([P, HALF], U8, name=f"xs{h}", align_bytes=64) for h in range(2)]
-        nc.vector.tensor_copy(xb[:, :, 0], x_pl[0][:].indirect(offsets[:]))
-        nc.vector.tensor_copy(xb[:, :, 1], x_pl[1][:].indirect(offsets[:]))
+        nc.vector.tensor_copy(xb[:, :, 0], x_lane[0][:].indirect(offsets[:]))
+        nc.vector.tensor_copy(xb[:, :, 1], x_lane[1][:].indirect(offsets[:]))
         wd_w = deal_words(nc, sb, "wd", wd_raw_w)
         wd_s = deal_scales(nc, sb, "wd", wd_raw_s)
-        nc.vector.tensor_copy(xb[:, :, 2], x_pl[2][:].indirect(offsets[:]))
-
-        def finish_half(h):
+        nc.vector.tensor_copy(xb[:, :, 2], x_lane[2][:].indirect(offsets[:]))
+        entries = [offsets[:, h * HALF_COLS : (h + 1) * HALF_COLS] for h in range(2)]
+        for h in range(2):
             cols = slice(h * HALF, (h + 1) * HALF)
-            nc.vector.tensor_copy(xb[:, cols, L - 1], x_pl[L - 1][:].indirect(offsets[:, 16 * h : 16 * h + 16]))
+            nc.vector.tensor_copy(xb[:, cols, 3], x_lane[3][:].indirect(entries[h]))
             nc.vector.quantize_mx(out=xq[h][:].bitcast(E4M3), scales=xs[h][:], in_=xb[:, cols, :].rearrange("p n r -> p (n r)"))
-
-        finish_half(0)
-        finish_half(1)
         wv_w = deal_words(nc, sb, "wv", wv_raw_w)
         wv_s = deal_scales(nc, sb, "wv", wv_raw_s)
 
         dx = [sb.tile([P, N], F32, name=f"dx{r}") for r in range(L)]
-
-        def back(r, first, tag):
-            acc = ps.tile([P, N], F32, name=f"dx_ps{r}", tag=tag)
-            nc.tensor.matmul_mx(
-                out=acc[:],
-                lhsT=wv_w[:, 2 * P * r : 2 * P * (r + 1)].bitcast(E2M1),
-                lhsT_scale=wv_s[:, P * r : P * (r + 1)],
-                rhs=gq[:, first : first + N].bitcast(E5M2),
-                rhs_scale=gs[:, first : first + N],
-                start=True,
-                stop=True,
-            )
-            return acc
-
         gb = [sb.tile([P, HALF * L], BF16, name=f"gb{h}", align_bytes=64) for h in range(2)]
         dif = [sb.tile([P, L, HALF], F32, name=f"dif{h}") for h in range(2)]
 
@@ -157,7 +156,7 @@ def tile_attend_gml_pl_nce_kernel(
                 )
             sig = sb.tile([P, count, HALF], F32, name=f"sig{bank}")
             nc.scalar.activation(sig[:], sc[:], ACT.Sigmoid)
-            nc.vector.tensor_tensor(dif[h][:, lanes, :], sig[:], y_h[h][:, lanes, :], ALU.subtract)
+            nc.vector.tensor_tensor(dif[h][:, lanes, :], sig[:], y_half[h][:, lanes, :], ALU.subtract)
 
         def weigh(h):
             nc.vector.tensor_tensor(
@@ -168,9 +167,21 @@ def tile_attend_gml_pl_nce_kernel(
             )
 
         def quantise_g(h):
-            nc.vector.quantize_mx(
-                out=gq[:, (h + 1) * HALF : (h + 2) * HALF].bitcast(E5M2), scales=gs[:, (h + 1) * HALF : (h + 2) * HALF], in_=gb[h][:]
+            cols = slice((h + 1) * HALF, (h + 2) * HALF)
+            nc.vector.quantize_mx(out=gq[:, cols].bitcast(E5M2), scales=gs[:, cols], in_=gb[h][:])
+
+        def back(r, first, bank):
+            acc = ps.tile([P, N], F32, name=f"dx_ps{r}", tag=f"bank{bank}")
+            nc.tensor.matmul_mx(
+                out=acc[:],
+                lhsT=wv_w[:, 2 * P * r : 2 * P * (r + 1)].bitcast(E2M1),
+                lhsT_scale=wv_s[:, P * r : P * (r + 1)],
+                rhs=gq[:, first : first + N].bitcast(E5M2),
+                rhs_scale=gs[:, first : first + N],
+                start=True,
+                stop=True,
             )
+            return acc
 
         for r in range(L):
             difference(0, r, 1, r)
@@ -178,13 +189,14 @@ def tile_attend_gml_pl_nce_kernel(
         difference(1, 0, 2, 4)
         difference(1, 2, 2, 5)
         quantise_g(0)
-        early = back(ORDER[0], 0, "bank7")
+        early = [back(r, 0, bank) for r, bank in zip(ORDER[:EARLY], (7, 3))]
         weigh(1)
         quantise_g(1)
-        dx_early = sb.tile([P, HALF], F32, name="dx_early", tag="dif1")
-        nc.scalar.copy(dx_early[:], early[:, HALF:])
+        for r, acc in zip(ORDER[:EARLY], early):
+            nc.scalar.copy(dx[r][:, :HALF], acc[:, HALF:])
+        for r in ORDER[:EARLY]:
+            nc.vector.tensor_copy(win[r][:].indirect(entries[0]), dx[r][:, :HALF])
 
-        o_rows = out_0.rearrange("(p r) t -> p r t", r=L)
         pairs = sb.tile([P, T * L], BF16, name="pairs", align_bytes=64)
 
         def round_lane(copy, r, lo, hi):
@@ -193,26 +205,24 @@ def tile_attend_gml_pl_nce_kernel(
                 win[r][:, lo:hi].rearrange("p (b n) -> p b n", n=BLK),
             )
 
-        nc.vector.tensor_copy(win[ORDER[0]][:].indirect(offsets[:, :16]), dx_early[:])
+        for k, (r, bank) in enumerate(zip(ORDER, (6, 0, 1, 2))):
+            acc = back(r, HALF, bank)
+            todo = slice(HALF, N) if k < EARLY else slice(0, N)
+            nc.scalar.copy(dx[r][:, todo], acc[:, todo])
+        o_rows = out_0.rearrange("(p r) t -> p r t", r=L)
         for k, r in enumerate(ORDER):
-            acc = back(r, HALF, f"bank{(6 + k) % 7}")
-            if k == 0:
-                nc.scalar.copy(dx[r][:, HALF:], acc[:, HALF:])
-            else:
-                nc.scalar.copy(dx[r][:], acc[:])
-        for k, r in enumerate(ORDER):
-            if k == 0:
-                nc.vector.tensor_copy(win[r][:].indirect(offsets[:, 16:]), dx[r][:, HALF:])
+            if k < EARLY:
+                nc.vector.tensor_copy(win[r][:].indirect(entries[1]), dx[r][:, HALF:])
             else:
                 nc.vector.tensor_copy(win[r][:].indirect(offsets[:]), dx[r][:])
             nc.sync.dma_start(out=o_rows[:, r, :], in_=win[r][:])
-            if r < L - 1:
+            if r != ORDER[-1]:
                 round_lane(nc.scalar.copy, r, 0, VECTOR_COLS)
                 round_lane(nc.scalar.copy, r, VECTOR_COLS, T)
 
-        os_ = sb.tile([P, 512], U8, name="os_", align_bytes=64)
-        oq = sb.tile([P, T], U32, name="oq", align_bytes=64)
-        o1 = out_1[0].rearrange("p n t -> p (n t)")
+        o_scales = sb.tile([P, PLANE], U8, name="os_", align_bytes=64)
+        o_codes = sb.tile([P, T], U32, name="oq", align_bytes=64)
+        o_words = out_1[0].rearrange("p n t -> p (n t)")
         ob = sb.tile([P, T * L], BF16, name="ob", align_bytes=64)
 
         def weave(copy, word, lo, hi):
@@ -221,28 +231,27 @@ def tile_attend_gml_pl_nce_kernel(
                 pairs[:, L * lo : L * hi].bitcast(word).rearrange("p (b u n) -> p b n u", u=2, n=BLK),
             )
 
-        def quantise_out(lo, hi):
-            j, first = divmod(lo, 512)
-            nc.vector.quantize_mx(out=oq[:, lo:hi].bitcast(E4M3), scales=os_[4 * j :, first : first + hi - lo], in_=ob[:, L * lo : L * hi])
-
-        def store_codes(lo, hi):
-            nc.sync.dma_start(out=o1[:, L * lo : L * hi].bitcast(I32), in_=oq[:, lo:hi].bitcast(I32))
-
-        for lo, hi in [(0, 512), (512, 1024)]:
-            round_lane(nc.vector.tensor_copy, L - 1, lo, hi)
-        for lo, hi in [(0, 512), (512, 1024)]:
+        for lo, hi in VECTOR_PIECES:
+            round_lane(nc.vector.tensor_copy, ORDER[-1], lo, hi)
+        for lo, hi in VECTOR_PIECES:
             weave(nc.vector.tensor_copy, I32, lo, hi)
-        round_lane(nc.scalar.copy, L - 1, 1024, 1536)
-        round_lane(nc.scalar.copy, L - 1, 1536, 2048)
-        for lo, hi in [(1024, 1536), (1536, 1792), (1792, 2048)]:
+        for lo, hi in SCALAR_ROUNDS:
+            round_lane(nc.scalar.copy, ORDER[-1], lo, hi)
+        for lo, hi in SCALAR_WEAVES:
             weave(nc.scalar.copy, U32, lo, hi)
-        for lo, hi in [(0, 512), (512, 1024), (1024, 1536), (1536, 1792), (1792, 2048)]:
-            for first in range(lo, hi, 256):
-                quantise_out(first, first + 256)
-            store_codes(lo, hi)
-        for q in range(4):
+        for lo, hi in CODE_STORES:
+            for first in range(lo, hi, QUANT):
+                last = min(first + QUANT, hi)
+                j, col = divmod(first, PLANE)
+                nc.vector.quantize_mx(
+                    out=o_codes[:, first:last].bitcast(E4M3),
+                    scales=o_scales[4 * j :, col : col + last - first],
+                    in_=ob[:, L * first : L * last],
+                )
+            nc.sync.dma_start(out=o_words[:, L * lo : L * hi].bitcast(I32), in_=o_codes[:, lo:hi].bitcast(I32))
+        for q in range(QUADRANTS):
             queue = nc.scalar if q % 2 == 0 else nc.sync
             queue.dma_start(
                 out=out_2[0, 4 * q : 4 * q + 4, :].bitcast(I32).rearrange("f (j n) -> j f n", j=4),
-                in_=os_[32 * q : 32 * q + 16, :].bitcast(I32),
+                in_=o_scales[32 * q : 32 * q + 16, :].bitcast(I32),
             )

@@ -27,10 +27,10 @@ HALF_COLS = HALF // 16
 ORDER = [2, 0, 1, 3]
 EARLY = 2
 
-VECTOR_COLS = 1280
-VECTOR_PIECES = [(0, 512), (512, 1024), (1024, VECTOR_COLS)]
+VECTOR_COLS = 1024
+VECTOR_PIECES = [(0, 512), (512, VECTOR_COLS)]
 SCALAR_ROUNDS = [(VECTOR_COLS, 1536), (1536, T)]
-SCALAR_WEAVES = [(VECTOR_COLS, 1536), (1536, 1792), (1792, 1920), (1920, T)]
+SCALAR_WEAVES = [(VECTOR_COLS, 1280), (1280, 1536), (1536, 1792), (1792, 1920), (1920, T)]
 CODE_STORES = [(0, 512), (512, 1024), (1024, 1536), (1536, 1920), (1920, T)]
 BLK = 128
 PLANE = T // 4
@@ -199,6 +199,9 @@ def tile_attend_gml_pl_nce_kernel(
 
         pairs = sb.tile([P, T * L], BF16, name="pairs", align_bytes=64)
 
+        def gpsimd_copy(out, in_):
+            nc.gpsimd.tensor_scalar(out, in_, 1.0, 0.0, ALU.mult, ALU.add)
+
         def round_lane(copy, r, lo, hi):
             copy(
                 pairs[:, L * lo : L * hi].rearrange("p (b u n e) -> p b u n e", u=2, n=BLK, e=2)[:, :, r // 2, :, r % 2],
@@ -218,7 +221,7 @@ def tile_attend_gml_pl_nce_kernel(
             nc.sync.dma_start(out=o_rows[:, r, :], in_=win[r][:])
             if r != ORDER[-1]:
                 round_lane(nc.scalar.copy, r, 0, VECTOR_COLS)
-                round_lane(nc.scalar.copy, r, VECTOR_COLS, T)
+                round_lane(gpsimd_copy, r, VECTOR_COLS, T)
 
         o_scales = sb.tile([P, PLANE], U8, name="os_", align_bytes=64)
         o_codes = sb.tile([P, T], U32, name="oq", align_bytes=64)

@@ -138,7 +138,7 @@ def tile_attend_gml_pl_nce_kernel(
 
         dx = [sb.tile([P, N], F32, name=f"dx{r}") for r in range(L)]
         gb = [sb.tile([P, HALF * L], BF16, name=f"gb{h}", align_bytes=64) for h in range(2)]
-        dif = [sb.tile([P, L, HALF], F32, name=f"dif{h}") for h in range(2)]
+        dif = [sb.tile([P, L, HALF], F32, name="dif0", tag="dif")]
 
         def difference(h, first, count, bank):
             lanes = slice(first, first + count)
@@ -158,11 +158,27 @@ def tile_attend_gml_pl_nce_kernel(
             nc.scalar.activation(sig[:], sc[:], ACT.Sigmoid)
             nc.vector.tensor_tensor(dif[h][:, lanes, :], sig[:], y_half[h][:, lanes, :], ALU.subtract)
 
-        def weigh(h):
-            nc.vector.tensor_tensor(
-                gb[h][:].rearrange("p (c i r) -> p c r i", i=2, r=L),
-                dif[h][:].rearrange("p r (c i) -> p c r i", i=2),
-                cc[:, :, h * HALF : (h + 1) * HALF].rearrange("p r (c i) -> p c r i", i=2),
+        def difference_by_positions(lo, hi, bank):
+            sc = ps.tile([P, L, hi - lo], F32, name=f"sc{bank}", tag=f"bank{bank}")
+            for r in range(L):
+                nc.tensor.matmul_mx(
+                    out=sc[:, r, :],
+                    lhsT=wd_w[:, 2 * P * r : 2 * P * (r + 1)].bitcast(E2M1),
+                    lhsT_scale=wd_s[:, P * r : P * (r + 1)],
+                    rhs=xq[1][:, lo:hi].bitcast(E4M3),
+                    rhs_scale=xs[1][:, lo:hi],
+                    start=True,
+                    stop=True,
+                )
+            sig = sb.tile([P, L, hi - lo], F32, name=f"sig{bank}")
+            nc.scalar.activation(sig[:], sc[:], ACT.Sigmoid)
+            nc.vector.tensor_tensor(dif[1][:, :, lo:hi], sig[:], y_half[1][:, :, lo:hi], ALU.subtract)
+
+        def weigh(engine, h, lo, hi):
+            engine.tensor_tensor(
+                gb[h][:, L * lo : L * hi].rearrange("p (c i r) -> p c r i", i=2, r=L),
+                dif[h][:, :, lo:hi].rearrange("p r (c i) -> p c r i", i=2),
+                cc[:, :, h * HALF + lo : h * HALF + hi].rearrange("p r (c i) -> p c r i", i=2),
                 ALU.mult,
             )
 
@@ -185,17 +201,20 @@ def tile_attend_gml_pl_nce_kernel(
 
         for r in range(L):
             difference(0, r, 1, r)
-        weigh(0)
-        difference(1, 0, 2, 4)
-        difference(1, 2, 2, 5)
+        weigh(nc.vector, 0, 0, HALF)
         quantise_g(0)
+        dif.append(sb.tile([P, L, HALF], F32, name="dif1", tag="dif"))
+        difference_by_positions(0, P, 4)
+        difference_by_positions(P, HALF, 5)
         early = [back(r, 0, bank) for r, bank in zip(ORDER[:EARLY], (7, 3))]
-        weigh(1)
+        weigh(nc.vector, 1, 0, P)
+        weigh(nc.gpsimd, 1, P, HALF)
+        nc.scalar.copy(dx[ORDER[0]][:, :HALF], early[0][:, HALF:])
+        dx_early = sb.tile([P, L, HALF], F32, name="dx_early", tag="dif")
+        nc.scalar.copy(dx_early[:, 0, :], early[1][:, HALF:])
+        nc.vector.tensor_copy(win[ORDER[0]][:].indirect(entries[0]), dx[ORDER[0]][:, :HALF])
         quantise_g(1)
-        for r, acc in zip(ORDER[:EARLY], early):
-            nc.scalar.copy(dx[r][:, :HALF], acc[:, HALF:])
-        for r in ORDER[:EARLY]:
-            nc.vector.tensor_copy(win[r][:].indirect(entries[0]), dx[r][:, :HALF])
+        nc.vector.tensor_copy(win[ORDER[1]][:].indirect(entries[0]), dx_early[:, 0, :])
 
         pairs = sb.tile([P, T * L], BF16, name="pairs", align_bytes=64)
 

@@ -78,7 +78,7 @@ def tile_attend_gml_pl_nce_kernel(
 
         offsets = lists.tile([P, N // 16], U16, name="offsets")
         x_rows = xT.rearrange("(p r) t -> p r t", r=L)
-        x_lane = [sb.tile([P, T], F32, name=f"x_pl{r}") for r in range(L)]
+        x_lane = [sb.tile([P, T], F32, name=f"x_pl{r}", tag=f"x_pl{r}") for r in range(L)]
         cw_sb = sb.tile([P, L], F32, name="cw_sb")
         rw_sb = sb.tile([P, L], F32, name="rw_sb")
         y_rows = y.rearrange("(p r) i -> p r i", r=L)
@@ -92,9 +92,9 @@ def tile_attend_gml_pl_nce_kernel(
         nc.sync.dma_start(out=wd_raw_w[:].bitcast(I32), in_=wd_words[0].bitcast(I32))
         load_scales(nc, wd_raw_s, wd_scales)
         nc.sync.dma_start(out=x_lane[2][:], in_=x_rows[:, 2, :])
-        nc.sync.dma_start(out=x_lane[3][:], in_=x_rows[:, 3, :])
         load_scales(nc, wv_raw_s, wv_scales)
         nc.sync.dma_start(out=wv_raw_w[:].bitcast(I32), in_=wv_words[0].bitcast(I32))
+        nc.sync.dma_start(out=x_lane[3][:], in_=x_rows[:, 3, :])
         nc.sync.dma_start(out=y_half[0][:], in_=y_rows[:, :, :HALF])
         nc.sync.dma_start(out=y_half[1][:], in_=y_rows[:, :, HALF:])
 
@@ -106,10 +106,10 @@ def tile_attend_gml_pl_nce_kernel(
         nc.vector.memset(gq[:, :HALF], 0)
         nc.vector.memset(gs[:, :HALF].bitcast(U32), 0)
 
-        windows = [sb.tile([P, T], F32, name=f"win{r}") for r in range(L - 1)]
-        for window in windows:
-            nc.vector.memset(window[:].bitcast(I32), 0)
-        win = windows + [windows[2]]
+        win = {r: sb.tile([P, T], F32, name=f"win{r}") for r in ORDER[:EARLY]}
+        for r in ORDER[:EARLY]:
+            nc.vector.memset(win[r][:].bitcast(I32), 0)
+        win[3] = win[2]
 
         rw_ps = ps.tile([P, L, P], F32, name="rw_ps", tag="bank7")
         for m in range(L):
@@ -123,56 +123,55 @@ def tile_attend_gml_pl_nce_kernel(
         xb = sb.tile([P, N, L], BF16, name="xb", align_bytes=64)
         xq = [sb.tile([P, HALF], U32, name=f"xq{h}", align_bytes=64) for h in range(2)]
         xs = [sb.tile([P, HALF], U8, name=f"xs{h}", align_bytes=64) for h in range(2)]
-        nc.vector.tensor_copy(xb[:, :, 0], x_lane[0][:].indirect(offsets[:]))
-        nc.vector.tensor_copy(xb[:, :, 1], x_lane[1][:].indirect(offsets[:]))
+        entries = [offsets[:, h * HALF_COLS : (h + 1) * HALF_COLS] for h in range(2)]
+        quarters = xb[:].rearrange("p (a n) r -> p a n r", n=P)
+        places = [quarters[:, 1:3], quarters[:, 0:4:3]]
+
+        def gather(r, h):
+            nc.vector.tensor_copy(places[h][:, :, :, r], x_lane[r][:].indirect(entries[h]))
+
+        for r in range(2):
+            gather(r, 0)
+            gather(r, 1)
+        win[1] = sb.tile([P, T], F32, name="win1", tag="x_pl0")
+        nc.gpsimd.memset(win[1][:].bitcast(I32), 0)
         wd_w = deal_words(nc, sb, "wd", wd_raw_w)
         wd_s = deal_scales(nc, sb, "wd", wd_raw_s)
-        nc.vector.tensor_copy(xb[:, :, 2], x_lane[2][:].indirect(offsets[:]))
-        entries = [offsets[:, h * HALF_COLS : (h + 1) * HALF_COLS] for h in range(2)]
-        for h in range(2):
-            cols = slice(h * HALF, (h + 1) * HALF)
-            nc.vector.tensor_copy(xb[:, cols, 3], x_lane[3][:].indirect(entries[h]))
-            nc.vector.quantize_mx(out=xq[h][:].bitcast(E4M3), scales=xs[h][:], in_=xb[:, cols, :].rearrange("p n r -> p (n r)"))
+        gather(2, 0)
+        gather(2, 1)
         wv_w = deal_words(nc, sb, "wv", wv_raw_w)
         wv_s = deal_scales(nc, sb, "wv", wv_raw_s)
+        gather(3, 0)
+        for a in range(2):
+            cols = slice(a * P, (a + 1) * P)
+            nc.vector.quantize_mx(out=xq[0][:, cols].bitcast(E4M3), scales=xs[0][:, cols], in_=quarters[:, 1 + a].rearrange("p n r -> p (n r)"))
+        gather(3, 1)
+        for a in range(2):
+            cols = slice(a * P, (a + 1) * P)
+            nc.vector.quantize_mx(out=xq[1][:, cols].bitcast(E4M3), scales=xs[1][:, cols], in_=quarters[:, 3 * a].rearrange("p n r -> p (n r)"))
 
         dx = [sb.tile([P, N], F32, name=f"dx{r}") for r in range(L)]
         gb = [sb.tile([P, HALF * L], BF16, name=f"gb{h}", align_bytes=64) for h in range(2)]
         dif = [sb.tile([P, L, HALF], F32, name="dif0", tag="dif")]
 
-        def difference(h, first, count, bank):
+        def difference(h, lo, first, count, bank):
             lanes = slice(first, first + count)
-            sc = ps.tile([P, count, HALF], F32, name=f"sc{bank}", tag=f"bank{bank}")
+            cols = slice(lo, lo + P)
+            sc = ps.tile([P, count, P], F32, name=f"sc{bank}", tag=f"bank{bank}")
             for e in range(count):
                 r = first + e
                 nc.tensor.matmul_mx(
                     out=sc[:, e, :],
                     lhsT=wd_w[:, 2 * P * r : 2 * P * (r + 1)].bitcast(E2M1),
                     lhsT_scale=wd_s[:, P * r : P * (r + 1)],
-                    rhs=xq[h][:].bitcast(E4M3),
-                    rhs_scale=xs[h][:],
+                    rhs=xq[h][:, cols].bitcast(E4M3),
+                    rhs_scale=xs[h][:, cols],
                     start=True,
                     stop=True,
                 )
-            sig = sb.tile([P, count, HALF], F32, name=f"sig{bank}")
+            sig = sb.tile([P, count, P], F32, name=f"sig{bank}")
             nc.scalar.activation(sig[:], sc[:], ACT.Sigmoid)
-            nc.vector.tensor_tensor(dif[h][:, lanes, :], sig[:], y_half[h][:, lanes, :], ALU.subtract)
-
-        def difference_by_positions(lo, hi, bank):
-            sc = ps.tile([P, L, hi - lo], F32, name=f"sc{bank}", tag=f"bank{bank}")
-            for r in range(L):
-                nc.tensor.matmul_mx(
-                    out=sc[:, r, :],
-                    lhsT=wd_w[:, 2 * P * r : 2 * P * (r + 1)].bitcast(E2M1),
-                    lhsT_scale=wd_s[:, P * r : P * (r + 1)],
-                    rhs=xq[1][:, lo:hi].bitcast(E4M3),
-                    rhs_scale=xs[1][:, lo:hi],
-                    start=True,
-                    stop=True,
-                )
-            sig = sb.tile([P, L, hi - lo], F32, name=f"sig{bank}")
-            nc.scalar.activation(sig[:], sc[:], ACT.Sigmoid)
-            nc.vector.tensor_tensor(dif[1][:, :, lo:hi], sig[:], y_half[1][:, :, lo:hi], ALU.subtract)
+            nc.vector.tensor_tensor(dif[h][:, lanes, cols], sig[:], y_half[h][:, lanes, cols], ALU.subtract)
 
         def weigh(engine, h, lo, hi):
             engine.tensor_tensor(
@@ -182,9 +181,9 @@ def tile_attend_gml_pl_nce_kernel(
                 ALU.mult,
             )
 
-        def quantise_g(h):
-            cols = slice((h + 1) * HALF, (h + 2) * HALF)
-            nc.vector.quantize_mx(out=gq[:, cols].bitcast(E5M2), scales=gs[:, cols], in_=gb[h][:])
+        def quantise_g(h, lo, hi):
+            cols = slice((h + 1) * HALF + lo, (h + 1) * HALF + hi)
+            nc.vector.quantize_mx(out=gq[:, cols].bitcast(E5M2), scales=gs[:, cols], in_=gb[h][:, L * lo : L * hi])
 
         def back(r, first, bank):
             acc = ps.tile([P, N], F32, name=f"dx_ps{r}", tag=f"bank{bank}")
@@ -199,13 +198,14 @@ def tile_attend_gml_pl_nce_kernel(
             )
             return acc
 
-        for r in range(L):
-            difference(0, r, 1, r)
-        weigh(nc.vector, 0, 0, HALF)
-        quantise_g(0)
+        for a in range(2):
+            difference(0, a * P, 0, 2, 2 * a)
+            difference(0, a * P, 2, 2, 2 * a + 1)
+            weigh(nc.vector, 0, a * P, (a + 1) * P)
+            quantise_g(0, a * P, (a + 1) * P)
         dif.append(sb.tile([P, L, HALF], F32, name="dif1", tag="dif"))
-        difference_by_positions(0, P, 4)
-        difference_by_positions(P, HALF, 5)
+        difference(1, 0, 0, L, 4)
+        difference(1, P, 0, L, 5)
         early = [back(r, 0, bank) for r, bank in zip(ORDER[:EARLY], (7, 3))]
         weigh(nc.vector, 1, 0, P)
         weigh(nc.gpsimd, 1, P, HALF)
@@ -213,7 +213,7 @@ def tile_attend_gml_pl_nce_kernel(
         dx_early = sb.tile([P, L, HALF], F32, name="dx_early", tag="dif")
         nc.scalar.copy(dx_early[:, 0, :], early[1][:, HALF:])
         nc.vector.tensor_copy(win[ORDER[0]][:].indirect(entries[0]), dx[ORDER[0]][:, :HALF])
-        quantise_g(1)
+        quantise_g(1, 0, HALF)
         nc.vector.tensor_copy(win[ORDER[1]][:].indirect(entries[0]), dx_early[:, 0, :])
 
         pairs = sb.tile([P, T * L], BF16, name="pairs", align_bytes=64)

@@ -28,13 +28,14 @@ ORDER = [2, 0, 1, 3]
 EARLY = 2
 
 VECTOR_COLS = 1024
-VECTOR_PIECES = [(0, 512), (512, VECTOR_COLS)]
+PLACED = 896
 SCALAR_ROUNDS = [(VECTOR_COLS, 1536), (1536, T)]
 SCALAR_WEAVES = [(VECTOR_COLS, 1280), (1280, 1536), (1536, 1792), (1792, 1920), (1920, T)]
-CODE_STORES = [(0, 512), (512, 1024), (1024, 1536), (1536, 1920), (1920, T)]
+CODE_STORES = [(0, 512), (512, 1024), (1024, 1536), (1536, T)]
 BLK = 128
 PLANE = T // 4
 QUANT = PLANE // 2
+QUANTS = [(c, c + QUANT) for c in range(0, T - QUANT, QUANT)] + [(1792, 1920), (1920, T)]
 
 
 def load_scales(nc, raw_s, scales):
@@ -69,6 +70,8 @@ def tile_attend_gml_pl_nce_kernel(
         sb = ctx.enter_context(tc.tile_pool(name="sb", bufs=1))
         ps = ctx.enter_context(tc.psum_pool(name="ps", bufs=1))
 
+        rows = sb.tile([P, 512], F32, name="rows")
+        nc.gpsimd.memset(rows[:], 0.0)
         wd_raw_s = sb.tile([P, 512], U8, name="wd_raw_s", align_bytes=64)
         wv_raw_s = sb.tile([P, 512], U8, name="wv_raw_s", align_bytes=64)
         nc.gpsimd.memset(wd_raw_s[:].bitcast(I32), 0)
@@ -79,14 +82,12 @@ def tile_attend_gml_pl_nce_kernel(
         offsets = lists.tile([P, N // 16], U16, name="offsets")
         x_rows = xT.rearrange("(p r) t -> p r t", r=L)
         x_lane = [sb.tile([P, T], F32, name=f"x_pl{r}", tag=f"x_pl{r}") for r in range(L)]
-        cw_sb = sb.tile([P, L], F32, name="cw_sb")
-        rw_sb = sb.tile([P, L], F32, name="rw_sb")
         y_rows = y.rearrange("(p r) i -> p r i", r=L)
         y_half = [sb.tile([P, L, HALF], F32, name=f"y_h{h}") for h in range(2)]
 
         nc.sync.dma_start(out=x_lane[0][:], in_=x_rows[:, 0, :])
-        nc.scalar.dma_start(out=rw_sb[:], in_=rw[0].rearrange("(c m) -> c m", m=L))
-        nc.scalar.dma_start(out=cw_sb[:], in_=cw.rearrange("(p r) o -> p (r o)", r=L))
+        nc.sync.dma_start(out=rows[0:1, :], in_=cw.rearrange("v o -> o v"))
+        nc.sync.dma_start(out=rows[1:2, :], in_=rw[0:1, :])
         nc.sync.dma_start(offsets[:], offs)
         nc.sync.dma_start(out=x_lane[1][:], in_=x_rows[:, 1, :])
         nc.sync.dma_start(out=wd_raw_w[:].bitcast(I32), in_=wd_words[0].bitcast(I32))
@@ -111,6 +112,12 @@ def tile_attend_gml_pl_nce_kernel(
             nc.vector.memset(win[r][:].bitcast(I32), 0)
         win[3] = win[2]
 
+        rows_ps = ps.tile([P, L, P], F32, name="rows_ps", tag="bank6")
+        for m in range(L):
+            nc.tensor.transpose(rows_ps[:, m, :], rows[:, m::L], ident[:])
+        weights = sb.tile([P, 2, L], F32, name="weights")
+        nc.scalar.copy(weights[:], rows_ps[:, :, 0:2].rearrange("p m k -> p k m"))
+        cw_sb, rw_sb = weights[:, 0, :], weights[:, 1, :]
         rw_ps = ps.tile([P, L, P], F32, name="rw_ps", tag="bank7")
         for m in range(L):
             nc.tensor.transpose(rw_ps[:, m, :], rw_sb[:, m : m + 1].to_broadcast([P, P]), ident[:])
@@ -125,7 +132,7 @@ def tile_attend_gml_pl_nce_kernel(
         xs = [sb.tile([P, HALF], U8, name=f"xs{h}", align_bytes=64) for h in range(2)]
         entries = [offsets[:, h * HALF_COLS : (h + 1) * HALF_COLS] for h in range(2)]
         quarters = xb[:].rearrange("p (a n) r -> p a n r", n=P)
-        places = [quarters[:, 1:3], quarters[:, 0:4:3]]
+        places = [quarters[:, 1:4:2], quarters[:, 0:3:2]]
 
         def gather(r, h):
             nc.vector.tensor_copy(places[h][:, :, :, r], x_lane[r][:].indirect(entries[h]))
@@ -144,11 +151,11 @@ def tile_attend_gml_pl_nce_kernel(
         gather(3, 0)
         for a in range(2):
             cols = slice(a * P, (a + 1) * P)
-            nc.vector.quantize_mx(out=xq[0][:, cols].bitcast(E4M3), scales=xs[0][:, cols], in_=quarters[:, 1 + a].rearrange("p n r -> p (n r)"))
+            nc.vector.quantize_mx(out=xq[0][:, cols].bitcast(E4M3), scales=xs[0][:, cols], in_=quarters[:, 1 + 2 * a].rearrange("p n r -> p (n r)"))
         gather(3, 1)
         for a in range(2):
             cols = slice(a * P, (a + 1) * P)
-            nc.vector.quantize_mx(out=xq[1][:, cols].bitcast(E4M3), scales=xs[1][:, cols], in_=quarters[:, 3 * a].rearrange("p n r -> p (n r)"))
+            nc.vector.quantize_mx(out=xq[1][:, cols].bitcast(E4M3), scales=xs[1][:, cols], in_=quarters[:, 2 * a].rearrange("p n r -> p (n r)"))
 
         dx = [sb.tile([P, N], F32, name=f"dx{r}") for r in range(L)]
         gb = [sb.tile([P, HALF * L], BF16, name=f"gb{h}", align_bytes=64) for h in range(2)]
@@ -218,6 +225,11 @@ def tile_attend_gml_pl_nce_kernel(
 
         pairs = sb.tile([P, T * L], BF16, name="pairs", align_bytes=64)
 
+        ob = sb.tile([P, T * L], BF16, name="ob", align_bytes=64)
+
+        def place_lane(copy, r, lo, hi):
+            copy(ob[:, L * lo : L * hi].rearrange("p (n r) -> p n r", r=L)[:, :, r], win[r][:, lo:hi])
+
         def gpsimd_copy(out, in_):
             nc.gpsimd.tensor_scalar(out, in_, 1.0, 0.0, ALU.mult, ALU.add)
 
@@ -239,13 +251,13 @@ def tile_attend_gml_pl_nce_kernel(
                 nc.vector.tensor_copy(win[r][:].indirect(offsets[:]), dx[r][:])
             nc.sync.dma_start(out=o_rows[:, r, :], in_=win[r][:])
             if r != ORDER[-1]:
-                round_lane(nc.scalar.copy, r, 0, VECTOR_COLS)
-                round_lane(gpsimd_copy, r, VECTOR_COLS, T)
+                placer, rounder = (gpsimd_copy, nc.scalar.copy) if k == 0 else (nc.scalar.copy, gpsimd_copy)
+                place_lane(placer, r, 0, PLACED)
+                round_lane(rounder, r, PLACED, T)
 
         o_scales = sb.tile([P, PLANE], U8, name="os_", align_bytes=64)
         o_codes = sb.tile([P, T], U32, name="oq", align_bytes=64)
         o_words = out_1[0].rearrange("p n t -> p (n t)")
-        ob = sb.tile([P, T * L], BF16, name="ob", align_bytes=64)
 
         def weave(copy, word, lo, hi):
             copy(
@@ -253,17 +265,16 @@ def tile_attend_gml_pl_nce_kernel(
                 pairs[:, L * lo : L * hi].bitcast(word).rearrange("p (b u n) -> p b n u", u=2, n=BLK),
             )
 
-        for lo, hi in VECTOR_PIECES:
-            round_lane(nc.vector.tensor_copy, ORDER[-1], lo, hi)
-        for lo, hi in VECTOR_PIECES:
-            weave(nc.vector.tensor_copy, I32, lo, hi)
+        place_lane(nc.vector.tensor_copy, ORDER[-1], 0, 512)
+        place_lane(nc.vector.tensor_copy, ORDER[-1], 512, PLACED)
+        round_lane(nc.vector.tensor_copy, ORDER[-1], PLACED, VECTOR_COLS)
+        weave(nc.vector.tensor_copy, I32, PLACED, VECTOR_COLS)
         for lo, hi in SCALAR_ROUNDS:
             round_lane(nc.scalar.copy, ORDER[-1], lo, hi)
         for lo, hi in SCALAR_WEAVES:
             weave(nc.scalar.copy, U32, lo, hi)
         for lo, hi in CODE_STORES:
-            for first in range(lo, hi, QUANT):
-                last = min(first + QUANT, hi)
+            for first, last in [c for c in QUANTS if lo <= c[0] < hi]:
                 j, col = divmod(first, PLANE)
                 nc.vector.quantize_mx(
                     out=o_codes[:, first:last].bitcast(E4M3),

@@ -52,8 +52,8 @@ def deal_words(nc, pool, name, raw_w):
     return w
 
 
-def deal_scales(nc, pool, name, raw_s):
-    s = pool.tile([P, 512], U8, name=name + "_s", align_bytes=64)
+def deal_scales(nc, pool, name, raw_s, tag):
+    s = pool.tile([P, 512], U8, name=name + "_s", tag=tag, align_bytes=64)
     nc.vector.tensor_copy(
         out=s[:].rearrange("p (r s) -> p r s", r=L),
         in_=raw_s[:].rearrange("p (s r) -> p r s", r=L),
@@ -90,13 +90,13 @@ def tile_attend_gml_pl_nce_kernel(
         nc.sync.dma_start(out=rows[1:2, :], in_=rw[0:1, :])
         nc.sync.dma_start(offsets[:], offs)
         nc.sync.dma_start(out=x_lane[1][:], in_=x_rows[:, 1, :])
-        nc.sync.dma_start(out=wd_raw_w[:].bitcast(I32), in_=wd_words[0].bitcast(I32))
         load_scales(nc, wd_raw_s, wd_scales)
         nc.sync.dma_start(out=x_lane[2][:], in_=x_rows[:, 2, :])
-        load_scales(nc, wv_raw_s, wv_scales)
-        nc.sync.dma_start(out=wv_raw_w[:].bitcast(I32), in_=wv_words[0].bitcast(I32))
         nc.sync.dma_start(out=x_lane[3][:], in_=x_rows[:, 3, :])
+        nc.sync.dma_start(out=wd_raw_w[:].bitcast(I32), in_=wd_words[0].bitcast(I32))
+        nc.sync.dma_start(out=wv_raw_w[:].bitcast(I32), in_=wv_words[0].bitcast(I32))
         nc.sync.dma_start(out=y_half[0][:], in_=y_rows[:, :, :HALF])
+        load_scales(nc, wv_raw_s, wv_scales)
         nc.sync.dma_start(out=y_half[1][:], in_=y_rows[:, :, HALF:])
 
         ident = sb.tile([P, P], F32, name="ident")
@@ -142,17 +142,16 @@ def tile_attend_gml_pl_nce_kernel(
             gather(r, 1)
         win[1] = sb.tile([P, T], F32, name="win1", tag="x_pl0")
         nc.gpsimd.memset(win[1][:].bitcast(I32), 0)
-        wd_w = deal_words(nc, sb, "wd", wd_raw_w)
-        wd_s = deal_scales(nc, sb, "wd", wd_raw_s)
+        wd_s = deal_scales(nc, sb, "wd", wd_raw_s, "wd_s")
         gather(2, 0)
         gather(2, 1)
-        wv_w = deal_words(nc, sb, "wv", wv_raw_w)
-        wv_s = deal_scales(nc, sb, "wv", wv_raw_s)
         gather(3, 0)
+        wd_w = deal_words(nc, sb, "wd", wd_raw_w)
         for a in range(2):
             cols = slice(a * P, (a + 1) * P)
             nc.vector.quantize_mx(out=xq[0][:, cols].bitcast(E4M3), scales=xs[0][:, cols], in_=quarters[:, 1 + 2 * a].rearrange("p n r -> p (n r)"))
         gather(3, 1)
+        wv_w = deal_words(nc, sb, "wv", wv_raw_w)
         for a in range(2):
             cols = slice(a * P, (a + 1) * P)
             nc.vector.quantize_mx(out=xq[1][:, cols].bitcast(E4M3), scales=xs[1][:, cols], in_=quarters[:, 2 * a].rearrange("p n r -> p (n r)"))
@@ -176,7 +175,7 @@ def tile_attend_gml_pl_nce_kernel(
                     start=True,
                     stop=True,
                 )
-            sig = sb.tile([P, count, P], F32, name=f"sig{bank}")
+            sig = sb.tile([P, count, P], F32, name=f"sig{bank}", tag=f"sig{bank}", align_bytes=64)
             nc.scalar.activation(sig[:], sc[:], ACT.Sigmoid)
             nc.vector.tensor_tensor(dif[h][:, lanes, cols], sig[:], y_half[h][:, lanes, cols], ALU.subtract)
 
@@ -210,6 +209,7 @@ def tile_attend_gml_pl_nce_kernel(
             difference(0, a * P, 2, 2, 2 * a + 1)
             weigh(nc.vector, 0, a * P, (a + 1) * P)
             quantise_g(0, a * P, (a + 1) * P)
+        wv_s = deal_scales(nc, sb, "wv", wv_raw_s, "sig3")
         dif.append(sb.tile([P, L, HALF], F32, name="dif1", tag="dif"))
         difference(1, 0, 0, L, 4)
         difference(1, P, 0, L, 5)

@@ -31,7 +31,7 @@ VECTOR_COLS = 1024
 PLACED = 896
 SCALAR_ROUNDS = [(VECTOR_COLS, 1536), (1536, T)]
 SCALAR_WEAVES = [(VECTOR_COLS, 1280), (1280, 1536), (1536, 1792), (1792, 1920), (1920, T)]
-CODE_STORES = [(0, 512), (512, 1024), (1024, 1536), (1536, T)]
+CODE_STORES = [(0, 512), (512, 1024), (1024, 1536), (1536, 1920), (1920, T)]
 BLK = 128
 PLANE = T // 4
 QUANT = PLANE // 2

@@ -27,15 +27,15 @@ HALF_COLS = HALF // 16
 ORDER = [2, 0, 1, 3]
 EARLY = 2
 
-VECTOR_COLS = 1024
 PLACED = 896
-SCALAR_ROUNDS = [(VECTOR_COLS, 1536), (1536, T)]
-SCALAR_WEAVES = [(VECTOR_COLS, 1280), (1280, 1536), (1536, 1792), (1792, 1920), (1920, T)]
+VECTOR_BLOCK = (1536, 1664)
+SCALAR_ROUNDS = [(PLACED, 1536), (1664, T)]
+SCALAR_WEAVES = [(PLACED, 1280), (1280, 1536), (1664, 1792), (1792, 1920), (1920, T)]
 CODE_STORES = [(0, 512), (512, 1024), (1024, 1536), (1536, 1920), (1920, T)]
 BLK = 128
 PLANE = T // 4
 QUANT = PLANE // 2
-QUANTS = [(c, c + QUANT) for c in range(0, T - QUANT, QUANT)] + [(1792, 1920), (1920, T)]
+QUANTS = [(c, c + QUANT) for c in range(0, 1536, QUANT)] + [(1664, 1792), (1792, 1920), (1536, 1664), (1920, T)]
 
 
 def load_scales(nc, raw_s, scales):
@@ -267,13 +267,14 @@ def tile_attend_gml_pl_nce_kernel(
 
         place_lane(nc.vector.tensor_copy, ORDER[-1], 0, 512)
         place_lane(nc.vector.tensor_copy, ORDER[-1], 512, PLACED)
-        round_lane(nc.vector.tensor_copy, ORDER[-1], PLACED, VECTOR_COLS)
-        weave(nc.vector.tensor_copy, I32, PLACED, VECTOR_COLS)
         for lo, hi in SCALAR_ROUNDS:
             round_lane(nc.scalar.copy, ORDER[-1], lo, hi)
-        for lo, hi in SCALAR_WEAVES:
-            weave(nc.scalar.copy, U32, lo, hi)
+            for first, last in [c for c in SCALAR_WEAVES if lo <= c[0] < hi]:
+                weave(nc.scalar.copy, U32, first, last)
         for lo, hi in CODE_STORES:
+            if lo == VECTOR_BLOCK[0]:
+                round_lane(nc.vector.tensor_copy, ORDER[-1], *VECTOR_BLOCK)
+                weave(nc.vector.tensor_copy, I32, *VECTOR_BLOCK)
             for first, last in [c for c in QUANTS if lo <= c[0] < hi]:
                 j, col = divmod(first, PLANE)
                 nc.vector.quantize_mx(

@@ -29,13 +29,13 @@ EARLY = 2
 
 PLACED = 896
 VECTOR_BLOCK = (1536, 1664)
-SCALAR_ROUNDS = [(PLACED, 1536), (1664, T)]
+SCALAR_ROUNDS = [(PLACED, 1280), (1280, 1536), (1664, T)]
 SCALAR_WEAVES = [(PLACED, 1280), (1280, 1536), (1664, 1792), (1792, 1920), (1920, T)]
 CODE_STORES = [(0, 512), (512, 1024), (1024, 1536), (1536, 1920), (1920, T)]
 BLK = 128
 PLANE = T // 4
 QUANT = PLANE // 2
-QUANTS = [(c, c + QUANT) for c in range(0, 1536, QUANT)] + [(1664, 1792), (1792, 1920), (1536, 1664), (1920, T)]
+QUANTS = [(c, c + QUANT) for c in range(0, 1536, QUANT)] + [(1664, 1792), (1536, 1664), (1792, 1920), (1920, T)]
 
 
 def load_scales(nc, raw_s, scales):
@@ -265,17 +265,25 @@ def tile_attend_gml_pl_nce_kernel(
                 pairs[:, L * lo : L * hi].bitcast(word).rearrange("p (b u n) -> p b n u", u=2, n=BLK),
             )
 
-        place_lane(nc.vector.tensor_copy, ORDER[-1], 0, 512)
-        place_lane(nc.vector.tensor_copy, ORDER[-1], 512, PLACED)
-        for lo, hi in SCALAR_ROUNDS:
-            round_lane(nc.scalar.copy, ORDER[-1], lo, hi)
-            for first, last in [c for c in SCALAR_WEAVES if lo <= c[0] < hi]:
-                weave(nc.scalar.copy, U32, first, last)
+        last_lane = ORDER[-1]
+        round_lane(nc.scalar.copy, last_lane, *SCALAR_ROUNDS[0])
+        round_lane(nc.scalar.copy, last_lane, *SCALAR_ROUNDS[1])
+        weave(nc.scalar.copy, U32, *SCALAR_WEAVES[0])
+        round_lane(nc.scalar.copy, last_lane, *SCALAR_ROUNDS[2])
+        for lo, hi in SCALAR_WEAVES[1:]:
+            weave(nc.scalar.copy, U32, lo, hi)
+
+        ahead = {
+            0: [(place_lane, last_lane, 0, 256), (place_lane, last_lane, 256, 512)],
+            256: [(place_lane, last_lane, 512, 768)],
+            512: [(place_lane, last_lane, 768, PLACED)],
+            1280: [(round_lane, last_lane, *VECTOR_BLOCK)],
+            1664: [(weave, I32, *VECTOR_BLOCK)],
+        }
         for lo, hi in CODE_STORES:
-            if lo == VECTOR_BLOCK[0]:
-                round_lane(nc.vector.tensor_copy, ORDER[-1], *VECTOR_BLOCK)
-                weave(nc.vector.tensor_copy, I32, *VECTOR_BLOCK)
             for first, last in [c for c in QUANTS if lo <= c[0] < hi]:
+                for step, *args in ahead.get(first, []):
+                    step(nc.vector.tensor_copy, *args)
                 j, col = divmod(first, PLANE)
                 nc.vector.quantize_mx(
                     out=o_codes[:, first:last].bitcast(E4M3),

@@ -28,14 +28,12 @@ ORDER = [2, 0, 1, 3]
 EARLY = 2
 
 PLACED = 896
-VECTOR_BLOCK = (1536, 1664)
-SCALAR_ROUNDS = [(PLACED, 1280), (1280, 1536), (1664, T)]
-SCALAR_WEAVES = [(PLACED, 1280), (1280, 1536), (1664, 1792), (1792, 1920), (1920, T)]
-CODE_STORES = [(0, 512), (512, 1024), (1024, 1536), (1536, 1920), (1920, T)]
+VECTOR_BLOCK = (1792, 1920)
+CODE_STORES = [(0, 512), (512, 1024), (1024, 1536), (1536, 1792), (1792, T)]
 BLK = 128
 PLANE = T // 4
 QUANT = PLANE // 2
-QUANTS = [(c, c + QUANT) for c in range(0, 1536, QUANT)] + [(1664, 1792), (1536, 1664), (1792, 1920), (1920, T)]
+QUANTS = [(c, c + QUANT) for c in range(0, 1536, QUANT)] + [(c, c + BLK) for c in range(1536, T, BLK)]
 
 
 def load_scales(nc, raw_s, scales):
@@ -266,18 +264,21 @@ def tile_attend_gml_pl_nce_kernel(
             )
 
         last_lane = ORDER[-1]
-        round_lane(nc.scalar.copy, last_lane, *SCALAR_ROUNDS[0])
-        round_lane(nc.scalar.copy, last_lane, *SCALAR_ROUNDS[1])
-        weave(nc.scalar.copy, U32, *SCALAR_WEAVES[0])
-        round_lane(nc.scalar.copy, last_lane, *SCALAR_ROUNDS[2])
-        for lo, hi in SCALAR_WEAVES[1:]:
-            weave(nc.scalar.copy, U32, lo, hi)
+        round_lane(nc.scalar.copy, last_lane, PLACED, 1280)
+        round_lane(nc.scalar.copy, last_lane, 1280, 1536)
+        weave(nc.scalar.copy, U32, PLACED, 1280)
+        round_lane(nc.scalar.copy, last_lane, 1536, 1792)
+        weave(nc.scalar.copy, U32, 1280, 1536)
+        weave(nc.scalar.copy, U32, 1536, 1664)
+        round_lane(nc.scalar.copy, last_lane, 1920, T)
+        weave(nc.scalar.copy, U32, 1664, 1792)
+        weave(nc.scalar.copy, U32, 1920, T)
 
         ahead = {
             0: [(place_lane, last_lane, 0, 256), (place_lane, last_lane, 256, 512)],
             256: [(place_lane, last_lane, 512, 768)],
             512: [(place_lane, last_lane, 768, PLACED)],
-            1280: [(round_lane, last_lane, *VECTOR_BLOCK)],
+            1536: [(round_lane, last_lane, *VECTOR_BLOCK)],
             1664: [(weave, I32, *VECTOR_BLOCK)],
         }
         for lo, hi in CODE_STORES:

@@ -23,17 +23,13 @@ L = 4
 QUADRANTS = 4
 HALF = N // 2
 HALF_COLS = HALF // 16
-
-ORDER = [2, 0, 1, 3]
-EARLY = 2
-
-PLACED = 896
-VECTOR_BLOCK = (1792, 1920)
-CODE_STORES = [(0, 512), (512, 1024), (1024, 1536), (1536, 1792), (1792, T)]
 BLK = 128
 PLANE = T // 4
-QUANT = PLANE // 2
-QUANTS = [(c, c + QUANT) for c in range(0, 1536, QUANT)] + [(c, c + BLK) for c in range(1536, T, BLK)]
+GPSIMD_COLS = 1536
+VECTOR_COLS = 1152
+VECTOR_PIECES = [(0, 256), (256, 512), (512, 768), (768, 1024), (1024, VECTOR_COLS)]
+SCALAR_PIECES = [(VECTOR_COLS, 1536), (1536, 1792), (1792, 1920), (1920, T)]
+CODE_STORES = [(0, 512), (512, 1024), (1024, 1536), (1536, 1792), (1792, T)]
 
 
 def load_scales(nc, raw_s, scales):
@@ -43,15 +39,15 @@ def load_scales(nc, raw_s, scales):
 
 def deal_words(nc, pool, name, raw_w):
     w = pool.tile([P, 2 * 512], U8, name=name + "_w", align_bytes=64)
-    nc.vector.tensor_copy(
-        out=w[:].bitcast(U16).rearrange("p (r s) -> p r s", r=L),
-        in_=raw_w[:].bitcast(U16).rearrange("p (s r) -> p r s", r=L),
+    nc.scalar.copy(
+        w[:].bitcast(U16).rearrange("p (r s) -> p r s", r=L),
+        raw_w[:].bitcast(U16).rearrange("p (s r) -> p r s", r=L),
     )
     return w
 
 
-def deal_scales(nc, pool, name, raw_s, tag):
-    s = pool.tile([P, 512], U8, name=name + "_s", tag=tag, align_bytes=64)
+def deal_scales(nc, pool, name, raw_s):
+    s = pool.tile([P, 512], U8, name=name + "_s", align_bytes=64)
     nc.vector.tensor_copy(
         out=s[:].rearrange("p (r s) -> p r s", r=L),
         in_=raw_s[:].rearrange("p (s r) -> p r s", r=L),
@@ -92,23 +88,17 @@ def tile_attend_gml_pl_nce_kernel(
         nc.sync.dma_start(out=x_lane[2][:], in_=x_rows[:, 2, :])
         nc.sync.dma_start(out=x_lane[3][:], in_=x_rows[:, 3, :])
         nc.sync.dma_start(out=wd_raw_w[:].bitcast(I32), in_=wd_words[0].bitcast(I32))
-        nc.sync.dma_start(out=wv_raw_w[:].bitcast(I32), in_=wv_words[0].bitcast(I32))
-        nc.sync.dma_start(out=y_half[0][:], in_=y_rows[:, :, :HALF])
         load_scales(nc, wv_raw_s, wv_scales)
+        nc.sync.dma_start(out=y_half[0][:], in_=y_rows[:, :, :HALF])
+        nc.sync.dma_start(out=wv_raw_w[:].bitcast(I32), in_=wv_words[0].bitcast(I32))
         nc.sync.dma_start(out=y_half[1][:], in_=y_rows[:, :, HALF:])
 
         ident = sb.tile([P, P], F32, name="ident")
         make_identity(nc, ident[:])
 
-        gq = sb.tile([P, HALF + N], U32, name="gq", align_bytes=64)
-        gs = sb.tile([P, HALF + N], U8, name="gs", align_bytes=64)
-        nc.vector.memset(gq[:, :HALF], 0)
-        nc.vector.memset(gs[:, :HALF].bitcast(U32), 0)
-
-        win = {r: sb.tile([P, T], F32, name=f"win{r}") for r in ORDER[:EARLY]}
-        for r in ORDER[:EARLY]:
+        win = {r: sb.tile([P, T], F32, name=f"win{r}") for r in range(2)}
+        for r in range(2):
             nc.vector.memset(win[r][:].bitcast(I32), 0)
-        win[3] = win[2]
 
         rows_ps = ps.tile([P, L, P], F32, name="rows_ps", tag="bank6")
         for m in range(L):
@@ -126,41 +116,52 @@ def tile_attend_gml_pl_nce_kernel(
             )
 
         xb = sb.tile([P, N, L], BF16, name="xb", align_bytes=64)
-        xq = [sb.tile([P, HALF], U32, name=f"xq{h}", align_bytes=64) for h in range(2)]
-        xs = [sb.tile([P, HALF], U8, name=f"xs{h}", align_bytes=64) for h in range(2)]
+        xq = sb.tile([P, N], U32, name="xq", align_bytes=64)
+        xs = sb.tile([P, N], U8, name="xs", align_bytes=64)
         entries = [offsets[:, h * HALF_COLS : (h + 1) * HALF_COLS] for h in range(2)]
-        quarters = xb[:].rearrange("p (a n) r -> p a n r", n=P)
-        places = [quarters[:, 1:4:2], quarters[:, 0:3:2]]
+        slots = xb[:].rearrange("p (a n) r -> p a n r", n=P)
+        places = [slots[:, 1:4:2], slots[:, 0:3:2]]
+
+        def quarter(q):
+            return slice(q * P, (q + 1) * P)
 
         def gather(r, h):
             nc.vector.tensor_copy(places[h][:, :, :, r], x_lane[r][:].indirect(entries[h]))
 
+        def quantise_x(q):
+            h, a = divmod(q, 2)
+            nc.vector.quantize_mx(
+                out=xq[:, quarter(q)].bitcast(E4M3), scales=xs[:, quarter(q)], in_=places[h][:, a].rearrange("p n r -> p (n r)")
+            )
+
         for r in range(2):
             gather(r, 0)
             gather(r, 1)
-        win[1] = sb.tile([P, T], F32, name="win1", tag="x_pl0")
-        nc.gpsimd.memset(win[1][:].bitcast(I32), 0)
-        wd_s = deal_scales(nc, sb, "wd", wd_raw_s, "wd_s")
+        win[3] = sb.tile([P, T], F32, name="win3", tag="x_pl0")
+        nc.gpsimd.memset(win[3][:].bitcast(I32), 0)
+        wd_s = deal_scales(nc, sb, "wd", wd_raw_s)
         gather(2, 0)
         gather(2, 1)
         gather(3, 0)
         wd_w = deal_words(nc, sb, "wd", wd_raw_w)
-        for a in range(2):
-            cols = slice(a * P, (a + 1) * P)
-            nc.vector.quantize_mx(out=xq[0][:, cols].bitcast(E4M3), scales=xs[0][:, cols], in_=quarters[:, 1 + 2 * a].rearrange("p n r -> p (n r)"))
+        quantise_x(0)
+        quantise_x(1)
         gather(3, 1)
+        wv_s = deal_scales(nc, sb, "wv", wv_raw_s)
+        quantise_x(2)
+        quantise_x(3)
         wv_w = deal_words(nc, sb, "wv", wv_raw_w)
-        for a in range(2):
-            cols = slice(a * P, (a + 1) * P)
-            nc.vector.quantize_mx(out=xq[1][:, cols].bitcast(E4M3), scales=xs[1][:, cols], in_=quarters[:, 2 * a].rearrange("p n r -> p (n r)"))
 
-        dx = [sb.tile([P, N], F32, name=f"dx{r}") for r in range(L)]
-        gb = [sb.tile([P, HALF * L], BF16, name=f"gb{h}", align_bytes=64) for h in range(2)]
-        dif = [sb.tile([P, L, HALF], F32, name="dif0", tag="dif")]
+        sig = [sb.tile([P, L, P], F32, name=f"sig{q}") for q in range(L)]
+        dif = [sb.tile([P, 2, L, P], F32, name="dif0", tag="dif")]
+        gb = [
+            sb.tile([P, HALF * L], BF16, name="gb0", align_bytes=64),
+            sb.tile([P, HALF * L], BF16, name="gb1", tag="late", align_bytes=64),
+        ]
+        gq = sb.tile([P, N], U32, name="gq", align_bytes=64)
+        gs = sb.tile([P, N], U8, name="gs", align_bytes=64)
 
-        def difference(h, lo, first, count, bank):
-            lanes = slice(first, first + count)
-            cols = slice(lo, lo + P)
+        def score(q, first, count, bank):
             sc = ps.tile([P, count, P], F32, name=f"sc{bank}", tag=f"bank{bank}")
             for e in range(count):
                 r = first + e
@@ -168,65 +169,118 @@ def tile_attend_gml_pl_nce_kernel(
                     out=sc[:, e, :],
                     lhsT=wd_w[:, 2 * P * r : 2 * P * (r + 1)].bitcast(E2M1),
                     lhsT_scale=wd_s[:, P * r : P * (r + 1)],
-                    rhs=xq[h][:, cols].bitcast(E4M3),
-                    rhs_scale=xs[h][:, cols],
+                    rhs=xq[:, quarter(q)].bitcast(E4M3),
+                    rhs_scale=xs[:, quarter(q)],
                     start=True,
                     stop=True,
                 )
-            sig = sb.tile([P, count, P], F32, name=f"sig{bank}", tag=f"sig{bank}", align_bytes=64)
-            nc.scalar.activation(sig[:], sc[:], ACT.Sigmoid)
-            nc.vector.tensor_tensor(dif[h][:, lanes, cols], sig[:], y_half[h][:, lanes, cols], ALU.subtract)
+            nc.scalar.activation(sig[q][:, first : first + count, :], sc[:], ACT.Sigmoid)
 
-        def weigh(engine, h, lo, hi):
-            engine.tensor_tensor(
-                gb[h][:, L * lo : L * hi].rearrange("p (c i r) -> p c r i", i=2, r=L),
-                dif[h][:, :, lo:hi].rearrange("p r (c i) -> p c r i", i=2),
-                cc[:, :, h * HALF + lo : h * HALF + hi].rearrange("p r (c i) -> p c r i", i=2),
+        def difference(q, first, count):
+            h, a = divmod(q, 2)
+            lanes = slice(first, first + count)
+            nc.vector.tensor_tensor(dif[h][:, a, lanes, :], sig[q][:, lanes, :], y_half[h][:, lanes, quarter(a)], ALU.subtract)
+
+        def weigh(q):
+            h, a = divmod(q, 2)
+            nc.vector.tensor_tensor(
+                gb[h][:, L * P * a : L * P * (a + 1)].rearrange("p (c i r) -> p c r i", i=2, r=L),
+                dif[h][:, a].rearrange("p r (c i) -> p c r i", i=2),
+                cc[:, :, quarter(q)].rearrange("p r (c i) -> p c r i", i=2),
                 ALU.mult,
             )
 
-        def quantise_g(h, lo, hi):
-            cols = slice((h + 1) * HALF + lo, (h + 1) * HALF + hi)
-            nc.vector.quantize_mx(out=gq[:, cols].bitcast(E5M2), scales=gs[:, cols], in_=gb[h][:, L * lo : L * hi])
+        def quantise_g(q):
+            h, a = divmod(q, 2)
+            nc.vector.quantize_mx(out=gq[:, quarter(q)].bitcast(E5M2), scales=gs[:, quarter(q)], in_=gb[h][:, L * P * a : L * P * (a + 1)])
 
-        def back(r, first, bank):
-            acc = ps.tile([P, N], F32, name=f"dx_ps{r}", tag=f"bank{bank}")
+        def back(out, r, lo, hi):
             nc.tensor.matmul_mx(
-                out=acc[:],
+                out=out,
                 lhsT=wv_w[:, 2 * P * r : 2 * P * (r + 1)].bitcast(E2M1),
                 lhsT_scale=wv_s[:, P * r : P * (r + 1)],
-                rhs=gq[:, first : first + N].bitcast(E5M2),
-                rhs_scale=gs[:, first : first + N],
+                rhs=gq[:, lo:hi].bitcast(E5M2),
+                rhs_scale=gs[:, lo:hi],
                 start=True,
                 stop=True,
             )
-            return acc
 
+        score(0, 0, 2, 0)
+        score(0, 2, 2, 1)
+        for q in range(1, L):
+            score(q, 0, L, q + 1)
+        difference(0, 0, 2)
+        difference(0, 2, 2)
+        difference(1, 0, L)
+        weigh(0)
+        weigh(1)
+        quantise_g(0)
+        quantise_g(1)
+        dif.append(sb.tile([P, 2, L, P], F32, name="dif1", tag="dif"))
+        difference(2, 0, L)
+        difference(3, 0, L)
+        weigh(2)
+        weigh(3)
+        quantise_g(2)
+        quantise_g(3)
+
+        def scalar_scatter(r, h, src):
+            nc.scalar.activation(win[r][:].indirect(entries[h]), src, ACT.Copy)
+
+        o_rows = out_0.rearrange("(p r) t -> p r t", r=L)
+
+        a_early_ps = ps.tile([P, HALF], F32, name="a_early_ps", tag="bank5")
         for a in range(2):
-            difference(0, a * P, 0, 2, 2 * a)
-            difference(0, a * P, 2, 2, 2 * a + 1)
-            weigh(nc.vector, 0, a * P, (a + 1) * P)
-            quantise_g(0, a * P, (a + 1) * P)
-        wv_s = deal_scales(nc, sb, "wv", wv_raw_s, "sig3")
-        dif.append(sb.tile([P, L, HALF], F32, name="dif1", tag="dif"))
-        difference(1, 0, 0, L, 4)
-        difference(1, P, 0, L, 5)
-        early = [back(r, 0, bank) for r, bank in zip(ORDER[:EARLY], (7, 3))]
-        weigh(nc.vector, 1, 0, P)
-        weigh(nc.gpsimd, 1, P, HALF)
-        nc.scalar.copy(dx[ORDER[0]][:, :HALF], early[0][:, HALF:])
-        dx_early = sb.tile([P, L, HALF], F32, name="dx_early", tag="dif")
-        nc.scalar.copy(dx_early[:, 0, :], early[1][:, HALF:])
-        nc.vector.tensor_copy(win[ORDER[0]][:].indirect(entries[0]), dx[ORDER[0]][:, :HALF])
-        quantise_g(1, 0, HALF)
-        nc.vector.tensor_copy(win[ORDER[1]][:].indirect(entries[0]), dx_early[:, 0, :])
+            back(a_early_ps[:, quarter(a)], 0, a * P, (a + 1) * P)
+        b_early_ps = ps.tile([P, HALF], F32, name="b_early_ps", tag="bank2")
+        back(b_early_ps[:], 1, 0, HALF)
+        c_early_ps = ps.tile([P, HALF], F32, name="c_early_ps", tag="bank3")
+        back(c_early_ps[:], 2, 0, HALF)
+        d_early_ps = ps.tile([P, HALF], F32, name="d_early_ps", tag="bank1")
+        back(d_early_ps[:], 3, 0, HALF)
+        a_early = sb.tile([P, HALF], F32, name="a_early")
+        nc.scalar.copy(a_early[:], a_early_ps[:])
+        scalar_scatter(0, 0, a_early[:])
+
+        win[2] = sb.tile([P, T], F32, name="win2", tag="late", align_bytes=64)
+        nc.gpsimd.memset(win[2][:].bitcast(I32), 0)
+
+        a_late_ps = ps.tile([P, HALF], F32, name="a_late_ps", tag="bank6")
+        for a in range(2):
+            back(a_late_ps[:, quarter(a)], 0, HALF + a * P, HALF + (a + 1) * P)
+        bc_late_ps = ps.tile([P, 2, HALF], F32, name="bc_late_ps", tag="bank7")
+        for e in range(2):
+            back(bc_late_ps[:, e, :], 1 + e, HALF, N)
+        d_late_ps = ps.tile([P, HALF], F32, name="d_late_ps", tag="bank0")
+        back(d_late_ps[:], 3, HALF, N)
+
+        a_late = sb.tile([P, HALF], F32, name="a_late", tag="turn")
+        bd = sb.tile([P, HALF + N], F32, name="bd", tag="dif")
+        b_early, d_all = bd[:, :HALF], bd[:, HALF:]
+        bc_late = sb.tile([P, 2, HALF], F32, name="bc_late")
+        nc.scalar.copy(a_late[:], a_late_ps[:])
+        scalar_scatter(0, 1, a_late[:])
+        nc.scalar.dma_start(out=o_rows[:, 0, :], in_=win[0][:])
+        nc.vector.tensor_copy(b_early, b_early_ps[:])
+        nc.vector.tensor_copy(d_all[:, :HALF], d_early_ps[:])
+        nc.vector.tensor_copy(win[1][:].indirect(entries[0]), b_early)
+        nc.vector.tensor_copy(bc_late[:], bc_late_ps[:])
+        nc.vector.tensor_copy(d_all[:, HALF:], d_late_ps[:])
+        nc.vector.tensor_copy(win[1][:].indirect(entries[1]), bc_late[:, 0, :])
+        nc.sync.dma_start(out=o_rows[:, 1, :], in_=win[1][:])
+        c_early = sb.tile([P, HALF], F32, name="c_early", tag="turn")
+        nc.scalar.copy(c_early[:], c_early_ps[:])
+        scalar_scatter(2, 0, c_early[:])
+        scalar_scatter(2, 1, bc_late[:, 1, :])
+        nc.scalar.dma_start(out=o_rows[:, 2, :], in_=win[2][:])
+        nc.vector.tensor_copy(win[3][:].indirect(offsets[:]), d_all)
+        nc.sync.dma_start(out=o_rows[:, 3, :], in_=win[3][:])
 
         pairs = sb.tile([P, T * L], BF16, name="pairs", align_bytes=64)
-
         ob = sb.tile([P, T * L], BF16, name="ob", align_bytes=64)
-
-        def place_lane(copy, r, lo, hi):
-            copy(ob[:, L * lo : L * hi].rearrange("p (n r) -> p n r", r=L)[:, :, r], win[r][:, lo:hi])
+        o_scales = sb.tile([P, PLANE], U8, name="os_", align_bytes=64)
+        o_codes = sb.tile([P, T], U32, name="oq", align_bytes=64)
+        o_words = out_1[0].rearrange("p n t -> p (n t)")
 
         def gpsimd_copy(out, in_):
             nc.gpsimd.tensor_scalar(out, in_, 1.0, 0.0, ALU.mult, ALU.add)
@@ -237,60 +291,42 @@ def tile_attend_gml_pl_nce_kernel(
                 win[r][:, lo:hi].rearrange("p (b n) -> p b n", n=BLK),
             )
 
-        for k, (r, bank) in enumerate(zip(ORDER, (6, 0, 1, 2))):
-            acc = back(r, HALF, bank)
-            todo = slice(HALF, N) if k < EARLY else slice(0, N)
-            nc.scalar.copy(dx[r][:, todo], acc[:, todo])
-        o_rows = out_0.rearrange("(p r) t -> p r t", r=L)
-        for k, r in enumerate(ORDER):
-            if k < EARLY:
-                nc.vector.tensor_copy(win[r][:].indirect(entries[1]), dx[r][:, HALF:])
-            else:
-                nc.vector.tensor_copy(win[r][:].indirect(offsets[:]), dx[r][:])
-            nc.sync.dma_start(out=o_rows[:, r, :], in_=win[r][:])
-            if r != ORDER[-1]:
-                placer, rounder = (gpsimd_copy, nc.scalar.copy) if k == 0 else (nc.scalar.copy, gpsimd_copy)
-                place_lane(placer, r, 0, PLACED)
-                round_lane(rounder, r, PLACED, T)
-
-        o_scales = sb.tile([P, PLANE], U8, name="os_", align_bytes=64)
-        o_codes = sb.tile([P, T], U32, name="oq", align_bytes=64)
-        o_words = out_1[0].rearrange("p n t -> p (n t)")
-
         def weave(copy, word, lo, hi):
             copy(
                 ob[:, L * lo : L * hi].bitcast(word).rearrange("p (b n u) -> p b n u", n=BLK, u=2),
                 pairs[:, L * lo : L * hi].bitcast(word).rearrange("p (b u n) -> p b n u", u=2, n=BLK),
             )
 
-        last_lane = ORDER[-1]
-        round_lane(nc.scalar.copy, last_lane, PLACED, 1280)
-        round_lane(nc.scalar.copy, last_lane, 1280, 1536)
-        weave(nc.scalar.copy, U32, PLACED, 1280)
-        round_lane(nc.scalar.copy, last_lane, 1536, 1792)
-        weave(nc.scalar.copy, U32, 1280, 1536)
-        weave(nc.scalar.copy, U32, 1536, 1664)
-        round_lane(nc.scalar.copy, last_lane, 1920, T)
-        weave(nc.scalar.copy, U32, 1664, 1792)
-        weave(nc.scalar.copy, U32, 1920, T)
+        def quantise_out(lo, hi):
+            j, col = divmod(lo, PLANE)
+            nc.vector.quantize_mx(
+                out=o_codes[:, lo:hi].bitcast(E4M3), scales=o_scales[4 * j :, col : col + hi - lo], in_=ob[:, L * lo : L * hi]
+            )
 
-        ahead = {
-            0: [(place_lane, last_lane, 0, 256), (place_lane, last_lane, 256, 512)],
-            256: [(place_lane, last_lane, 512, 768)],
-            512: [(place_lane, last_lane, 768, PLACED)],
-            1536: [(round_lane, last_lane, *VECTOR_BLOCK)],
-            1664: [(weave, I32, *VECTOR_BLOCK)],
-        }
+        round_lane(gpsimd_copy, 0, 0, GPSIMD_COLS)
+        round_lane(gpsimd_copy, 1, 0, GPSIMD_COLS)
+        for r in range(2):
+            round_lane(nc.scalar.copy, r, GPSIMD_COLS, T)
+        round_lane(nc.scalar.copy, 2, VECTOR_COLS, T)
+        for k, piece in enumerate(SCALAR_PIECES):
+            round_lane(nc.scalar.copy, 3, *piece)
+            if k > 0:
+                weave(nc.scalar.copy, U32, *SCALAR_PIECES[k - 1])
+        weave(nc.scalar.copy, U32, *SCALAR_PIECES[-1])
+
+        round_lane(nc.vector.tensor_copy, 2, 0, VECTOR_COLS)
+        steps = len(VECTOR_PIECES)
+        for k in range(steps + 2):
+            if k < steps:
+                round_lane(nc.vector.tensor_copy, 3, *VECTOR_PIECES[k])
+            if 1 <= k <= steps:
+                weave(nc.vector.tensor_copy, I32, *VECTOR_PIECES[k - 1])
+            if k >= 2:
+                quantise_out(*VECTOR_PIECES[k - 2])
+        for lo, hi in SCALAR_PIECES:
+            for first in range(lo, hi, BLK):
+                quantise_out(first, first + BLK)
         for lo, hi in CODE_STORES:
-            for first, last in [c for c in QUANTS if lo <= c[0] < hi]:
-                for step, *args in ahead.get(first, []):
-                    step(nc.vector.tensor_copy, *args)
-                j, col = divmod(first, PLANE)
-                nc.vector.quantize_mx(
-                    out=o_codes[:, first:last].bitcast(E4M3),
-                    scales=o_scales[4 * j :, col : col + last - first],
-                    in_=ob[:, L * first : L * last],
-                )
             nc.sync.dma_start(out=o_words[:, L * lo : L * hi].bitcast(I32), in_=o_codes[:, lo:hi].bitcast(I32))
         for q in range(QUADRANTS):
             queue = nc.scalar if q % 2 == 0 else nc.sync

@@ -28,7 +28,7 @@ PLANE = T // 4
 GPSIMD_COLS = 1536
 VECTOR_COLS = 1152
 VECTOR_PIECES = [(0, 256), (256, 512), (512, 768), (768, 1024), (1024, VECTOR_COLS)]
-SCALAR_PIECES = [(VECTOR_COLS, 1536), (1536, 1792), (1792, 1920), (1920, T)]
+SCALAR_PIECES = [(VECTOR_COLS, 1280), (1280, 1536), (1536, 1792), (1792, 1920), (1920, T)]
 CODE_STORES = [(0, 512), (512, 1024), (1024, 1536), (1536, 1792), (1792, T)]
 
 
@@ -95,6 +95,8 @@ def tile_attend_gml_pl_nce_kernel(
 
         ident = sb.tile([P, P], F32, name="ident")
         make_identity(nc, ident[:])
+        warm = sb.tile([P, 1], F32, name="warm")
+        nc.scalar.activation(warm[:], ident[:, 0:1], ACT.Sigmoid)
 
         win = {r: sb.tile([P, T], F32, name=f"win{r}") for r in range(2)}
         for r in range(2):
@@ -314,7 +316,8 @@ def tile_attend_gml_pl_nce_kernel(
                 weave(nc.scalar.copy, U32, *SCALAR_PIECES[k - 1])
         weave(nc.scalar.copy, U32, *SCALAR_PIECES[-1])
 
-        round_lane(nc.vector.tensor_copy, 2, 0, VECTOR_COLS)
+        round_lane(nc.vector.tensor_copy, 2, 0, 1024)
+        round_lane(nc.vector.tensor_copy, 2, 1024, VECTOR_COLS)
         steps = len(VECTOR_PIECES)
         for k in range(steps + 2):
             if k < steps:
@@ -323,9 +326,8 @@ def tile_attend_gml_pl_nce_kernel(
                 weave(nc.vector.tensor_copy, I32, *VECTOR_PIECES[k - 1])
             if k >= 2:
                 quantise_out(*VECTOR_PIECES[k - 2])
-        for lo, hi in SCALAR_PIECES:
-            for first in range(lo, hi, BLK):
-                quantise_out(first, first + BLK)
+        for piece in SCALAR_PIECES:
+            quantise_out(*piece)
         for lo, hi in CODE_STORES:
             nc.sync.dma_start(out=o_words[:, L * lo : L * hi].bitcast(I32), in_=o_codes[:, lo:hi].bitcast(I32))
         for q in range(QUADRANTS):

@@ -25,10 +25,10 @@ HALF = N // 2
 HALF_COLS = HALF // 16
 BLK = 128
 PLANE = T // 4
-GPSIMD_COLS = 1536
+GPSIMD_COLS = 1664
 VECTOR_COLS = 1152
 VECTOR_PIECES = [(0, 256), (256, 512), (512, 768), (768, 1024), (1024, VECTOR_COLS)]
-SCALAR_PIECES = [(VECTOR_COLS, 1280), (1280, 1536), (1536, 1792), (1792, 1920), (1920, T)]
+SCALAR_PIECES = [(VECTOR_COLS, 1536), (1536, 1792), (1792, 1920), (1920, T)]
 CODE_STORES = [(0, 512), (512, 1024), (1024, 1536), (1536, 1792), (1792, T)]
 
 
@@ -326,7 +326,7 @@ def tile_attend_gml_pl_nce_kernel(
                 weave(nc.vector.tensor_copy, I32, *VECTOR_PIECES[k - 1])
             if k >= 2:
                 quantise_out(*VECTOR_PIECES[k - 2])
-        for piece in SCALAR_PIECES:
+        for piece in [(VECTOR_COLS, 1280), (1280, 1536)] + SCALAR_PIECES[1:]:
             quantise_out(*piece)
         for lo, hi in CODE_STORES:
             nc.sync.dma_start(out=o_words[:, L * lo : L * hi].bitcast(I32), in_=o_codes[:, lo:hi].bitcast(I32))

@@ -25,7 +25,7 @@ HALF = N // 2
 HALF_COLS = HALF // 16
 BLK = 128
 PLANE = T // 4
-GPSIMD_COLS = 1664
+GPSIMD_COLS = 1408
 VECTOR_COLS = 1152
 VECTOR_PIECES = [(0, 256), (256, 512), (512, 768), (768, 1024), (1024, VECTOR_COLS)]
 SCALAR_PIECES = [(VECTOR_COLS, 1536), (1536, 1792), (1792, 1920), (1920, T)]

@@ -25,10 +25,12 @@ HALF = N // 2
 HALF_COLS = HALF // 16
 BLK = 128
 PLANE = T // 4
+
 GPSIMD_COLS = 1408
 VECTOR_COLS = 1152
-VECTOR_PIECES = [(0, 256), (256, 512), (512, 768), (768, 1024), (1024, VECTOR_COLS)]
-SCALAR_PIECES = [(VECTOR_COLS, 1536), (1536, 1792), (1792, 1920), (1920, T)]
+VECTOR_EVEN = 1024
+VECTOR_PIECES = [(c, c + 2 * BLK) for c in range(0, VECTOR_EVEN, 2 * BLK)] + [(VECTOR_EVEN, VECTOR_COLS)]
+SCALAR_PIECES = [(VECTOR_COLS, 1280), (1280, 1536), (1536, 1792), (1792, 1920), (1920, T)]
 CODE_STORES = [(0, 512), (512, 1024), (1024, 1536), (1536, 1792), (1792, T)]
 
 
@@ -121,8 +123,8 @@ def tile_attend_gml_pl_nce_kernel(
         xq = sb.tile([P, N], U32, name="xq", align_bytes=64)
         xs = sb.tile([P, N], U8, name="xs", align_bytes=64)
         entries = [offsets[:, h * HALF_COLS : (h + 1) * HALF_COLS] for h in range(2)]
-        slots = xb[:].rearrange("p (a n) r -> p a n r", n=P)
-        places = [slots[:, 1:4:2], slots[:, 0:3:2]]
+        runs = xb[:].rearrange("p (a n) r -> p a n r", n=P)
+        places = [runs[:, 1:4:2], runs[:, 0:3:2]]
 
         def quarter(q):
             return slice(q * P, (q + 1) * P)
@@ -305,10 +307,11 @@ def tile_attend_gml_pl_nce_kernel(
                 out=o_codes[:, lo:hi].bitcast(E4M3), scales=o_scales[4 * j :, col : col + hi - lo], in_=ob[:, L * lo : L * hi]
             )
 
-        round_lane(gpsimd_copy, 0, 0, GPSIMD_COLS)
-        round_lane(gpsimd_copy, 1, 0, GPSIMD_COLS)
         for r in range(2):
-            round_lane(nc.scalar.copy, r, GPSIMD_COLS, T)
+            round_lane(gpsimd_copy, r, 0, GPSIMD_COLS)
+        for lo in range(GPSIMD_COLS, T, BLK):
+            round_lane(nc.scalar.copy, 0, lo, lo + BLK)
+        round_lane(nc.scalar.copy, 1, GPSIMD_COLS, T)
         round_lane(nc.scalar.copy, 2, VECTOR_COLS, T)
         for k, piece in enumerate(SCALAR_PIECES):
             round_lane(nc.scalar.copy, 3, *piece)
@@ -316,17 +319,16 @@ def tile_attend_gml_pl_nce_kernel(
                 weave(nc.scalar.copy, U32, *SCALAR_PIECES[k - 1])
         weave(nc.scalar.copy, U32, *SCALAR_PIECES[-1])
 
-        round_lane(nc.vector.tensor_copy, 2, 0, 1024)
-        round_lane(nc.vector.tensor_copy, 2, 1024, VECTOR_COLS)
         steps = len(VECTOR_PIECES)
         for k in range(steps + 2):
             if k < steps:
-                round_lane(nc.vector.tensor_copy, 3, *VECTOR_PIECES[k])
+                for r in (3, 2):
+                    round_lane(nc.vector.tensor_copy, r, *VECTOR_PIECES[k])
             if 1 <= k <= steps:
                 weave(nc.vector.tensor_copy, I32, *VECTOR_PIECES[k - 1])
             if k >= 2:
                 quantise_out(*VECTOR_PIECES[k - 2])
-        for piece in [(VECTOR_COLS, 1280), (1280, 1536)] + SCALAR_PIECES[1:]:
+        for piece in SCALAR_PIECES:
             quantise_out(*piece)
         for lo, hi in CODE_STORES:
             nc.sync.dma_start(out=o_words[:, L * lo : L * hi].bitcast(I32), in_=o_codes[:, lo:hi].bitcast(I32))

@@ -48,9 +48,9 @@ def deal_words(nc, pool, name, raw_w):
     return w
 
 
-def deal_scales(nc, pool, name, raw_s):
+def deal_scales(engine, pool, name, raw_s):
     s = pool.tile([P, 512], U8, name=name + "_s", align_bytes=64)
-    nc.vector.tensor_copy(
+    engine.tensor_copy(
         out=s[:].rearrange("p (r s) -> p r s", r=L),
         in_=raw_s[:].rearrange("p (s r) -> p r s", r=L),
     )
@@ -143,7 +143,7 @@ def tile_attend_gml_pl_nce_kernel(
             gather(r, 1)
         win[3] = sb.tile([P, T], F32, name="win3", tag="x_pl0")
         nc.gpsimd.memset(win[3][:].bitcast(I32), 0)
-        wd_s = deal_scales(nc, sb, "wd", wd_raw_s)
+        wd_s = deal_scales(nc.gpsimd, sb, "wd", wd_raw_s)
         gather(2, 0)
         gather(2, 1)
         gather(3, 0)
@@ -151,7 +151,7 @@ def tile_attend_gml_pl_nce_kernel(
         quantise_x(0)
         quantise_x(1)
         gather(3, 1)
-        wv_s = deal_scales(nc, sb, "wv", wv_raw_s)
+        wv_s = deal_scales(nc.vector, sb, "wv", wv_raw_s)
         quantise_x(2)
         quantise_x(3)
         wv_w = deal_words(nc, sb, "wv", wv_raw_w)

@@ -71,7 +71,6 @@ def tile_attend_gml_pl_nce_kernel(
         wd_raw_s = sb.tile([P, 512], U8, name="wd_raw_s", align_bytes=64)
         wv_raw_s = sb.tile([P, 512], U8, name="wv_raw_s", align_bytes=64)
         nc.gpsimd.memset(wd_raw_s[:].bitcast(I32), 0)
-        nc.gpsimd.memset(wv_raw_s[:].bitcast(I32), 0)
         wd_raw_w = sb.tile([P, 2 * 512], U8, name="wd_raw_w", align_bytes=64)
         wv_raw_w = sb.tile([P, 2 * 512], U8, name="wv_raw_w", align_bytes=64)
 
@@ -80,6 +79,10 @@ def tile_attend_gml_pl_nce_kernel(
         x_lane = [sb.tile([P, T], F32, name=f"x_pl{r}", tag=f"x_pl{r}") for r in range(L)]
         y_rows = y.rearrange("(p r) i -> p r i", r=L)
         y_half = [sb.tile([P, L, HALF], F32, name=f"y_h{h}") for h in range(2)]
+
+        ident = sb.tile([P, P], F32, name="ident")
+        make_identity(nc, ident[:])
+        nc.gpsimd.memset(wv_raw_s[:].bitcast(I32), 0)
 
         nc.sync.dma_start(out=x_lane[0][:], in_=x_rows[:, 0, :])
         nc.sync.dma_start(out=rows[0:1, :], in_=cw.rearrange("v o -> o v"))
@@ -95,14 +98,14 @@ def tile_attend_gml_pl_nce_kernel(
         nc.sync.dma_start(out=wv_raw_w[:].bitcast(I32), in_=wv_words[0].bitcast(I32))
         nc.sync.dma_start(out=y_half[1][:], in_=y_rows[:, :, HALF:])
 
-        ident = sb.tile([P, P], F32, name="ident")
-        make_identity(nc, ident[:])
         warm = sb.tile([P, 1], F32, name="warm")
         nc.scalar.activation(warm[:], ident[:, 0:1], ACT.Sigmoid)
 
         win = {r: sb.tile([P, T], F32, name=f"win{r}") for r in range(2)}
         for r in range(2):
             nc.vector.memset(win[r][:].bitcast(I32), 0)
+        win[3] = sb.tile([P, T], F32, name="win3")
+        nc.gpsimd.memset(win[3][:].bitcast(I32), 0)
 
         rows_ps = ps.tile([P, L, P], F32, name="rows_ps", tag="bank6")
         for m in range(L):
@@ -141,8 +144,6 @@ def tile_attend_gml_pl_nce_kernel(
         for r in range(2):
             gather(r, 0)
             gather(r, 1)
-        win[3] = sb.tile([P, T], F32, name="win3", tag="x_pl0")
-        nc.gpsimd.memset(win[3][:].bitcast(I32), 0)
         wd_s = deal_scales(nc.gpsimd, sb, "wd", wd_raw_s)
         gather(2, 0)
         gather(2, 1)

@@ -160,8 +160,8 @@ def tile_attend_gml_pl_nce_kernel(
         sig = [sb.tile([P, L, P], F32, name=f"sig{q}") for q in range(L)]
         dif = [sb.tile([P, 2, L, P], F32, name="dif0", tag="dif")]
         gb = [
-            sb.tile([P, HALF * L], BF16, name="gb0", align_bytes=64),
-            sb.tile([P, HALF * L], BF16, name="gb1", tag="late", align_bytes=64),
+            sb.tile([P, HALF * L], BF16, name="gb0", tag="early", align_bytes=64),
+            sb.tile([P, HALF * L], BF16, name="gb1", align_bytes=64),
         ]
         gq = sb.tile([P, N], U32, name="gq", align_bytes=64)
         gs = sb.tile([P, N], U8, name="gs", align_bytes=64)
@@ -221,64 +221,69 @@ def tile_attend_gml_pl_nce_kernel(
         weigh(1)
         quantise_g(0)
         quantise_g(1)
+
+        def scalar_scatter(r, h, src):
+            nc.scalar.activation(win[r][:].indirect(entries[h]), src, ACT.Copy)
+
+        def vector_scatter(r, lists, src):
+            nc.vector.tensor_copy(win[r][:].indirect(lists), src)
+
+        o_rows = out_0.rearrange("(p r) t -> p r t", r=L)
+
+        win[2] = sb.tile([P, T], F32, name="win2", tag="early", align_bytes=64)
+        nc.gpsimd.memset(win[2][:].bitcast(I32), 0)
+
+        a_early_ps = ps.tile([P, HALF], F32, name="a_early_ps", tag="bank5")
+        for a in range(2):
+            back(a_early_ps[:, quarter(a)], 0, a * P, (a + 1) * P)
+        d_early_ps = ps.tile([P, HALF], F32, name="d_early_ps", tag="bank1")
+        back(d_early_ps[:], 3, 0, HALF)
+        b_early_ps = ps.tile([P, HALF], F32, name="b_early_ps", tag="bank2")
+        back(b_early_ps[:], 1, 0, HALF)
+        shared_ps = ps.tile([P, HALF + P], F32, name="shared_ps", tag="bank3")
+        back(shared_ps[:, :HALF], 2, 0, HALF)
+        a_early = sb.tile([P, HALF], F32, name="a_early")
+        d_all = sb.tile([P, N], F32, name="d_all")
+        nc.scalar.copy(a_early[:], a_early_ps[:])
+        nc.scalar.copy(d_all[:, :HALF], d_early_ps[:])
+        scalar_scatter(0, 0, a_early[:])
+
         dif.append(sb.tile([P, 2, L, P], F32, name="dif1", tag="dif"))
         difference(2, 0, L)
         difference(3, 0, L)
         weigh(2)
         weigh(3)
+        b_early = sb.tile([P, HALF], F32, name="b_early", tag="dif")
+        nc.vector.tensor_copy(b_early[:], b_early_ps[:])
         quantise_g(2)
         quantise_g(3)
+        vector_scatter(1, entries[0], b_early[:])
 
-        def scalar_scatter(r, h, src):
-            nc.scalar.activation(win[r][:].indirect(entries[h]), src, ACT.Copy)
-
-        o_rows = out_0.rearrange("(p r) t -> p r t", r=L)
-
-        a_early_ps = ps.tile([P, HALF], F32, name="a_early_ps", tag="bank5")
-        for a in range(2):
-            back(a_early_ps[:, quarter(a)], 0, a * P, (a + 1) * P)
-        b_early_ps = ps.tile([P, HALF], F32, name="b_early_ps", tag="bank2")
-        back(b_early_ps[:], 1, 0, HALF)
-        c_early_ps = ps.tile([P, HALF], F32, name="c_early_ps", tag="bank3")
-        back(c_early_ps[:], 2, 0, HALF)
-        d_early_ps = ps.tile([P, HALF], F32, name="d_early_ps", tag="bank1")
-        back(d_early_ps[:], 3, 0, HALF)
-        a_early = sb.tile([P, HALF], F32, name="a_early")
-        nc.scalar.copy(a_early[:], a_early_ps[:])
-        scalar_scatter(0, 0, a_early[:])
-
-        win[2] = sb.tile([P, T], F32, name="win2", tag="late", align_bytes=64)
-        nc.gpsimd.memset(win[2][:].bitcast(I32), 0)
-
-        a_late_ps = ps.tile([P, HALF], F32, name="a_late_ps", tag="bank6")
-        for a in range(2):
-            back(a_late_ps[:, quarter(a)], 0, HALF + a * P, HALF + (a + 1) * P)
+        a_third_ps = ps.tile([P, P], F32, name="a_third_ps", tag="bank6")
+        back(a_third_ps[:], 0, HALF, HALF + P)
+        back(shared_ps[:, HALF:], 0, HALF + P, N)
         bc_late_ps = ps.tile([P, 2, HALF], F32, name="bc_late_ps", tag="bank7")
         for e in range(2):
             back(bc_late_ps[:, e, :], 1 + e, HALF, N)
         d_late_ps = ps.tile([P, HALF], F32, name="d_late_ps", tag="bank0")
         back(d_late_ps[:], 3, HALF, N)
 
-        a_late = sb.tile([P, HALF], F32, name="a_late", tag="turn")
-        bd = sb.tile([P, HALF + N], F32, name="bd", tag="dif")
-        b_early, d_all = bd[:, :HALF], bd[:, HALF:]
+        a_late = sb.tile([P, HALF], F32, name="a_late")
+        c_early = sb.tile([P, HALF], F32, name="c_early")
         bc_late = sb.tile([P, 2, HALF], F32, name="bc_late")
-        nc.scalar.copy(a_late[:], a_late_ps[:])
+        nc.scalar.copy(a_late[:, :P], a_third_ps[:])
+        nc.scalar.copy(a_late[:, P:], shared_ps[:, HALF:])
+        nc.scalar.copy(c_early[:], shared_ps[:, :HALF])
         scalar_scatter(0, 1, a_late[:])
-        nc.scalar.dma_start(out=o_rows[:, 0, :], in_=win[0][:])
-        nc.vector.tensor_copy(b_early, b_early_ps[:])
-        nc.vector.tensor_copy(d_all[:, :HALF], d_early_ps[:])
-        nc.vector.tensor_copy(win[1][:].indirect(entries[0]), b_early)
+        nc.sync.dma_start(out=o_rows[:, 0, :], in_=win[0][:])
+        scalar_scatter(2, 0, c_early[:])
         nc.vector.tensor_copy(bc_late[:], bc_late_ps[:])
         nc.vector.tensor_copy(d_all[:, HALF:], d_late_ps[:])
-        nc.vector.tensor_copy(win[1][:].indirect(entries[1]), bc_late[:, 0, :])
+        vector_scatter(1, entries[1], bc_late[:, 0, :])
         nc.sync.dma_start(out=o_rows[:, 1, :], in_=win[1][:])
-        c_early = sb.tile([P, HALF], F32, name="c_early", tag="turn")
-        nc.scalar.copy(c_early[:], c_early_ps[:])
-        scalar_scatter(2, 0, c_early[:])
         scalar_scatter(2, 1, bc_late[:, 1, :])
         nc.scalar.dma_start(out=o_rows[:, 2, :], in_=win[2][:])
-        nc.vector.tensor_copy(win[3][:].indirect(offsets[:]), d_all)
+        vector_scatter(3, offsets[:], d_all[:])
         nc.sync.dma_start(out=o_rows[:, 3, :], in_=win[3][:])
 
         pairs = sb.tile([P, T * L], BF16, name="pairs", align_bytes=64)

@@ -275,7 +275,7 @@ def tile_attend_gml_pl_nce_kernel(
         nc.scalar.copy(a_late[:, P:], shared_ps[:, HALF:])
         nc.scalar.copy(c_early[:], shared_ps[:, :HALF])
         scalar_scatter(0, 1, a_late[:])
-        nc.sync.dma_start(out=o_rows[:, 0, :], in_=win[0][:])
+        nc.scalar.dma_start(out=o_rows[:, 0, :], in_=win[0][:])
         scalar_scatter(2, 0, c_early[:])
         nc.vector.tensor_copy(bc_late[:], bc_late_ps[:])
         nc.vector.tensor_copy(d_all[:, HALF:], d_late_ps[:])

@@ -282,9 +282,8 @@ def tile_attend_gml_pl_nce_kernel(
         vector_scatter(1, entries[1], bc_late[:, 0, :])
         nc.sync.dma_start(out=o_rows[:, 1, :], in_=win[1][:])
         scalar_scatter(2, 1, bc_late[:, 1, :])
-        nc.scalar.dma_start(out=o_rows[:, 2, :], in_=win[2][:])
+        nc.sync.dma_start(out=o_rows[:, 2, :], in_=win[2][:])
         vector_scatter(3, offsets[:], d_all[:])
-        nc.sync.dma_start(out=o_rows[:, 3, :], in_=win[3][:])
 
         pairs = sb.tile([P, T * L], BF16, name="pairs", align_bytes=64)
         ob = sb.tile([P, T * L], BF16, name="ob", align_bytes=64)
@@ -319,6 +318,7 @@ def tile_attend_gml_pl_nce_kernel(
             round_lane(nc.scalar.copy, 0, lo, lo + BLK)
         round_lane(nc.scalar.copy, 1, GPSIMD_COLS, T)
         round_lane(nc.scalar.copy, 2, VECTOR_COLS, T)
+        nc.scalar.dma_start(out=o_rows[:, 3, :], in_=win[3][:])
         for k, piece in enumerate(SCALAR_PIECES):
             round_lane(nc.scalar.copy, 3, *piece)
             if k > 0:

@@ -26,10 +26,9 @@ HALF_COLS = HALF // 16
 BLK = 128
 PLANE = T // 4
 
-GPSIMD_COLS = 1408
-VECTOR_COLS = 1152
-VECTOR_EVEN = 1024
-VECTOR_PIECES = [(c, c + 2 * BLK) for c in range(0, VECTOR_EVEN, 2 * BLK)] + [(VECTOR_EVEN, VECTOR_COLS)]
+GPSIMD_COLS = 1536
+VECTOR_COLS = 1024
+VECTOR_PIECES = [(c, c + 2 * BLK) for c in range(0, VECTOR_COLS, 2 * BLK)]
 SCALAR_PIECES = [(VECTOR_COLS, 1280), (1280, 1536), (1536, 1792), (1792, 1920), (1920, T)]
 CODE_STORES = [(0, 512), (512, 1024), (1024, 1536), (1536, 1792), (1792, T)]
 
@@ -159,10 +158,7 @@ def tile_attend_gml_pl_nce_kernel(
 
         sig = [sb.tile([P, L, P], F32, name=f"sig{q}") for q in range(L)]
         dif = [sb.tile([P, 2, L, P], F32, name="dif0", tag="dif")]
-        gb = [
-            sb.tile([P, HALF * L], BF16, name="gb0", tag="early", align_bytes=64),
-            sb.tile([P, HALF * L], BF16, name="gb1", align_bytes=64),
-        ]
+        gb = [sb.tile([P, P * L], BF16, name=f"gb{q}", tag=f"gb{q}", align_bytes=64) for q in range(L)]
         gq = sb.tile([P, N], U32, name="gq", align_bytes=64)
         gs = sb.tile([P, N], U8, name="gs", align_bytes=64)
 
@@ -189,15 +185,14 @@ def tile_attend_gml_pl_nce_kernel(
         def weigh(q):
             h, a = divmod(q, 2)
             nc.vector.tensor_tensor(
-                gb[h][:, L * P * a : L * P * (a + 1)].rearrange("p (c i r) -> p c r i", i=2, r=L),
+                gb[q][:].rearrange("p (c i r) -> p c r i", i=2, r=L),
                 dif[h][:, a].rearrange("p r (c i) -> p c r i", i=2),
                 cc[:, :, quarter(q)].rearrange("p r (c i) -> p c r i", i=2),
                 ALU.mult,
             )
 
         def quantise_g(q):
-            h, a = divmod(q, 2)
-            nc.vector.quantize_mx(out=gq[:, quarter(q)].bitcast(E5M2), scales=gs[:, quarter(q)], in_=gb[h][:, L * P * a : L * P * (a + 1)])
+            nc.vector.quantize_mx(out=gq[:, quarter(q)].bitcast(E5M2), scales=gs[:, quarter(q)], in_=gb[q][:])
 
         def back(out, r, lo, hi):
             nc.tensor.matmul_mx(
@@ -230,7 +225,7 @@ def tile_attend_gml_pl_nce_kernel(
 
         o_rows = out_0.rearrange("(p r) t -> p r t", r=L)
 
-        win[2] = sb.tile([P, T], F32, name="win2", tag="early", align_bytes=64)
+        win[2] = sb.tile([P, T], F32, name="win2", tag="gb0", align_bytes=64)
         nc.gpsimd.memset(win[2][:].bitcast(I32), 0)
 
         a_early_ps = ps.tile([P, HALF], F32, name="a_early_ps", tag="bank5")
@@ -253,11 +248,8 @@ def tile_attend_gml_pl_nce_kernel(
         difference(3, 0, L)
         weigh(2)
         weigh(3)
-        b_early = sb.tile([P, HALF], F32, name="b_early", tag="dif")
-        nc.vector.tensor_copy(b_early[:], b_early_ps[:])
         quantise_g(2)
         quantise_g(3)
-        vector_scatter(1, entries[0], b_early[:])
 
         a_third_ps = ps.tile([P, P], F32, name="a_third_ps", tag="bank6")
         back(a_third_ps[:], 0, HALF, HALF + P)
@@ -271,7 +263,10 @@ def tile_attend_gml_pl_nce_kernel(
         a_late = sb.tile([P, HALF], F32, name="a_late")
         c_early = sb.tile([P, HALF], F32, name="c_early")
         bc_late = sb.tile([P, 2, HALF], F32, name="bc_late")
-        nc.scalar.copy(a_late[:, :P], a_third_ps[:])
+        b_early = sb.tile([P, HALF], F32, name="b_early", tag="dif")
+        nc.vector.tensor_copy(b_early[:], b_early_ps[:])
+        nc.vector.tensor_copy(a_late[:, :P], a_third_ps[:])
+        vector_scatter(1, entries[0], b_early[:])
         nc.scalar.copy(a_late[:, P:], shared_ps[:, HALF:])
         nc.scalar.copy(c_early[:], shared_ps[:, :HALF])
         scalar_scatter(0, 1, a_late[:])
@@ -317,8 +312,9 @@ def tile_attend_gml_pl_nce_kernel(
         for lo in range(GPSIMD_COLS, T, BLK):
             round_lane(nc.scalar.copy, 0, lo, lo + BLK)
         round_lane(nc.scalar.copy, 1, GPSIMD_COLS, T)
-        round_lane(nc.scalar.copy, 2, VECTOR_COLS, T)
+        round_lane(nc.scalar.copy, 2, VECTOR_COLS, GPSIMD_COLS)
         nc.scalar.dma_start(out=o_rows[:, 3, :], in_=win[3][:])
+        round_lane(nc.scalar.copy, 2, GPSIMD_COLS, T)
         for k, piece in enumerate(SCALAR_PIECES):
             round_lane(nc.scalar.copy, 3, *piece)
             if k > 0:

@@ -321,15 +321,15 @@ def tile_attend_gml_pl_nce_kernel(
                 weave(nc.scalar.copy, U32, *SCALAR_PIECES[k - 1])
         weave(nc.scalar.copy, U32, *SCALAR_PIECES[-1])
 
-        steps = len(VECTOR_PIECES)
-        for k in range(steps + 2):
-            if k < steps:
+        for first in range(0, len(VECTOR_PIECES), 2):
+            both = VECTOR_PIECES[first : first + 2]
+            for piece in both:
                 for r in (3, 2):
-                    round_lane(nc.vector.tensor_copy, r, *VECTOR_PIECES[k])
-            if 1 <= k <= steps:
-                weave(nc.vector.tensor_copy, I32, *VECTOR_PIECES[k - 1])
-            if k >= 2:
-                quantise_out(*VECTOR_PIECES[k - 2])
+                    round_lane(nc.vector.tensor_copy, r, *piece)
+            for piece in both:
+                weave(nc.vector.tensor_copy, I32, *piece)
+            for piece in both:
+                quantise_out(*piece)
         for piece in SCALAR_PIECES:
             quantise_out(*piece)
         for lo, hi in CODE_STORES:

from contextlib import ExitStack

import concourse.mybir as mybir
from concourse.masks import make_identity

N, T, D, V = 512, 2048, 512, 512
FLOPS = 2 * 2 * N * D * V

F32 = mybir.dt.float32
BF16 = mybir.dt.bfloat16
I32 = mybir.dt.int32
U32 = mybir.dt.uint32
U16 = mybir.dt.uint16
U8 = mybir.dt.uint8
E4M3 = mybir.dt.float8_e4m3fn_x4
E5M2 = mybir.dt.float8_e5m2_x4
E2M1 = mybir.dt.float4_e2m1fn_x4
ACT = mybir.ActivationFunctionType
ALU = mybir.AluOpType

P = 128
L = 4
QUADRANTS = 4
HALF = N // 2
HALF_COLS = HALF // 16
BLK = 128
PLANE = T // 4

GPSIMD_COLS = 1536
VECTOR_COLS = 1024
VECTOR_PIECES = [(c, c + 2 * BLK) for c in range(0, VECTOR_COLS, 2 * BLK)]
SCALAR_PIECES = [(VECTOR_COLS, 1280), (1280, 1536), (1536, 1792), (1792, 1920), (1920, T)]
CODE_STORES = [(0, 512), (512, 1024), (1024, 1536), (1536, 1792), (1792, T)]


def load_scales(nc, raw_s, scales):
    for q in range(QUADRANTS):
        nc.sync.dma_start(out=raw_s[32 * q : 32 * q + 4, :].bitcast(I32), in_=scales[0, 4 * q : 4 * q + 4, :].bitcast(I32))


def deal_words(nc, pool, name, raw_w):
    w = pool.tile([P, 2 * 512], U8, name=name + "_w", align_bytes=64)
    nc.scalar.copy(
        w[:].bitcast(U16).rearrange("p (r s) -> p r s", r=L),
        raw_w[:].bitcast(U16).rearrange("p (s r) -> p r s", r=L),
    )
    return w


def deal_scales(engine, pool, name, raw_s):
    s = pool.tile([P, 512], U8, name=name + "_s", align_bytes=64)
    engine.tensor_copy(
        out=s[:].rearrange("p (r s) -> p r s", r=L),
        in_=raw_s[:].rearrange("p (s r) -> p r s", r=L),
    )
    return s


def tile_attend_gml_pl_nce_kernel(
    tc, xT, wd_words, wd_scales, wv_words, wv_scales, y, cw, rw, offs, out_0, out_1, out_2
):
    nc = tc.nc
    with ExitStack() as ctx:
        lists = ctx.enter_context(tc.tile_pool(name="lists", bufs=1))
        sb = ctx.enter_context(tc.tile_pool(name="sb", bufs=1))
        ps = ctx.enter_context(tc.psum_pool(name="ps", bufs=1))

        rows = sb.tile([P, 512], F32, name="rows")
        nc.gpsimd.memset(rows[:], 0.0)
        wd_raw_s = sb.tile([P, 512], U8, name="wd_raw_s", align_bytes=64)
        wv_raw_s = sb.tile([P, 512], U8, name="wv_raw_s", align_bytes=64)
        nc.gpsimd.memset(wd_raw_s[:].bitcast(I32), 0)
        wd_raw_w = sb.tile([P, 2 * 512], U8, name="wd_raw_w", align_bytes=64)
        wv_raw_w = sb.tile([P, 2 * 512], U8, name="wv_raw_w", align_bytes=64)

        offsets = lists.tile([P, N // 16], U16, name="offsets")
        x_rows = xT.rearrange("(p r) t -> p r t", r=L)
        x_lane = [sb.tile([P, T], F32, name=f"x_pl{r}", tag=f"x_pl{r}") for r in range(L)]
        y_rows = y.rearrange("(p r) i -> p r i", r=L)
        y_half = [sb.tile([P, L, HALF], F32, name=f"y_h{h}") for h in range(2)]

        ident = sb.tile([P, P], F32, name="ident")
        make_identity(nc, ident[:])
        nc.gpsimd.memset(wv_raw_s[:].bitcast(I32), 0)

        nc.sync.dma_start(out=x_lane[0][:], in_=x_rows[:, 0, :])
        nc.sync.dma_start(out=rows[0:1, :], in_=cw.rearrange("v o -> o v"))
        nc.sync.dma_start(out=rows[1:2, :], in_=rw[0:1, :])
        nc.sync.dma_start(offsets[:], offs)
        nc.sync.dma_start(out=x_lane[1][:], in_=x_rows[:, 1, :])
        load_scales(nc, wd_raw_s, wd_scales)
        nc.sync.dma_start(out=x_lane[2][:], in_=x_rows[:, 2, :])
        nc.sync.dma_start(out=x_lane[3][:], in_=x_rows[:, 3, :])
        nc.sync.dma_start(out=wd_raw_w[:].bitcast(I32), in_=wd_words[0].bitcast(I32))
        load_scales(nc, wv_raw_s, wv_scales)
        nc.sync.dma_start(out=y_half[0][:], in_=y_rows[:, :, :HALF])
        nc.sync.dma_start(out=wv_raw_w[:].bitcast(I32), in_=wv_words[0].bitcast(I32))
        nc.sync.dma_start(out=y_half[1][:], in_=y_rows[:, :, HALF:])

        warm = sb.tile([P, 1], F32, name="warm")
        nc.scalar.activation(warm[:], ident[:, 0:1], ACT.Sigmoid)

        win = {r: sb.tile([P, T], F32, name=f"win{r}") for r in range(2)}
        for r in range(2):
            nc.vector.memset(win[r][:].bitcast(I32), 0)
        win[3] = sb.tile([P, T], F32, name="win3")
        nc.gpsimd.memset(win[3][:].bitcast(I32), 0)

        rows_ps = ps.tile([P, L, P], F32, name="rows_ps", tag="bank6")
        for m in range(L):
            nc.tensor.transpose(rows_ps[:, m, :], rows[:, m::L], ident[:])
        weights = sb.tile([P, 2, L], F32, name="weights")
        nc.scalar.copy(weights[:], rows_ps[:, :, 0:2].rearrange("p m k -> p k m"))
        cw_sb, rw_sb = weights[:, 0, :], weights[:, 1, :]
        rw_ps = ps.tile([P, L, P], F32, name="rw_ps", tag="bank7")
        for m in range(L):
            nc.tensor.transpose(rw_ps[:, m, :], rw_sb[:, m : m + 1].to_broadcast([P, P]), ident[:])
        cc = sb.tile([P, L, N], F32, name="cc")
        for r in range(L):
            nc.scalar.activation(
                cc[:, r, :].rearrange("p (c m) -> p c m", m=L), rw_ps[:].rearrange("p m c -> p c m"), ACT.Copy, scale=cw_sb[:, r : r + 1]
            )

        xb = sb.tile([P, N, L], BF16, name="xb", align_bytes=64)
        xq = sb.tile([P, N], U32, name="xq", align_bytes=64)
        xs = sb.tile([P, N], U8, name="xs", align_bytes=64)
        entries = [offsets[:, h * HALF_COLS : (h + 1) * HALF_COLS] for h in range(2)]
        runs = xb[:].rearrange("p (a n) r -> p a n r", n=P)
        places = [runs[:, 1:4:2], runs[:, 0:3:2]]

        def quarter(q):
            return slice(q * P, (q + 1) * P)

        def gather(r, h):
            nc.vector.tensor_copy(places[h][:, :, :, r], x_lane[r][:].indirect(entries[h]))

        def quantise_x(q):
            h, a = divmod(q, 2)
            nc.vector.quantize_mx(
                out=xq[:, quarter(q)].bitcast(E4M3), scales=xs[:, quarter(q)], in_=places[h][:, a].rearrange("p n r -> p (n r)")
            )

        for r in range(2):
            gather(r, 0)
            gather(r, 1)
        wd_s = deal_scales(nc.gpsimd, sb, "wd", wd_raw_s)
        gather(2, 0)
        gather(2, 1)
        gather(3, 0)
        wd_w = deal_words(nc, sb, "wd", wd_raw_w)
        quantise_x(0)
        quantise_x(1)
        gather(3, 1)
        wv_s = deal_scales(nc.vector, sb, "wv", wv_raw_s)
        quantise_x(2)
        quantise_x(3)
        wv_w = deal_words(nc, sb, "wv", wv_raw_w)

        sig = [sb.tile([P, L, P], F32, name=f"sig{q}") for q in range(L)]
        dif = [sb.tile([P, 2, L, P], F32, name="dif0", tag="dif")]
        gb = [sb.tile([P, P * L], BF16, name=f"gb{q}", tag=f"gb{q}", align_bytes=64) for q in range(L)]
        gq = sb.tile([P, N], U32, name="gq", align_bytes=64)
        gs = sb.tile([P, N], U8, name="gs", align_bytes=64)

        def score(q, first, count, bank):
            sc = ps.tile([P, count, P], F32, name=f"sc{bank}", tag=f"bank{bank}")
            for e in range(count):
                r = first + e
                nc.tensor.matmul_mx(
                    out=sc[:, e, :],
                    lhsT=wd_w[:, 2 * P * r : 2 * P * (r + 1)].bitcast(E2M1),
                    lhsT_scale=wd_s[:, P * r : P * (r + 1)],
                    rhs=xq[:, quarter(q)].bitcast(E4M3),
                    rhs_scale=xs[:, quarter(q)],
                    start=True,
                    stop=True,
                )
            nc.scalar.activation(sig[q][:, first : first + count, :], sc[:], ACT.Sigmoid)

        def difference(q, first, count):
            h, a = divmod(q, 2)
            lanes = slice(first, first + count)
            nc.vector.tensor_tensor(dif[h][:, a, lanes, :], sig[q][:, lanes, :], y_half[h][:, lanes, quarter(a)], ALU.subtract)

        def weigh(q):
            h, a = divmod(q, 2)
            nc.vector.tensor_tensor(
                gb[q][:].rearrange("p (c i r) -> p c r i", i=2, r=L),
                dif[h][:, a].rearrange("p r (c i) -> p c r i", i=2),
                cc[:, :, quarter(q)].rearrange("p r (c i) -> p c r i", i=2),
                ALU.mult,
            )

        def quantise_g(q):
            nc.vector.quantize_mx(out=gq[:, quarter(q)].bitcast(E5M2), scales=gs[:, quarter(q)], in_=gb[q][:])

        def back(out, r, lo, hi):
            nc.tensor.matmul_mx(
                out=out,
                lhsT=wv_w[:, 2 * P * r : 2 * P * (r + 1)].bitcast(E2M1),
                lhsT_scale=wv_s[:, P * r : P * (r + 1)],
                rhs=gq[:, lo:hi].bitcast(E5M2),
                rhs_scale=gs[:, lo:hi],
                start=True,
                stop=True,
            )

        score(0, 0, 2, 0)
        score(0, 2, 2, 1)
        for q in range(1, L):
            score(q, 0, L, q + 1)
        difference(0, 0, 2)
        difference(0, 2, 2)
        difference(1, 0, L)
        weigh(0)
        weigh(1)
        quantise_g(0)
        quantise_g(1)

        def scalar_scatter(r, h, src):
            nc.scalar.activation(win[r][:].indirect(entries[h]), src, ACT.Copy)

        def vector_scatter(r, lists, src):
            nc.vector.tensor_copy(win[r][:].indirect(lists), src)

        o_rows = out_0.rearrange("(p r) t -> p r t", r=L)

        win[2] = sb.tile([P, T], F32, name="win2", tag="gb0", align_bytes=64)
        nc.gpsimd.memset(win[2][:].bitcast(I32), 0)

        a_early_ps = ps.tile([P, HALF], F32, name="a_early_ps", tag="bank5")
        for a in range(2):
            back(a_early_ps[:, quarter(a)], 0, a * P, (a + 1) * P)
        d_early_ps = ps.tile([P, HALF], F32, name="d_early_ps", tag="bank1")
        back(d_early_ps[:], 3, 0, HALF)
        b_early_ps = ps.tile([P, HALF], F32, name="b_early_ps", tag="bank2")
        back(b_early_ps[:], 1, 0, HALF)
        shared_ps = ps.tile([P, HALF + P], F32, name="shared_ps", tag="bank3")
        back(shared_ps[:, :HALF], 2, 0, HALF)
        a_early = sb.tile([P, HALF], F32, name="a_early")
        d_all = sb.tile([P, N], F32, name="d_all")
        nc.scalar.copy(a_early[:], a_early_ps[:])
        nc.scalar.copy(d_all[:, :HALF], d_early_ps[:])
        scalar_scatter(0, 0, a_early[:])

        dif.append(sb.tile([P, 2, L, P], F32, name="dif1", tag="dif"))
        difference(2, 0, L)
        difference(3, 0, L)
        weigh(2)
        weigh(3)
        quantise_g(2)
        quantise_g(3)

        a_third_ps = ps.tile([P, P], F32, name="a_third_ps", tag="bank6")
        back(a_third_ps[:], 0, HALF, HALF + P)
        back(shared_ps[:, HALF:], 0, HALF + P, N)
        bc_late_ps = ps.tile([P, 2, HALF], F32, name="bc_late_ps", tag="bank7")
        for e in range(2):
            back(bc_late_ps[:, e, :], 1 + e, HALF, N)
        d_late_ps = ps.tile([P, HALF], F32, name="d_late_ps", tag="bank0")
        back(d_late_ps[:], 3, HALF, N)

        a_late = sb.tile([P, HALF], F32, name="a_late")
        c_early = sb.tile([P, HALF], F32, name="c_early")
        bc_late = sb.tile([P, 2, HALF], F32, name="bc_late")
        b_early = sb.tile([P, HALF], F32, name="b_early", tag="dif")
        nc.vector.tensor_copy(b_early[:], b_early_ps[:])
        nc.vector.tensor_copy(a_late[:, :P], a_third_ps[:])
        vector_scatter(1, entries[0], b_early[:])
        nc.scalar.copy(a_late[:, P:], shared_ps[:, HALF:])
        nc.scalar.copy(c_early[:], shared_ps[:, :HALF])
        scalar_scatter(0, 1, a_late[:])
        nc.scalar.dma_start(out=o_rows[:, 0, :], in_=win[0][:])
        scalar_scatter(2, 0, c_early[:])
        nc.vector.tensor_copy(bc_late[:], bc_late_ps[:])
        nc.vector.tensor_copy(d_all[:, HALF:], d_late_ps[:])
        vector_scatter(1, entries[1], bc_late[:, 0, :])
        nc.sync.dma_start(out=o_rows[:, 1, :], in_=win[1][:])
        scalar_scatter(2, 1, bc_late[:, 1, :])
        nc.sync.dma_start(out=o_rows[:, 2, :], in_=win[2][:])
        vector_scatter(3, offsets[:], d_all[:])

        pairs = sb.tile([P, T * L], BF16, name="pairs", align_bytes=64)
        ob = sb.tile([P, T * L], BF16, name="ob", align_bytes=64)
        o_scales = sb.tile([P, PLANE], U8, name="os_", align_bytes=64)
        o_codes = sb.tile([P, T], U32, name="oq", align_bytes=64)
        o_words = out_1[0].rearrange("p n t -> p (n t)")

        def gpsimd_copy(out, in_):
            nc.gpsimd.tensor_scalar(out, in_, 1.0, 0.0, ALU.mult, ALU.add)

        def round_lane(copy, r, lo, hi):
            copy(
                pairs[:, L * lo : L * hi].rearrange("p (b u n e) -> p b u n e", u=2, n=BLK, e=2)[:, :, r // 2, :, r % 2],
                win[r][:, lo:hi].rearrange("p (b n) -> p b n", n=BLK),
            )

        def weave(copy, word, lo, hi):
            copy(
                ob[:, L * lo : L * hi].bitcast(word).rearrange("p (b n u) -> p b n u", n=BLK, u=2),
                pairs[:, L * lo : L * hi].bitcast(word).rearrange("p (b u n) -> p b n u", u=2, n=BLK),
            )

        def quantise_out(lo, hi):
            j, col = divmod(lo, PLANE)
            nc.vector.quantize_mx(
                out=o_codes[:, lo:hi].bitcast(E4M3), scales=o_scales[4 * j :, col : col + hi - lo], in_=ob[:, L * lo : L * hi]
            )

        for r in range(2):
            round_lane(gpsimd_copy, r, 0, GPSIMD_COLS)
        for lo in range(GPSIMD_COLS, T, BLK):
            round_lane(nc.scalar.copy, 0, lo, lo + BLK)
        round_lane(nc.scalar.copy, 1, GPSIMD_COLS, T)
        round_lane(nc.scalar.copy, 2, VECTOR_COLS, GPSIMD_COLS)
        nc.scalar.dma_start(out=o_rows[:, 3, :], in_=win[3][:])
        round_lane(nc.scalar.copy, 2, GPSIMD_COLS, T)
        for k, piece in enumerate(SCALAR_PIECES):
            round_lane(nc.scalar.copy, 3, *piece)
            if k > 0:
                weave(nc.scalar.copy, U32, *SCALAR_PIECES[k - 1])
        weave(nc.scalar.copy, U32, *SCALAR_PIECES[-1])

        for first in range(0, len(VECTOR_PIECES), 2):
            both = VECTOR_PIECES[first : first + 2]
            for piece in both:
                for r in (3, 2):
                    round_lane(nc.vector.tensor_copy, r, *piece)
            for piece in both:
                weave(nc.vector.tensor_copy, I32, *piece)
            for piece in both:
                quantise_out(*piece)
        for piece in SCALAR_PIECES:
            quantise_out(*piece)
        for lo, hi in CODE_STORES:
            nc.sync.dma_start(out=o_words[:, L * lo : L * hi].bitcast(I32), in_=o_codes[:, lo:hi].bitcast(I32))
        for q in range(QUADRANTS):
            queue = nc.scalar if q % 2 == 0 else nc.sync
            queue.dma_start(
                out=out_2[0, 4 * q : 4 * q + 4, :].bitcast(I32).rearrange("f (j n) -> j f n", j=4),
                in_=o_scales[32 * q : 32 * q + 16, :].bitcast(I32),
            )
